import numpy as np, ml_dtypes
CORES = [23,119,17,113]
N = 4
import mx_ref
BF = ml_dtypes.bfloat16
def gcols(t, e):
    v = np.concatenate([t.reshape(8, 16, -1, 4), np.zeros((8, 16, 1, 4), BF)], axis=2)
    return np.ascontiguousarray(np.stack([v[g][:, e[g]] for g in range(8)])).reshape(128, -1)
def cut(t, i, w=512):
    return t[:, w * i:w * i + w]
def pick(q, e):
    c = np.concatenate([q[0].reshape(128, -1, 4), np.zeros((128, 1, 4), np.uint8)], axis=1); s = np.concatenate([q[1], np.ones((16, 1), np.uint8)], axis=1)
    return (np.ascontiguousarray(c[:, e].reshape(128, -1)), np.ascontiguousarray(s[:, e]))
def join(*qs):
    return (np.concatenate([q[0] for q in qs], axis=1), np.concatenate([q[1] for q in qs], axis=1))
def put(q, e, v):
    c, s = q[0].reshape(128, -1, 4).copy(), q[1].copy(); c[:, e] = v[0].reshape(128, -1, 4); s[:, e] = v[1]
    return (c.reshape(128, -1), s)
def pk(c, s):
    return (np.ascontiguousarray(c), mx_ref.live(s))
def emit(q):
    return q[0], q[1]
def packed(v, rng):
    q = [mx_ref.quantize(np.ascontiguousarray(v[r])) for r in range(N)]
    return np.stack([a for a, b in q]), np.stack([mx_ref.plane(b, rng) for a, b in q])
def values_of_codes():
    e, c = np.zeros((128, 128, 4), np.float32), np.zeros((128, 2, 4), np.uint8)
    e[np.arange(128), np.arange(128), 0] = 1
    c[:127, :, 0] = np.arange(256).reshape(2, 128).T[:127]
    return mx_ref.matmul(mx_ref.quantize(e.reshape(128, 512).astype(BF)), (c.reshape(128, 8), np.full((16, 2), 127, np.uint8))).T.reshape(-1).astype(np.float64)
CODE_VALUE, SCALE_VALUE = values_of_codes(), 2.0 ** (np.arange(256) - 127.0)
def decode(q):
    return (CODE_VALUE[q[0]].reshape(16, 8, -1, 4) * SCALE_VALUE[q[1]][:, None, :, None] + 0.0).reshape(128, -1).astype(np.float32)
def f(rng, *shape):
    return mx_ref.flush((rng.standard_normal(shape, dtype=np.float32) * np.exp2(rng.integers(-2, 3, shape[:-1] + (1,)))).astype(BF))
def wide(rng, *shape, cols=0):
    v = rng.standard_normal(shape, dtype=np.float32) * np.exp2(rng.integers(-12, 13, shape)).astype(np.float32)
    if cols: v *= np.repeat(np.exp2(rng.integers(-cols, cols + 1, shape[:-2] + (1, shape[-1] // 4))) * (rng.random(shape[:-2] + (1, shape[-1] // 4)) > 0.0625), 4, axis=-1).astype(np.float32)
    return mx_ref.flush(v.astype(BF))
C, M, L, T = 288, 512, 9, 3
def two(i):
    return np.arange(2 * C * i, 2 * C * i + 2 * C)
def product(a, q):
    return np.concatenate([mx_ref.matmul(a, pick(q, two(i))) for i in range(N // 2)], axis=1)
def unpacked(q):
    return np.concatenate([decode(pick(q, two(i))) for i in range(N // 2)], axis=1)
def place(a):
    e = np.full((8, M), C)
    np.minimum.at(e, (np.arange(8)[:, None], a), np.arange(C)[None, :])
    return np.where(e < C, M + e, np.arange(M)[None, :])
def same(a):
    return np.stack([a] * N)
def weights(rng, w):
    c, p = packed(same(w), rng)
    return {"wc": c, "ws": p}
def numbers_of(rng):
    return {"x": np.array(f(rng, N, 128, 4 * C)), "m": np.array(f(rng, N, 128, 4 * M))}
def digits(e, size):
    v = np.zeros(e.shape + (32,))
    v[..., :L] = (((e[..., None] >> np.arange(L)) & 1) * 2 - 1) * size[None, :, None, None]
    return np.moveaxis(v.reshape(e.shape + (8, 4)), 2, 3).astype(np.float32).astype(BF)
def setup_inputs(rng):
    return {**numbers_of(rng), "u": same(f(rng, 128, 512)), **weights(rng, f(rng, 128, 2048))}
def setup_inputs_ties(rng):
    d = numbers_of(rng)
    e = rng.permutation(N)
    x = d["x"].reshape(N, 8, 16, C, 4)
    for r in range(N):
        k = rng.permutation(C)
        if r == e[0]: k = np.zeros(C, int)
        elif r == e[2]: k = np.where(k < 256, 0, 2)
        else: k = k % 3
        a = x[r][:, :8, :3].copy()
        a[:, :, 2] = 0
        x[r][:, :8] = a[:, :, k]
    x[e[1]] = 0
    u = np.array(f(rng, 128, 512)).reshape(8, 16, 128, 4)
    u[:, 8:] = 0
    w = np.array(f(rng, 128, 2048)).reshape(8, 16, 4, 8, 16, 4)
    w[:, 8:, :, :, :8] = 0
    return {"x": x.reshape(N, 128, 4 * C), "m": d["m"], "u": same(u.reshape(128, 512)), **weights(rng, w.reshape(128, 2048))}
def setup_inputs_crowd(rng):
    d = numbers_of(rng)
    for n in ("x", "m"):
        p = d[n].reshape(N, 128, -1, 4)
        p[:, 15] = 0
        p[:, 15, :, 0] = 1
        d[n] = p.reshape(N, 128, -1)
    u = np.array(f(rng, 128, 512)).reshape(128, 128, 4)
    k = rng.permutation(np.array([0, 0, 1, 2, 3, 5, 7, L]))
    h = np.flatnonzero(k == 0)
    for g in range(8):
        z = 16 * g + rng.permutation(L)[k[g]:]
        s = rng.integers(-1, 2, len(z)) if k[g] else np.full(len(z), int(g == h[0]))
        u[:, z] = 0
        u[15, z, 0] = s.astype(np.float32).astype(BF)
    w = np.array(f(rng, 128, 2048)).reshape(128, 4, 128, 4)
    w[:, :, 15] = 0
    return {**d, "u": same(u.reshape(128, 512)), **weights(rng, w.reshape(128, 2048))}
def setup_inputs_chain(rng):
    d = numbers_of(rng)
    s = rng.permutation(8) % 2 * 2 - 1
    size = np.where(s > 0, 2.0 ** 28, 2.0 ** -30)
    x, m = d["x"].reshape(N, 8, 16, C, 4), d["m"].reshape(N, 8, 16, M, 4)
    to = np.stack([[rng.permutation(M) for g in range(8)] for r in range(N)])
    at = np.stack([[rng.permutation(M)[:C] for g in range(8)] for r in range(N)])
    x[:, :, :8] = digits(at, size)
    m[:, :, :8] = digits(to, size)
    u = np.array(f(rng, 128, 512)).reshape(8, 16, 128, 4)
    for g in range(8):
        for i in range(L):
            u[:, :, 16 * g + i] = 0
            u[g, i // 4, 16 * g + i, i % 4] = 2.0 ** 30 if s[g] > 0 else 2.0 ** -30
    w = np.array(f(rng, 128, 2048)).reshape(8, 16, 4, 8, 16, 4)
    w[:, :8] = 0
    w[:, :, :, :, :8] = 0
    for g in rng.permutation(8)[:4]:
        z = (N, 8, M, 4)
        m[:, g, 8:] = (rng.integers(8, 16, z) * np.exp2(-1.0 * rng.integers(13, 22, z)) * rng.choice([-1.0, 1.0], z)).astype(np.float32).astype(BF)
        m[:, g, 8, :, 0] = 1.625
        x[:, g, 8, :, 0] = -0.6875
        w[:, :, :, g, 8:] = 0
        w[g, 8, 0, g, 8, 0] = -32
    return {"x": x.reshape(N, 128, 4 * C), "m": m.reshape(N, 128, 4 * M), "u": same(u.reshape(128, 512)), **weights(rng, w.reshape(128, 2048))}
def setup_inputs_spread(rng):
    d = setup_inputs(rng)
    d["x"] = wide(rng, N, 128, 4 * C, cols=6)
    d["m"] = wide(rng, N, 128, 4 * M, cols=6)
    return d
def check_inputs(d):
    b = []
    for k in ("x", "m", "u"):
        a = np.abs(d[k].astype(np.float32))
        if not (np.isfinite(a).all() and ((a == 0) | (a >= 2.0 ** -30) & (a <= 2.0 ** 30)).all()): b.append("a value of " + k)
    if (d["u"].astype(np.float32) != d["u"][:1].astype(np.float32)).any(): b.append("u differs between ranks")
    if (d["wc"] != d["wc"][:1]).any(): b.append("wc differs between ranks")
    s = [mx_ref.live(p) for p in d["ws"]]
    if any((p != s[0]).any() for p in s): b.append("ws differs between ranks")
    a = np.abs(decode(pk(d["wc"][0], d["ws"][0])))
    if ((d["wc"] & 127) == 127).any() or not ((a == 0) | (a >= 2.0 ** -30) & (a <= 2.0 ** 30)).all(): b.append("a value of W")
    return b
def reference(x, m, u, wc, ws):
    w, qu = pk(wc[0], ws[0]), mx_ref.quantize(u[0])
    part = [pick(w, np.arange(128 * b, 128 * b + 128)) for b in range(4)]
    state = join(*[mx_ref.quantize(x[r]) for r in range(N)])
    maps = [m[r] for r in range(N)]
    power = (1 << np.arange(L)).reshape(1, L, 1, 1)
    for t in range(T):
        a = product(qu, state).reshape(8, 16, N, C)
        at = np.sum((a[:, :L] > 0) * power, axis=1)
        reads = np.concatenate([gcols(maps[(r + t) % N], at[:, r]) for r in range(N)], axis=1)
        layer = np.stack([product(part[b], state) * np.float32(0.015625) for b in range(4)], axis=2).reshape(128, -1)
        state = mx_ref.quantize((layer + unpacked(mx_ref.quantize(reads))).astype(BF))
        new = unpacked(state).astype(BF)
        for r in range(N):
            h = (r + t) % N
            maps[h] = gcols(np.concatenate([maps[h], cut(new, r, 4 * C)], axis=1), place(at[:, r]))
    last = product(part[0], state)
    y = np.zeros((N, 128, C), np.float32)
    oc, osc = np.zeros((N, 128, 4 * (C + M)), np.uint8), np.zeros((N, 16, C + M), np.uint8)
    for r in range(N):
        y[r] = cut(last, r, C)
        oc[r], osc[r] = emit(join(pick(state, C * r + np.arange(C)), mx_ref.quantize(maps[r])))
    return {"y": y, "oc": oc, "osc": osc}

@@ -1,0 +1,518 @@
+from concourse.mybir import dt, AluOpType, AxisListType, ActivationFunctionType
+
+C, M, NV = 288, 512, 3
+K16 = C // 16
+CH = 64
+POOL = M + NV * C
+BIG, KEEP = 16384.0, 8192.0
+CUT = 160
+HA, HB, ALL = (0, CUT), (CUT, C), (0, C)
+
+Q4, U8, BF, F32, I32, U16 = "float8_e4m3fn_x4", "uint8", "bfloat16", "float32", "int32", "uint16"
+SCRATCH = {
+    "xin": ("sbuf", [128, 4 * C], BF), "uin": ("sbuf", [128, 512], BF), "pool": ("sbuf", [128, 4 * POOL], BF),
+    "wq": ("sbuf", [128, 512], Q4), "wp": ("sbuf", [128, 512], U8),
+    "uq": ("sbuf", [128, 128], Q4), "up": ("sbuf", [128, 128], U8),
+    "oq": ("sbuf", [128, C + M], Q4), "op": ("sbuf", [128, C + M], U8),
+    "bt": ("sbuf", [128, 4 * C], BF), "bq": ("sbuf", [128, C], Q4), "bp": ("sbuf", [128, C], U8),
+    "yt": ("sbuf", [128, 4 * C], BF), "mt": ("sbuf", [128, 4 * M], BF), "yo": ("sbuf", [128, C], F32),
+    "ft": ("sbuf", [128, 512], BF), "fq": ("sbuf", [128, 384], Q4), "fp": ("sbuf", [128, 384], U8),
+    "ze": ("sbuf", [128, 528], BF), "zz": ("sbuf", [128, 528], BF),
+    "wa": ("sbuf", [128, 512], BF), "wb": ("sbuf", [128, 512], BF),
+    "eq": ("sbuf", [128, 512], Q4), "ep": ("sbuf", [128, 512], U8),
+    "zq": ("sbuf", [128, 512], Q4), "zp": ("sbuf", [128, 512], U8),
+    "aq": ("sbuf", [128, 256], Q4), "ap": ("sbuf", [128, 256], U8),
+    "pi": ("sbuf", [128, 8], I32), "pj": ("sbuf", [128, 8], I32), "pf": ("sbuf", [128, 8], F32),
+    "j16": ("sbuf", [128, 16], F32), "d16": ("sbuf", [128, 16], F32), "col": ("sbuf", [128, 8], F32),
+    "gm": ("sbuf", [128, 8], F32), "c4b": ("sbuf", [128, 12], F32),
+    "mi": ("sbuf", [128, 192], BF), "mk": ("sbuf", [128, 192], BF), "idj": ("sbuf", [128, 128], BF),
+    "c4": ("sbuf", [128, 512], BF), "cdi": ("sbuf", [128, 256], BF), "cd": ("sbuf", [128, K16 * CH], BF),
+    "dni": ("sbuf", [128, 20], F32), "dn": ("sbuf", [128, 20], F32),
+    "tab": ("sbuf", [128, M + CH], F32), "val": ("sbuf", [128, NV * C], F32),
+    "sca": ("sbuf", [128, 72], F32), "prow": ("sbuf", [128, C], F32), "scp": ("sbuf", [128, M], F32),
+    "boff": ("sbuf", [128, 72], U16), "moff": ("sbuf", [128, 128], U16),
+    "ne": ("sbuf", [128, K16 * CH], BF), "scd": ("sbuf", [128, K16 * CH], BF),
+    "t1": ("sbuf", [128, K16], F32), "t2": ("sbuf", [128, K16], F32),
+    "py": ("psum", [128, 2048], F32), "pn": ("psum", [128, 2048], F32),
+}
+for _t in range(NV):
+    SCRATCH["sq%d" % _t] = ("sbuf", [128, C], Q4)
+    SCRATCH["sp%d" % _t] = ("sbuf", [128, C], U8)
+    SCRATCH["yq%d" % _t] = ("sbuf", [128, C], Q4)
+    SCRATCH["yp%d" % _t] = ("sbuf", [128, C], U8)
+    SCRATCH["af%d" % _t] = ("sbuf", [128, K16], F32)
+    SCRATCH["am%d" % _t] = ("sbuf", [128, K16], F32)
+    SCRATCH["ar%d" % _t] = ("sbuf", [128, 320], BF)
+    SCRATCH["so%d" % _t] = ("sbuf", [128, K16], U16)
+    if _t:
+        SCRATCH["ao%d" % _t] = ("sbuf", [128, K16], U16)
+        SCRATCH["la%d" % _t] = ("sbuf", [128, K16], U16)
+        SCRATCH["ls%d" % _t] = ("sbuf", [128, K16], U16)
+SEMAPHORES = ["cv", "cs", "ct", "cg", "sent", "dx", "du", "dm", "dw", "st1", "st2", "st3",
+              "la1", "la2", "ls1", "ls2", "out"]
+COUNTER = {"v": "cv", "s": "cs", "t": "ct", "g": "cg"}
+
+
+def _emit(g, T, ops):
+    queue = {"v": g.vector, "s": g.scalar, "t": g.tensor, "g": g, "y": g.sync}
+    known = {q: {} for q in queue}
+    total, waited = {}, {}
+    writer, readers = {}, {}
+    for q, fn, reads, writes, sem, inc in ops:
+        need = [writer[r] for r in list(reads) + list(writes) if r in writer]
+        for r in writes:
+            need += readers.get(r, [])
+        for r in reads:
+            if r[0] == "@":
+                need += [e for e in readers.get(r, []) if e[0] != q]
+        if fn is not None:
+            for eq, esem, count, clock in sorted(need, key=lambda e: -e[2]):
+                if (eq == q == "t") or known[q].get(esem, 0) >= count:
+                    continue
+                queue[q].wait_ge(T.sem[esem], count)
+                waited[esem] = max(waited.get(esem, 0), count)
+                for s, v in clock.items():
+                    known[q][s] = max(known[q].get(s, 0), v)
+        if sem is None:
+            sem, inc = COUNTER[q], 1
+        total[sem] = total.get(sem, 0) + inc
+        clock = dict(known[q]) if fn is not None else {}
+        clock[sem] = total[sem]
+        if fn is not None:
+            ins = fn()
+            if sem != "sent":
+                ins.then_inc(T.sem[sem], inc)
+        ev = (q, sem, total[sem], clock)
+        for r in reads:
+            readers.setdefault(r, []).append(ev)
+        for r in writes:
+            writer[r] = ev
+            readers[r] = []
+    for s in total:
+        if waited.get(s, 0) < total[s]:
+            queue["y" if s == "out" else "g"].wait_ge(T.sem[s], total[s])
+
+
+def rank_program(g, core, T, topo):
+    rank = T.rank_of(core)
+    if rank is None:
+        return
+    n = len(T.cores)
+    nxt, home = T.cores[(rank + 1) % n], T.cores[(rank - (NV - 1)) % n]
+    V, S, P = g.vector, g.scalar, g.tensor
+    A, F = AluOpType, ActivationFunctionType
+    ops = []
+
+    def op(q, fn, reads, writes, sem=None, inc=None):
+        ops.append((q, fn, reads, writes, sem, inc))
+
+    def by(view):
+        return view.bitcast(dt.uint8)
+
+    def bank(name):
+        return T["p" + name[1]], 512 * int(name[2])
+
+    def runs(h):
+        return "a" if h == HA else "b" if h == HB else "ab"
+
+    def ts(out, in0, s1, s2, op0, op1, reads, writes):
+        if op1 is None:
+            op("v", lambda: V.tensor_scalar(out, in0, s1, None, op0), reads, writes)
+        else:
+            op("v", lambda: V.tensor_scalar(out, in0, s1, s2, op0, op1), reads, writes)
+
+    def quant(q, p, src, reads, writes):
+        op("v", lambda: V.quantize_mx(q, p, src), reads, writes)
+
+    def mm(bk, cols, lq, lp, rq, rp, start, stop, reads):
+        buf, o = bank(bk)
+        op("t", lambda: P.matmul_mx(buf[:, o:o + cols], lq, lp, rq, rp, start, stop), reads, [bk])
+
+    def act(out, in_, func, reads, writes, **kw):
+        op("s", lambda: S.activation(out, in_, func, **kw), reads, writes)
+
+    def iota(out, pattern, base, mult, writes, small=True):
+        if small:
+            op("g", lambda: g.iota(out, pattern, base, mult, allow_small_or_imprecise_dtypes=True), [], writes)
+        else:
+            op("g", lambda: g.iota(out, pattern, base, mult), [], writes)
+
+    def send(dst, mask, out, in_, sem, reads):
+        rid, pid = topo.addr(dst)[:2]
+        op("g", lambda: g.remote_dma(out, in_, T.sem[sem], T.sem["sent"], pid, rid, mask),
+           reads, [], "sent", bin(mask).count("1"))
+
+    def arrive(sem, count, writes):
+        op("g", None, [], writes, sem, count)
+
+    far, near = topo.mask(core, nxt), topo.mask(core, home)
+    nfar, nnear = bin(far).count("1"), bin(near).count("1")
+    for t in (1, 2):
+        arrive("st%d" % t, 2 * nfar, ["s%d" % t])
+        arrive("la%d" % t, nfar, ["la%d" % t])
+        arrive("ls%d" % t, nfar, ["ls%d" % t])
+    arrive("st3", 2 * nnear, ["s3"])
+
+    op("y", lambda: g.sync.dma_start(T.xin[:], T.x[:]), [], ["xin"], "dx", 16)
+    op("s", lambda: S.dma_start(T.uin[:], T.u[:]), [], ["uin"], "du", 16)
+    op("y", lambda: g.sync.dma_start(T.pool[:, 0:4 * M], T.m[:]), [], ["pool"], "dm", 16)
+    op("y", lambda: g.sync.dma_start(by(T.wq[:]), T.wc[:]), [], ["w0"], "dw", 16)
+    op("y", lambda: g.sync.dma_start(T.wp[:], T.ws[:]), [], ["w"], "dw", 16)
+
+    cc, grp, w4, t4 = (T.pf[:, i:i + 1] for i in range(4))
+    iota(T.pi[:, 0:1], [[0, 1]], 0, 1, ["pi"], small=False)
+    iota(T.j16[:], [[1, 16]], 0, 0, ["j16"])
+    iota(T.mi[:, 0:64], [[1, 4], [0, 4], [-1, 4]], 0, 0, ["mi0"])
+    iota(T.idj[:], [[1, 128]], 0, -1, ["idj"])
+    iota(T.mi[:, 64:128], [[0, 4], [1, 4], [-1, 4]], 0, 0, ["mi1"])
+    iota(T.mi[:, 128:192], [[0, 16], [1, 4]], -3, 0, ["mi2"])
+    iota(T.cdi[:], [[-16, 4], [1, 64]], 0, 0, ["cdi"])
+    iota(T.dni[:], [[0, 5], [-16, 4]], -M, 0, ["dni"])
+    iota(T.tab[:], [[4, M + CH]], 0, 0, ["tab"])
+    iota(T.val[:], [[4, NV * C]], 4 * M, 0, ["val"])
+
+    op("v", lambda: V.memset(T.ze[:], 0.0), [], ["ze"])
+    op("v", lambda: V.memset(T.ft[:, C:512], 0.0), [], ["ftz"])
+    ts(T.pj[:, 0:1], T.pi[:, 0:1], 15, None, A.bitwise_and, None, ["pi"], ["pj0"])
+    ts(T.pj[:, 1:2], T.pi[:, 0:1], 4, None, A.arith_shift_right, None, ["pi"], ["pj1"])
+    ts(T.pj[:, 2:3], T.pi[:, 0:1], 2, 3, A.arith_shift_right, A.bitwise_and, ["pi"], ["pj2"])
+    ts(T.pj[:, 3:4], T.pi[:, 0:1], 3, None, A.bitwise_and, None, ["pi"], ["pj3"])
+    quant(T.fq[:, 0:128], T.fp[:, 0:128], T.ze[:, 0:512], ["ze"], ["fz0"])
+    op("v", lambda: V.tensor_copy(T.pf[:, 0:4], T.pj[:, 0:4]), ["pj0", "pj1", "pj2", "pj3"], ["pf"])
+    quant(T.fq[:, 256:384], T.fp[:, 256:384], T.ze[:, 0:512], ["ze"], ["fz1"])
+    ts(T.d16[:], T.j16[:], cc, 1.0, A.is_lt, A.add, ["j16", "pf"], ["d16"])
+    ts(T.mk[:, 0:64], T.mi[:, 0:64], 0.0, None, A.is_equal, None, ["mi0"], ["mk0"])
+    op("v", lambda: V.tensor_reduce(T.col[:, 0:1], T.d16[:], AxisListType.X, A.mult), ["d16"], ["col0"])
+    ts(T.c4b[:, 0:4], T.j16[:, 0:4], w4, -BIG, A.is_equal, A.mult, ["j16", "pf"], ["c4b0"])
+    ts(T.col[:, 1:2], cc, 8.5, T.col[:, 0:1], A.is_lt, A.mult, ["pf", "col0"], ["col1"])
+    ts(T.c4b[:, 4:8], T.j16[:, 0:4], -1.0, w4, A.add, A.is_equal, ["j16", "pf"], ["c4b1"])
+    ts(T.gm[:], T.j16[:, 0:8], grp, T.col[:, 1:2], A.is_equal, A.mult, ["j16", "pf", "col1"], ["gm"])
+    ts(T.ze[:, 3:512:4], T.idj[:], 0.0, 64.0, A.is_equal, A.mult, ["idj"], ["ze"])
+
+    def weights(q, tile, mask, ms, name):
+        for m in ms:
+            o, i, s = tile[:, 64 * m:64 * m + 64], T.mk[:, 64 * mask:64 * mask + 64], T.gm[:, m:m + 1]
+            if q == "v":
+                ts(o, i, s, None, A.mult, None, ["mk%d" % mask, "gm"], [name + str(m)])
+            else:
+                act(o, i, F.Copy, ["mk%d" % mask, "gm"], [name + str(m)], scale=s)
+
+    def names(name):
+        return [name + str(m) for m in range(8)]
+
+    weights("s", T.wb, 0, range(4, 8), "wb")
+    weights("v", T.wb, 0, range(0, 4), "wb")
+    ts(T.mk[:, 64:192], T.mi[:, 64:192], 0.0, None, A.is_equal, None, ["mi1", "mi2"], ["mk1", "mk2"])
+    op("v", lambda: V.memset(T.zz[:, 512:528], 0.0), [], ["zzt"])
+    weights("s", T.zz, 2, range(8), "zz")
+    weights("s", T.wa, 1, range(8), "wa")
+    for b in range(4):
+        quant(T.eq[:, 128 * b:128 * b + 128], T.ep[:, 128 * b:128 * b + 128], T.ze[:, 3 - b:515 - b], ["ze"], ["e%d" % b])
+    quant(T.aq[:, 128:256], T.ap[:, 128:256], T.wb[:], names("wb"), ["qwb"])
+    quant(T.uq[:], T.up[:], T.uin[:], ["uin"], ["uq"])
+    ts(T.c4b[:, 8:12], T.c4b[:, 4:8], KEEP, None, A.mult, None, ["c4b1"], ["c4b2"])
+    ts(T.col[:, 2:3], w4, 2.5, -KEEP, A.is_lt, A.mult, ["pf"], ["col2"])
+    ts(T.cd[:, 0:256], T.cdi[:], cc, -1.0, A.is_equal, A.mult, ["cdi", "pf"], ["cd0"])
+    op("v", lambda: V.tensor_tensor(T.c4b[:, 4:8], T.c4b[:, 8:12], T.c4b[:, 0:4], A.add), ["c4b0", "c4b2"], ["c4b1"])
+    ts(T.col[:, 3:4], T.col[:, 2:3], t4, None, A.add, None, ["col2", "pf"], ["col3"])
+    ts(T.col[:, 4:5], T.col[:, 2:3], -256.0, None, A.add, None, ["col2"], ["col4"])
+    for i in range(4):
+        act(T.c4[:, i:512:4], T.idj[:], F.Identity, ["idj", "c4b1"], ["c4%d" % i], scale=0.0, bias=T.c4b[:, 4 + i:5 + i])
+    ts(T.dn[:], T.dni[:], cc, None, A.subtract, None, ["dni", "pf"], ["dn"])
+    ts(T.cd[:, 0:256:64], T.j16[:, 0:4], 0.0, 8.0, A.mult, A.add, ["j16"], ["cd0"])
+    for t in range(NV):
+        op("v", lambda t=t: V.memset(T["ar%d" % t][:, C:320], 300.0), [], ["art%d" % t])
+
+    def dedupe_period():
+        for i, (a, b) in enumerate(((256, 512), (512, 1024), (1024, K16 * CH))):
+            op("v", lambda a=a, b=b: V.tensor_copy(T.cd[:, a:b], T.cd[:, 0:b - a]),
+               ["cd%d" % j for j in range(i + 1)], ["cd%d" % (i + 1)])
+
+    C4 = ["c40", "c41", "c42", "c43"]
+    CD = ["cd0", "cd1", "cd2", "cd3"]
+
+    def qz(b):
+        quant(T.zq[:, 128 * b:128 * b + 128], T.zp[:, 128 * b:128 * b + 128], T.zz[:, 3 - b:515 - b],
+              names("zz") + ["zzt"], ["z%d" % b])
+
+    def a_mm(q, p, res, bk, h):
+        mm(bk, h[1] - h[0], T.uq[:], T.up[:], q[:, h[0]:h[1]], p[:, h[0]:h[1]], True, True, ["uq", res])
+
+    def bits(bk, h):
+        buf, o = bank(bk)
+        ts(T.ft[:, h[0]:h[1]], buf[:, o:o + h[1] - h[0]], 0.0, None, A.is_gt, None, [bk], ["ft" + c for c in runs(h)])
+
+    def q_bits():
+        quant(T.fq[:, 128:256], T.fp[:, 128:256], T.ft[:], ["fta", "ftb", "ftz"], ["fq"])
+
+    def list_mm(bk, which):
+        o = 128 * which
+        mm(bk, 128, T.aq[:, o:o + 128], T.ap[:, o:o + 128], T.fq[:, 128:256], T.fp[:, 128:256], True, True,
+           ["fq", "qwb" if which else "qwa"])
+
+    def row_mm(bk, half):
+        for i, o in ((0, 128), (1, 56)):
+            t = 2 * half + i
+            mm(bk, 144, T.zq[:, 128 * t:128 * t + 128], T.zp[:, 128 * t:128 * t + 128],
+               T.fq[:, o:o + 144], T.fp[:, o:o + 144], i == 0, i == 1, ["fq", "fz0", "fz1", "z%d" % t])
+
+    def row_read(v, bk, half):
+        buf, o = bank(bk)
+        for i in range(2):
+            t = 2 * half + i
+            act(T["ar%d" % v][:, t:C:4], buf[:, o + 72 * i:o + 72 * i + 72], F.Identity, [bk], ["ar%d%d" % (v, t)],
+                bias=-256.0)
+
+    def list_scan(bk):
+        buf, o = bank(bk)
+        op("v", lambda: V.tensor_tensor_scan(T.sca[:], T.c4[:, 0:72], buf[:, o:o + 72], 0.0, A.add, A.max),
+           [bk] + C4, ["sca"])
+
+    def list_u16(v):
+        ts(T["ao%d" % v][:], T.sca[:, 3:72:4], T.col[:, 2:3], None, A.add, None, ["sca", "col2"], ["ao%d" % v])
+
+    def list_f32(v):
+        act(T["af%d" % v][:], T.sca[:, 3:72:4], F.Identity, ["sca", "col2"], ["af%d" % v], bias=T.col[:, 2:3])
+        act(T["am%d" % v][:], T.sca[:, 3:72:4], F.Identity, ["sca", "col4"], ["am%d" % v], bias=T.col[:, 4:5])
+
+    def compare(q, v, ks):
+        for k in ks:
+            c0 = CH * (k // 4)
+            o, i, s = T.ne[:, CH * k:CH * k + CH], T["ar%d" % v][:, c0:c0 + CH], T["am%d" % v][:, k:k + 1]
+            rd = ["ar%d%d" % (v, t) for t in range(4)] + ["art%d" % v, "am%d" % v]
+            if q == "v":
+                ts(o, i, s, None, A.not_equal, None, rd, ["ne%d" % k])
+            else:
+                act(o, i, F.Abs, rd, ["ne%d" % k], scale=-1.0, bias=s)
+
+    def dedupe(v):
+        op("v", lambda: V.tensor_tensor_scan(T.scd[:], T.cd[:], T.ne[:], 0.0, A.add, A.min),
+           CD + ["ne%d" % k for k in range(K16)], ["scd"])
+        op("v", lambda: V.tensor_tensor(T.t1[:], T.scd[:, CH - 1:K16 * CH:CH], T.dn[:, 0:K16], A.mult), ["scd", "dn"], ["t1"])
+        op("v", lambda: V.tensor_tensor(T.t2[:], T.t1[:], T["af%d" % v][:], A.max), ["t1", "af%d" % v], ["t2"])
+        op("v", lambda: V.tensor_copy(T["so%d" % v][:], T.t2[:]), ["t2"], ["so%d" % v])
+        if v:
+            send(nxt, far, T["ls%d" % v][:], T["so%d" % v][:], "ls%d" % v, ["so%d" % v])
+
+    def scatter(v, chunks):
+        name = "ls%d" % v if v else "so0"
+        for c in chunks:
+            a, b = 4 * c, min(4 * c + 4, K16)
+            op("v", lambda a=a, b=b: V.tensor_copy(T.tab[:].indirect(T[name][:, a:b]),
+                                                   T.val[:, C * v + 16 * a:C * v + 16 * b]),
+               [name, "val"], ["tab"])
+
+    def pool_names(v):
+        return ["pool"] + ["n%d%d%s" % (t, b, c) for t in range(v) for b in range(4) for c in "ab"]
+
+    def gather(q, out, win, off, reads, writes):
+        if q == "v":
+            op("v", lambda: V.tensor_copy(out, win.indirect(off)), reads, writes)
+        else:
+            act(out, win.indirect(off), F.Copy, reads, writes)
+
+    def select_scan(src, res, a, b):
+        op("v", lambda: V.tensor_tensor_scan(T.scp[:, a:b], T.c4[:, a:b], src[:, a:b], 0.0, A.add, A.max),
+           [res] + C4, ["scp%d" % min(a, 1)])
+
+    def select_u16(off, out, a, b):
+        ts(off[:, a // 4:b // 4], T.scp[:, a + 3:b:4], T.col[:, 3:4], None, A.add, None,
+           ["scp%d" % min(a, 1), "col3"], [out])
+
+    def pointers(v):
+        la = T["la%d" % v]
+        gather("v", T.prow[:, 0:CUT], T.tab[:], la[:, 0:CUT // 16], ["tab", "la%d" % v], ["prowa"])
+        gather("s", T.prow[:, CUT:C], T.tab[:], la[:, CUT // 16:K16], ["tab", "la%d" % v], ["prowb"])
+        select_scan(T.prow, "prowa", 0, CUT)
+        select_scan(T.prow, "prowb", CUT, C)
+        select_u16(T.boff, "boffa", 0, CUT)
+        select_u16(T.boff, "boffb", CUT, C)
+
+    def read_map(v):
+        win = T.pool[:, 0:4 * (M + C * v)]
+        gather("s", T.bt[:, 0:4 * CUT], win, T.boff[:, 0:CUT // 4], pool_names(v) + ["boffa"], ["bta"])
+        gather("v", T.bt[:, 4 * CUT:4 * C], win, T.boff[:, CUT // 4:72], pool_names(v) + ["boffb"], ["btb"])
+
+    def q_b():
+        quant(T.bq[:, CUT:C], T.bp[:, CUT:C], T.bt[:, 4 * CUT:4 * C], ["btb"], ["bqb"])
+        quant(T.bq[:, 0:CUT], T.bp[:, 0:CUT], T.bt[:, 0:4 * CUT], ["bta"], ["bqa"])
+
+    def r_mm(v, x, h):
+        for b in range(4):
+            mm("@%s%d" % (x, b), h[1] - h[0], T.wq[:, 128 * b:128 * b + 128], T.wp[:, 128 * b:128 * b + 128],
+               T["sq%d" % v][:, h[0]:h[1]], T["sp%d" % v][:, h[0]:h[1]], True, False, ["w", "s%d" % v])
+
+    def d_mm(x, h):
+        for b in range(4):
+            mm("@%s%d" % (x, b), h[1] - h[0], T.eq[:, 128 * b:128 * b + 128], T.ep[:, 128 * b:128 * b + 128],
+               T.bq[:, h[0]:h[1]], T.bp[:, h[0]:h[1]], False, True, ["e%d" % b] + ["bq" + c for c in runs(h)])
+
+    def unload(q, bk, tile, o, b, h, res):
+        buf, p = bank(bk)
+        out, in_ = tile[:, o + 4 * h[0] + b:o + 4 * h[1]:4], buf[:, p:p + h[1] - h[0]]
+        if q == "v":
+            ts(out, in_, 0.015625, None, A.mult, None, [bk], res)
+        else:
+            act(out, in_, F.Copy, [bk], res, scale=0.015625)
+
+    def y_read(q, x, b, h):
+        unload(q, "@%s%d" % (x, b), T.yt, 0, b, h, ["yt%s%d" % (c, b) for c in runs(h)])
+
+    def q_y(v, h):
+        quant(T["yq%d" % v][:, h[0]:h[1]], T["yp%d" % v][:, h[0]:h[1]], T.yt[:, 4 * h[0]:4 * h[1]],
+              ["yt%s%d" % (runs(h), b) for b in range(4)], ["y%d%s" % (v, runs(h))])
+
+    def n_mm(v, b, bk, h):
+        mm(bk, h[1] - h[0], T.eq[:, 128 * b:128 * b + 128], T.ep[:, 128 * b:128 * b + 128],
+           T["yq%d" % v][:, h[0]:h[1]], T["yp%d" % v][:, h[0]:h[1]], True, True,
+           ["e%d" % b] + ["y%d%s" % (v, c) for c in runs(h)])
+
+    def n_read(q, v, b, bk, h):
+        unload(q, bk, T.pool, 4 * (M + C * v), b, h, ["n%d%d%s" % (v, b, c) for c in runs(h)])
+
+    def visit(v, after_b):
+        r_mm(v, "n", HB)
+        r_mm(v, "y", HA)
+        pointers(v)
+        read_map(v)
+        q_b()
+        d_mm("n", HB)
+        d_mm("y", HA)
+        for b in range(4):
+            y_read("sv"[b % 2], "n", b, HB)
+        y_read("s", "y", 0, HA)
+        y_read("v", "y", 1, HA)
+        q_y(v, HB)
+        after_b()
+        y_read("s", "y", 2, HA)
+        y_read("v", "y", 3, HA)
+        q_y(v, HA)
+
+    NB = ("@n1", "@n2", "@n3", "@n0")
+
+    def first_bits(v):
+        a_mm(T["yq%d" % v], T["yp%d" % v], "y%db" % v, "@n0", HB)
+
+    def next_addresses(v, gap):
+        w, y = v + 1, ["y%da" % v, "y%db" % v]
+        send(nxt, far, by(T["sq%d" % w][:]), by(T["yq%d" % v][:]), "st%d" % w, y)
+        a_mm(T["yq%d" % v], T["yp%d" % v], "y%da" % v, "@y0", HA)
+        n_mm(v, 0, NB[0], ALL)
+        n_mm(v, 1, NB[1], ALL)
+        bits("@n0", HB)
+        bits("@y0", HA)
+        q_bits()
+        list_mm("@y1", 0)
+        gap()
+        list_scan("@y1")
+        list_u16(w)
+        send(nxt, far, T["la%d" % w][:], T["ao%d" % w][:], "la%d" % w, ["ao%d" % w])
+        send(nxt, far, T["sp%d" % w][:], T["yp%d" % v][:], "st%d" % w, y)
+        n_read("s", v, 0, NB[0], ALL)
+        n_read("s", v, 1, NB[1], ALL)
+        list_f32(w)
+        row_mm("@y2", 0)
+        row_mm("@y3", 1)
+        n_mm(v, 2, NB[2], ALL)
+        n_mm(v, 3, NB[3], ALL)
+        row_read(w, "@y2", 0)
+        row_read(w, "@y3", 1)
+
+    def late_n(v):
+        n_read("s", v, 2, NB[2], ALL)
+        n_read("s", v, 3, NB[3], ALL)
+
+    quant(T.sq0[:], T.sp0[:], T.xin[:], ["xin"], ["s0"])
+    a_mm(T.sq0, T.sp0, "s0", "@n0", ALL)
+    qz(0)
+    qz(1)
+    bits("@n0", ALL)
+    q_bits()
+    list_mm("@n1", 1)
+    qz(2)
+    ts(T.boff[:], T.pn[:, 512:584], 4.0, t4, A.mult, A.add, ["@n1", "pf"], ["boffa", "boffb"])
+    qz(3)
+    quant(T.aq[:, 0:128], T.ap[:, 0:128], T.wa[:], names("wa"), ["qwa"])
+    read_map(0)
+    row_mm("@n3", 0)
+    row_mm("@n0", 1)
+    list_mm("@n2", 0)
+    r_mm(0, "y", ALL)
+    list_scan("@n2")
+    q_b()
+    row_read(0, "@n3", 0)
+    row_read(0, "@n0", 1)
+    list_f32(0)
+    d_mm("y", ALL)
+    dedupe_period()
+    compare("v", 0, range(0, 6))
+    for b in range(4):
+        y_read("sv"[b % 2], "y", b, ALL)
+    q_y(0, HB)
+    first_bits(0)
+    q_y(0, HA)
+    next_addresses(0, lambda: compare("v", 0, range(6, 9)))
+    compare("v", 0, range(9, K16))
+    dedupe(0)
+    compare("s", 1, range(0, 8))
+    late_n(0)
+    for c in (4, 3, 2, 1, 0):
+        scatter(0, (c,))
+        compare("v", 1, range(16 - 2 * c, 18 - 2 * c))
+    dedupe(1)
+
+    visit(1, lambda: first_bits(1))
+    next_addresses(1, lambda: scatter(1, (4,)))
+    compare("s", 2, range(0, 8))
+    late_n(1)
+    scatter(1, (3, 2))
+    compare("v", 2, range(8, 13))
+    scatter(1, (1,))
+    compare("v", 2, range(13, K16))
+    scatter(1, (0,))
+    dedupe(2)
+
+    def last_b():
+        for b in range(4):
+            n_mm(2, b, "@n%d" % b, HB)
+
+    visit(2, last_b)
+    send(home, near, by(T.oq[:, 0:C]), by(T.yq2[:]), "st3", ["y2a", "y2b"])
+    send(home, near, T.op[:, 0:C], T.yp2[:], "st3", ["y2a", "y2b"])
+    for b in range(4):
+        n_mm(2, b, "@y%d" % b, HA)
+    for b in range(4):
+        n_read("s", 2, b, "@n%d" % b, HB)
+    for b in range(4):
+        n_read("s", 2, b, "@y%d" % b, HA)
+    scatter(2, (4, 3, 2, 1, 0))
+
+    win, c1, c2, c3 = T.pool[:], 128, 280, 400
+
+    def g_m(q, a, b, res, out):
+        gather(q, T.mt[:, 4 * a:4 * b], win, T.moff[:, a // 4:b // 4], pool_names(NV) + [res], [out])
+
+    def q_m(a, b, reads, out):
+        quant(T.oq[:, C + a:C + b], T.op[:, C + a:C + b], T.mt[:, 4 * a:4 * b], reads, [out])
+
+    def store(q, out, in_, reads):
+        op(q, lambda: (g.sync if q == "y" else S).dma_start(out, in_), reads, [], "out", 16)
+
+    select_scan(T.tab, "tab", 0, c1)
+    select_u16(T.moff, "moffa", 0, c1)
+    g_m("s", 0, c1, "moffa", "mt0")
+    select_scan(T.tab, "tab", c1, M)
+    select_u16(T.moff, "moffb", c1, M)
+    g_m("s", c1, c2, "moffb", "mt1")
+    g_m("v", c2, c3, "moffb", "mt2")
+    mm("@y0", C, T.wq[:, 0:128], T.wp[:, 0:128], T.oq[:, 0:C], T.op[:, 0:C], True, True, ["w", "s3"])
+    q_m(0, c1, ["mt0"], "o0")
+    store("y", T.oc[:, 0:4 * (C + c1)], by(T.oq[:, 0:C + c1]), ["s3", "o0"])
+    g_m("v", c3, M, "moffb", "mt3")
+    q_m(c1, M, ["mt1", "mt2", "mt3"], "o1")
+    act(T.yo[:], T.py[:, 0:C], F.Copy, ["@y0"], ["yo"])
+    store("y", T.oc[:, 4 * (C + c1):4 * (C + M)], by(T.oq[:, C + c1:C + M]), ["o1"])
+    store("s", T.y[:], T.yo[:], ["yo"])
+    for k in range(4):
+        store("ys"[k % 2], T.osc[4 * k:4 * k + 4, :], T.op[32 * k:32 * k + 4, :], ["o0", "o1", "s3"])
+    _emit(g, T, ops)

@@ -3,51 +3,30 @@ from concourse.mybir import dt, AluOpType, AxisListType, ActivationFunctionType
 C, M, NV = 288, 512, 3
 K16 = C // 16
 CH = 64
+SEG = CH + 2
 POOL = M + NV * C
 BIG, KEEP = 16384.0, 8192.0
 CUT = 160
 HA, HB, ALL = (0, CUT), (CUT, C), (0, C)
 
 Q4, U8, BF, F32, I32, U16 = "float8_e4m3fn_x4", "uint8", "bfloat16", "float32", "int32", "uint16"
-SCRATCH = {
-    "xin": ("sbuf", [128, 4 * C], BF), "uin": ("sbuf", [128, 512], BF), "pool": ("sbuf", [128, 4 * POOL], BF),
-    "wq": ("sbuf", [128, 512], Q4), "wp": ("sbuf", [128, 512], U8),
-    "uq": ("sbuf", [128, 128], Q4), "up": ("sbuf", [128, 128], U8),
-    "oq": ("sbuf", [128, C + M], Q4), "op": ("sbuf", [128, C + M], U8),
-    "bt": ("sbuf", [128, 4 * C], BF), "bq": ("sbuf", [128, C], Q4), "bp": ("sbuf", [128, C], U8),
-    "yt": ("sbuf", [128, 4 * C], BF), "mt": ("sbuf", [128, 4 * M], BF), "yo": ("sbuf", [128, C], F32),
-    "ft": ("sbuf", [128, 512], BF), "fq": ("sbuf", [128, 384], Q4), "fp": ("sbuf", [128, 384], U8),
-    "ze": ("sbuf", [128, 528], BF), "zz": ("sbuf", [128, 528], BF),
-    "wa": ("sbuf", [128, 512], BF), "wb": ("sbuf", [128, 512], BF),
-    "eq": ("sbuf", [128, 512], Q4), "ep": ("sbuf", [128, 512], U8),
-    "zq": ("sbuf", [128, 512], Q4), "zp": ("sbuf", [128, 512], U8),
-    "aq": ("sbuf", [128, 256], Q4), "ap": ("sbuf", [128, 256], U8),
-    "pi": ("sbuf", [128, 8], I32), "pj": ("sbuf", [128, 8], I32), "pf": ("sbuf", [128, 8], F32),
-    "j16": ("sbuf", [128, 16], F32), "d16": ("sbuf", [128, 16], F32), "col": ("sbuf", [128, 8], F32),
-    "gm": ("sbuf", [128, 8], F32), "c4b": ("sbuf", [128, 12], F32),
-    "mi": ("sbuf", [128, 192], BF), "mk": ("sbuf", [128, 192], BF), "idj": ("sbuf", [128, 128], BF),
-    "c4": ("sbuf", [128, 512], BF), "cdi": ("sbuf", [128, 256], BF), "cd": ("sbuf", [128, K16 * CH], BF),
-    "dni": ("sbuf", [128, 20], F32), "dn": ("sbuf", [128, 20], F32),
-    "tab": ("sbuf", [128, M + CH], F32), "val": ("sbuf", [128, NV * C], F32),
-    "sca": ("sbuf", [128, 72], F32), "prow": ("sbuf", [128, C], F32), "scp": ("sbuf", [128, M], F32),
-    "boff": ("sbuf", [128, 72], U16), "moff": ("sbuf", [128, 128], U16),
-    "ne": ("sbuf", [128, K16 * CH], BF), "scd": ("sbuf", [128, K16 * CH], BF),
-    "t1": ("sbuf", [128, K16], F32), "t2": ("sbuf", [128, K16], F32),
-    "py": ("psum", [128, 2048], F32), "pn": ("psum", [128, 2048], F32),
-}
+SCRATCH = {"py": ("psum", [128, 2048], F32), "pn": ("psum", [128, 2048], F32)}
+for _n, _w, _d in (
+        ("xin", 4 * C, BF), ("uin", 512, BF), ("pool", 4 * POOL, BF), ("wq", 512, Q4), ("wp", 512, U8),
+        ("uq", 128, Q4), ("up", 128, U8), ("oq", C + M, Q4), ("op", C + M, U8), ("bt", 4 * C, BF), ("bq", C, Q4),
+        ("bp", C, U8), ("yt", 4 * C, BF), ("mt", 4 * M, BF), ("yo", C, F32), ("ft", 512, BF), ("fq", 384, Q4),
+        ("fp", 384, U8), ("ze", 528, BF), ("zz", 528, BF), ("wa", 512, BF), ("wb", 512, BF), ("eq", 512, Q4),
+        ("ep", 512, U8), ("zq", 512, Q4), ("zp", 512, U8), ("aq", 256, Q4), ("ap", 256, U8), ("pi", 8, I32),
+        ("pj", 8, I32), ("pf", 8, F32), ("j16", 16, F32), ("d16", 16, F32), ("col", 8, F32), ("gm", 8, F32),
+        ("c4b", 12, F32), ("mi", 192, BF), ("mk", 192, BF), ("idj", 128, BF), ("c4", 512, BF),
+        ("cdi", 4 * SEG, BF), ("cdj", 4 * SEG, BF), ("cd", K16 * SEG, BF), ("tab", M + 4 * CH, F32),
+        ("val", NV * C, F32), ("sca", 72, F32), ("prow", C, F32), ("scp", M, F32), ("boff", 72, U16),
+        ("moff", 128, U16), ("ne0", K16 * SEG, BF), ("ne1", K16 * SEG, BF), ("scd", K16 * SEG, BF)):
+    SCRATCH[_n] = ("sbuf", [128, _w], _d)
 for _t in range(NV):
-    SCRATCH["sq%d" % _t] = ("sbuf", [128, C], Q4)
-    SCRATCH["sp%d" % _t] = ("sbuf", [128, C], U8)
-    SCRATCH["yq%d" % _t] = ("sbuf", [128, C], Q4)
-    SCRATCH["yp%d" % _t] = ("sbuf", [128, C], U8)
-    SCRATCH["af%d" % _t] = ("sbuf", [128, K16], F32)
-    SCRATCH["am%d" % _t] = ("sbuf", [128, K16], F32)
-    SCRATCH["ar%d" % _t] = ("sbuf", [128, 320], BF)
-    SCRATCH["so%d" % _t] = ("sbuf", [128, K16], U16)
-    if _t:
-        SCRATCH["ao%d" % _t] = ("sbuf", [128, K16], U16)
-        SCRATCH["la%d" % _t] = ("sbuf", [128, K16], U16)
-        SCRATCH["ls%d" % _t] = ("sbuf", [128, K16], U16)
+    for _n, _w, _d in (("sq", C, Q4), ("sp", C, U8), ("yq", C, Q4), ("yp", C, U8), ("af", K16, F32), ("am", K16, F32),
+                       ("ar", 320, BF), ("so", K16, U16), ("ao", K16, U16), ("la", K16, U16), ("ls", K16, U16)):
+        SCRATCH[_n + str(_t)] = ("sbuf", [128, _w], _d)
 SEMAPHORES = ["cv", "cs", "ct", "cg", "sent", "dx", "du", "dm", "dw", "st1", "st2", "st3",
               "la1", "la2", "ls1", "ls2", "out"]
 COUNTER = {"v": "cv", "s": "cs", "t": "ct", "g": "cg"}
@@ -166,9 +145,11 @@ def rank_program(g, core, T, topo):
     iota(T.idj[:], [[1, 128]], 0, -1, ["idj"])
     iota(T.mi[:, 64:128], [[0, 4], [1, 4], [-1, 4]], 0, 0, ["mi1"])
     iota(T.mi[:, 128:192], [[0, 16], [1, 4]], -3, 0, ["mi2"])
-    iota(T.cdi[:], [[-16, 4], [1, 64]], 0, 0, ["cdi"])
-    iota(T.dni[:], [[0, 5], [-16, 4]], -M, 0, ["dni"])
-    iota(T.tab[:], [[4, M + CH]], 0, 0, ["tab"])
+    iota(T.cdi[:], [[-16, 4], [1, SEG]], 0, 0, ["cdi"])
+    iota(T.cdj[:], [[0, 4], [-4, SEG]], -M, 0, ["cdj"])
+    for t in range(NV):
+        iota(T["ar%d" % t][:, C:320], [[0, 32]], 300, 0, ["art%d" % t])
+    iota(T.tab[:], [[4, M + 4 * CH]], 0, 0, ["tab"])
     iota(T.val[:], [[4, NV * C]], 4 * M, 0, ["val"])
 
     op("v", lambda: V.memset(T.ze[:], 0.0), [], ["ze"])
@@ -212,24 +193,23 @@ def rank_program(g, core, T, topo):
     quant(T.uq[:], T.up[:], T.uin[:], ["uin"], ["uq"])
     ts(T.c4b[:, 8:12], T.c4b[:, 4:8], KEEP, None, A.mult, None, ["c4b1"], ["c4b2"])
     ts(T.col[:, 2:3], w4, 2.5, -KEEP, A.is_lt, A.mult, ["pf"], ["col2"])
-    ts(T.cd[:, 0:256], T.cdi[:], cc, -1.0, A.is_equal, A.mult, ["cdi", "pf"], ["cd0"])
+    ts(T.cdi[:], T.cdi[:], cc, None, A.is_equal, None, ["cdi", "pf"], ["cdi"])
     op("v", lambda: V.tensor_tensor(T.c4b[:, 4:8], T.c4b[:, 8:12], T.c4b[:, 0:4], A.add), ["c4b0", "c4b2"], ["c4b1"])
     ts(T.col[:, 3:4], T.col[:, 2:3], t4, None, A.add, None, ["col2", "pf"], ["col3"])
     ts(T.col[:, 4:5], T.col[:, 2:3], -256.0, None, A.add, None, ["col2"], ["col4"])
+    ts(T.col[:, 5:6], T.col[:, 2:3], -256.0, 1024.0, A.add, A.mult, ["col2"], ["col5"])
     for i in range(4):
         act(T.c4[:, i:512:4], T.idj[:], F.Identity, ["idj", "c4b1"], ["c4%d" % i], scale=0.0, bias=T.c4b[:, 4 + i:5 + i])
-    ts(T.dn[:], T.dni[:], cc, None, A.subtract, None, ["dni", "pf"], ["dn"])
-    ts(T.cd[:, 0:256:64], T.j16[:, 0:4], 0.0, 8.0, A.mult, A.add, ["j16"], ["cd0"])
-    for t in range(NV):
-        op("v", lambda t=t: V.memset(T["ar%d" % t][:, C:320], 300.0), [], ["art%d" % t])
-
-    def dedupe_period():
-        for i, (a, b) in enumerate(((256, 512), (512, 1024), (1024, K16 * CH))):
-            op("v", lambda a=a, b=b: V.tensor_copy(T.cd[:, a:b], T.cd[:, 0:b - a]),
-               ["cd%d" % j for j in range(i + 1)], ["cd%d" % (i + 1)])
+    for t in range(2):
+        act(T["ne%d" % t][:, SEG - 1:K16 * SEG:SEG], T.idj[:, 0:K16], F.Identity, ["idj"], ["nez%d" % t],
+            scale=0.0, bias=1024.0)
 
     C4 = ["c40", "c41", "c42", "c43"]
-    CD = ["cd0", "cd1", "cd2", "cd3"]
+    CD = ["cd0", "cd0b", "cd1", "cd2", "cd3", "cd4"]
+
+    def cd_copy(i):
+        w = min(4 * SEG, (K16 - 4 * i) * SEG)
+        act(T.cd[:, 4 * SEG * i:4 * SEG * i + w], T.cd[:, 0:w], F.Copy, ["cd0", "cd0b"], ["cd%d" % i])
 
     def qz(b):
         quant(T.zq[:, 128 * b:128 * b + 128], T.zp[:, 128 * b:128 * b + 128], T.zz[:, 3 - b:515 - b],
@@ -272,25 +252,29 @@ def rank_program(g, core, T, topo):
         ts(T["ao%d" % v][:], T.sca[:, 3:72:4], T.col[:, 2:3], None, A.add, None, ["sca", "col2"], ["ao%d" % v])
 
     def list_f32(v):
-        act(T["af%d" % v][:], T.sca[:, 3:72:4], F.Identity, ["sca", "col2"], ["af%d" % v], bias=T.col[:, 2:3])
         act(T["am%d" % v][:], T.sca[:, 3:72:4], F.Identity, ["sca", "col4"], ["am%d" % v], bias=T.col[:, 4:5])
+        act(T["af%d" % v][:], T.sca[:, 3:72:4], F.Identity, ["sca", "col5"], ["af%d" % v], scale=1024.0, bias=T.col[:, 5:6])
 
     def compare(q, v, ks):
         for k in ks:
-            c0 = CH * (k // 4)
-            o, i, s = T.ne[:, CH * k:CH * k + CH], T["ar%d" % v][:, c0:c0 + CH], T["am%d" % v][:, k:k + 1]
+            c0, x = CH * (k // 4), v % 2
+            o, i, s = T["ne%d" % x][:, SEG * k:SEG * k + CH], T["ar%d" % v][:, c0:c0 + CH], T["am%d" % v][:, k:k + 1]
             rd = ["ar%d%d" % (v, t) for t in range(4)] + ["art%d" % v, "am%d" % v]
             if q == "v":
-                ts(o, i, s, None, A.not_equal, None, rd, ["ne%d" % k])
+                ts(o, i, s, 1024.0, A.not_equal, A.mult, rd, ["ne%d_%d" % (x, k)])
             else:
-                act(o, i, F.Abs, rd, ["ne%d" % k], scale=-1.0, bias=s)
+                act(o, i, F.Abs, rd + ["af%d" % v], ["ne%d_%d" % (x, k)], scale=-1024.0, bias=T["af%d" % v][:, k:k + 1])
 
-    def dedupe(v):
-        op("v", lambda: V.tensor_tensor_scan(T.scd[:], T.cd[:], T.ne[:], 0.0, A.add, A.min),
-           CD + ["ne%d" % k for k in range(K16)], ["scd"])
-        op("v", lambda: V.tensor_tensor(T.t1[:], T.scd[:, CH - 1:K16 * CH:CH], T.dn[:, 0:K16], A.mult), ["scd", "dn"], ["t1"])
-        op("v", lambda: V.tensor_tensor(T.t2[:], T.t1[:], T["af%d" % v][:], A.max), ["t1", "af%d" % v], ["t2"])
-        op("v", lambda: V.tensor_copy(T["so%d" % v][:], T.t2[:]), ["t2"], ["so%d" % v])
+    def own(v):
+        act(T["ne%d" % (v % 2)][:, CH:K16 * SEG:SEG], T["am%d" % v][:], F.Copy, ["am%d" % v], ["neo%d" % (v % 2)],
+            scale=-1.0)
+
+    def dedupe(v, gap):
+        x = v % 2
+        op("v", lambda: V.tensor_tensor_scan(T.scd[:], T.cd[:], T["ne%d" % x][:], 0.0, A.add, A.min),
+           CD + ["neo%d" % x, "nez%d" % x] + ["ne%d_%d" % (x, k) for k in range(K16)], ["scd"])
+        gap()
+        ts(T["so%d" % v][:], T.scd[:, CH:K16 * SEG:SEG], -1.0, 256.0, A.mult, A.add, ["scd"], ["so%d" % v])
         if v:
             send(nxt, far, T["ls%d" % v][:], T["so%d" % v][:], "ls%d" % v, ["so%d" % v])
 
@@ -438,39 +422,48 @@ def rank_program(g, core, T, topo):
     row_mm("@n0", 1)
     list_mm("@n2", 0)
     r_mm(0, "y", ALL)
-    list_scan("@n2")
     q_b()
     row_read(0, "@n3", 0)
     row_read(0, "@n0", 1)
-    list_f32(0)
     d_mm("y", ALL)
-    dedupe_period()
-    compare("v", 0, range(0, 6))
+    op("v", lambda: V.tensor_tensor(T.cd[:, 0:4 * SEG], T.cdi[:], T.cdj[:], A.mult), ["cdi", "cdj"], ["cd0"])
+    list_scan("@n2")
+    op("v", lambda: V.memset(T.cd[:, 0:4 * SEG:SEG], 4096.0), [], ["cd0"])
+    op("v", lambda: V.memset(T.cd[:, CH:4 * SEG:SEG], 256.0), ["cd0"], ["cd0b"])
+    list_f32(0)
+    cd_copy(1)
+    compare("v", 0, range(0, 4))
     for b in range(4):
         y_read("sv"[b % 2], "y", b, ALL)
+    own(0)
+    cd_copy(2)
+    cd_copy(3)
+    cd_copy(4)
+    compare("s", 0, range(15, K16))
     q_y(0, HB)
     first_bits(0)
     q_y(0, HA)
-    next_addresses(0, lambda: compare("v", 0, range(6, 9)))
-    compare("v", 0, range(9, K16))
-    dedupe(0)
-    compare("s", 1, range(0, 8))
+    next_addresses(0, lambda: compare("v", 0, range(4, 7)))
+    compare("v", 0, range(7, 15))
+    dedupe(0, lambda: None)
+    own(1)
+    compare("s", 1, range(0, 14))
     late_n(0)
-    for c in (4, 3, 2, 1, 0):
+    for c in (4, 3, 2, 1):
         scatter(0, (c,))
-        compare("v", 1, range(16 - 2 * c, 18 - 2 * c))
-    dedupe(1)
+        compare("v", 1, (13 + c,))
+    dedupe(1, lambda: scatter(0, (0,)))
 
     visit(1, lambda: first_bits(1))
     next_addresses(1, lambda: scatter(1, (4,)))
-    compare("s", 2, range(0, 8))
+    own(2)
+    compare("s", 2, range(0, 9))
     late_n(1)
     scatter(1, (3, 2))
-    compare("v", 2, range(8, 13))
+    compare("v", 2, range(9, 14))
     scatter(1, (1,))
-    compare("v", 2, range(13, K16))
-    scatter(1, (0,))
-    dedupe(2)
+    compare("v", 2, range(14, K16))
+    dedupe(2, lambda: scatter(1, (0,)))
 
     def last_b():
         for b in range(4):

@@ -14,12 +14,12 @@ SCRATCH = {"py": ("psum", [128, 2048], F32), "pn": ("psum", [128, 2048], F32)}
 for _n, _w, _d in (
         ("xin", 4 * C, BF), ("uin", 512, BF), ("pool", 4 * POOL, BF), ("wq", 512, Q4), ("wp", 512, U8),
         ("uq", 128, Q4), ("up", 128, U8), ("oq", C + M, Q4), ("op", C + M, U8), ("bt", 4 * C, BF), ("bq", C, Q4),
-        ("bp", C, U8), ("yt", 4 * C, BF), ("mt", 4 * M, BF), ("yo", C, F32), ("ft", 512, BF), ("fq", 384, Q4),
+        ("bp", C, U8), ("yt", 4 * C, BF), ("mt", 4 * M, BF), ("yo", C, F32), ("ft", 576, BF), ("fq", 384, Q4),
         ("fp", 384, U8), ("ze", 528, BF), ("zz", 528, BF), ("wa", 512, BF), ("wb", 512, BF), ("eq", 512, Q4),
         ("ep", 512, U8), ("zq", 512, Q4), ("zp", 512, U8), ("aq", 256, Q4), ("ap", 256, U8), ("pi", 8, I32),
-        ("pj", 8, I32), ("pf", 8, F32), ("j16", 16, F32), ("d16", 16, F32), ("col", 8, F32), ("gm", 8, F32),
-        ("c4b", 12, F32), ("mi", 192, BF), ("mk", 192, BF), ("idj", 128, BF), ("c4", 512, BF),
-        ("cdi", 4 * SEG, BF), ("cdj", 4 * SEG, BF), ("cd", K16 * SEG, BF), ("tab", M + 4 * CH, F32),
+        ("pj", 8, I32), ("pf", 8, F32), ("j16", 16, F32), ("jm", 4, F32), ("spare", 8, F32), ("d16", 16, F32),
+        ("col", 8, F32), ("gm", 8, F32), ("c4b", 12, F32), ("mi", 192, BF), ("mk", 192, BF), ("idj", 128, BF),
+        ("c4", 512, BF), ("cdi", 4 * SEG, BF), ("cd", K16 * SEG, BF), ("tab", M + 4 * CH, F32),
         ("val", NV * C, F32), ("sca", 72, F32), ("prow", C, F32), ("scp", M, F32), ("boff", 72, U16),
         ("moff", 128, U16), ("ne0", K16 * SEG, BF), ("ne1", K16 * SEG, BF), ("scd", K16 * SEG, BF)):
     SCRATCH[_n] = ("sbuf", [128, _w], _d)
@@ -124,6 +124,9 @@ def rank_program(g, core, T, topo):
     def arrive(sem, count, writes):
         op("g", None, [], writes, sem, count)
 
+    def nop():
+        pass
+
     far, near = topo.mask(core, nxt), topo.mask(core, home)
     nfar, nnear = bin(far).count("1"), bin(near).count("1")
     for t in (1, 2):
@@ -146,60 +149,56 @@ def rank_program(g, core, T, topo):
     iota(T.mi[:, 64:128], [[0, 4], [1, 4], [-1, 4]], 0, 0, ["mi1"])
     iota(T.mi[:, 128:192], [[0, 16], [1, 4]], -3, 0, ["mi2"])
     iota(T.cdi[:], [[-16, 4], [1, SEG]], 0, 0, ["cdi"])
-    iota(T.cdj[:], [[0, 4], [-4, SEG]], -M, 0, ["cdj"])
-    for t in range(NV):
-        iota(T["ar%d" % t][:, C:320], [[0, 32]], 300, 0, ["art%d" % t])
+    iota(T.ar0[:, C:320], [[0, 32]], 300, 0, ["art0"])
     iota(T.tab[:], [[4, M + 4 * CH]], 0, 0, ["tab"])
-    iota(T.val[:], [[4, NV * C]], 4 * M, 0, ["val"])
+    iota(T.val[:, 0:C], [[4, C]], 4 * M, 0, ["val0"])
+    for t in range(1, NV):
+        iota(T["ar%d" % t][:, C:320], [[0, 32]], 300, 0, ["art%d" % t])
 
+    act(T.jm[:], T.j16[:, 0:4], F.Identity, ["j16"], ["jm"], bias=-1.0)
     op("v", lambda: V.memset(T.ze[:], 0.0), [], ["ze"])
-    op("v", lambda: V.memset(T.ft[:, C:512], 0.0), [], ["ftz"])
+    op("v", lambda: V.memset(T.ft[:, C:576], 0.0), [], ["ftz"])
     ts(T.pj[:, 0:1], T.pi[:, 0:1], 15, None, A.bitwise_and, None, ["pi"], ["pj0"])
     ts(T.pj[:, 1:2], T.pi[:, 0:1], 4, None, A.arith_shift_right, None, ["pi"], ["pj1"])
     ts(T.pj[:, 2:3], T.pi[:, 0:1], 2, 3, A.arith_shift_right, A.bitwise_and, ["pi"], ["pj2"])
     ts(T.pj[:, 3:4], T.pi[:, 0:1], 3, None, A.bitwise_and, None, ["pi"], ["pj3"])
     quant(T.fq[:, 0:128], T.fp[:, 0:128], T.ze[:, 0:512], ["ze"], ["fz0"])
     op("v", lambda: V.tensor_copy(T.pf[:, 0:4], T.pj[:, 0:4]), ["pj0", "pj1", "pj2", "pj3"], ["pf"])
-    quant(T.fq[:, 256:384], T.fp[:, 256:384], T.ze[:, 0:512], ["ze"], ["fz1"])
-    ts(T.d16[:], T.j16[:], cc, 1.0, A.is_lt, A.add, ["j16", "pf"], ["d16"])
     ts(T.mk[:, 0:64], T.mi[:, 0:64], 0.0, None, A.is_equal, None, ["mi0"], ["mk0"])
-    op("v", lambda: V.tensor_reduce(T.col[:, 0:1], T.d16[:], AxisListType.X, A.mult), ["d16"], ["col0"])
+    ts(T.d16[:], T.j16[:], cc, 1.0, A.is_lt, A.add, ["j16", "pf"], ["d16"])
     ts(T.c4b[:, 0:4], T.j16[:, 0:4], w4, -BIG, A.is_equal, A.mult, ["j16", "pf"], ["c4b0"])
+    op("v", lambda: V.tensor_reduce(T.col[:, 0:1], T.d16[:], AxisListType.X, A.mult), ["d16"], ["col0"])
+    ts(T.c4b[:, 8:12], T.jm[:], w4, KEEP, A.is_equal, A.mult, ["jm", "pf"], ["c4b2"])
     ts(T.col[:, 1:2], cc, 8.5, T.col[:, 0:1], A.is_lt, A.mult, ["pf", "col0"], ["col1"])
-    ts(T.c4b[:, 4:8], T.j16[:, 0:4], -1.0, w4, A.add, A.is_equal, ["j16", "pf"], ["c4b1"])
+    ts(T.col[:, 2:3], w4, 2.5, -KEEP, A.is_lt, A.mult, ["pf"], ["col2"])
     ts(T.gm[:], T.j16[:, 0:8], grp, T.col[:, 1:2], A.is_equal, A.mult, ["j16", "pf", "col1"], ["gm"])
     ts(T.ze[:, 3:512:4], T.idj[:], 0.0, 64.0, A.is_equal, A.mult, ["idj"], ["ze"])
+    op("v", lambda: V.tensor_tensor(T.c4b[:, 4:8], T.c4b[:, 8:12], T.c4b[:, 0:4], A.add), ["c4b0", "c4b2"], ["c4b1"])
+    act(T.spare[:, 4:5], cc, F.Identity, ["pf"], ["sp4"], scale=-4.0, bias=-float(M))
+    act(T.spare[:, 0:4], T.j16[:, 0:4], F.Identity, ["j16", "sp4"], ["spare"], scale=-64.0, bias=T.spare[:, 4:5])
 
-    def weights(q, tile, mask, ms, name):
-        for m in ms:
-            o, i, s = tile[:, 64 * m:64 * m + 64], T.mk[:, 64 * mask:64 * mask + 64], T.gm[:, m:m + 1]
-            if q == "v":
-                ts(o, i, s, None, A.mult, None, ["mk%d" % mask, "gm"], [name + str(m)])
-            else:
-                act(o, i, F.Copy, ["mk%d" % mask, "gm"], [name + str(m)], scale=s)
+    def weights(tile, mask, name):
+        for m in range(8):
+            act(tile[:, 64 * m:64 * m + 64], T.mk[:, 64 * mask:64 * mask + 64], F.Copy, ["mk%d" % mask, "gm"],
+                [name + str(m)], scale=T.gm[:, m:m + 1])
 
     def names(name):
         return [name + str(m) for m in range(8)]
 
-    weights("s", T.wb, 0, range(4, 8), "wb")
-    weights("v", T.wb, 0, range(0, 4), "wb")
+    weights(T.wb, 0, "wb")
     ts(T.mk[:, 64:192], T.mi[:, 64:192], 0.0, None, A.is_equal, None, ["mi1", "mi2"], ["mk1", "mk2"])
     op("v", lambda: V.memset(T.zz[:, 512:528], 0.0), [], ["zzt"])
-    weights("s", T.zz, 2, range(8), "zz")
-    weights("s", T.wa, 1, range(8), "wa")
+    weights(T.wa, 1, "wa")
+    weights(T.zz, 2, "zz")
     for b in range(4):
         quant(T.eq[:, 128 * b:128 * b + 128], T.ep[:, 128 * b:128 * b + 128], T.ze[:, 3 - b:515 - b], ["ze"], ["e%d" % b])
     quant(T.aq[:, 128:256], T.ap[:, 128:256], T.wb[:], names("wb"), ["qwb"])
     quant(T.uq[:], T.up[:], T.uin[:], ["uin"], ["uq"])
-    ts(T.c4b[:, 8:12], T.c4b[:, 4:8], KEEP, None, A.mult, None, ["c4b1"], ["c4b2"])
-    ts(T.col[:, 2:3], w4, 2.5, -KEEP, A.is_lt, A.mult, ["pf"], ["col2"])
-    ts(T.cdi[:], T.cdi[:], cc, None, A.is_equal, None, ["cdi", "pf"], ["cdi"])
-    op("v", lambda: V.tensor_tensor(T.c4b[:, 4:8], T.c4b[:, 8:12], T.c4b[:, 0:4], A.add), ["c4b0", "c4b2"], ["c4b1"])
-    ts(T.col[:, 3:4], T.col[:, 2:3], t4, None, A.add, None, ["col2", "pf"], ["col3"])
-    ts(T.col[:, 4:5], T.col[:, 2:3], -256.0, None, A.add, None, ["col2"], ["col4"])
-    ts(T.col[:, 5:6], T.col[:, 2:3], -256.0, 1024.0, A.add, A.mult, ["col2"], ["col5"])
     for i in range(4):
         act(T.c4[:, i:512:4], T.idj[:], F.Identity, ["idj", "c4b1"], ["c4%d" % i], scale=0.0, bias=T.c4b[:, 4 + i:5 + i])
+    act(T.col[:, 3:4], T.col[:, 2:3], F.Identity, ["col2", "pf"], ["col3"], bias=t4)
+    act(T.col[:, 4:5], T.col[:, 2:3], F.Identity, ["col2"], ["col4"], bias=-256.0)
+    act(T.col[:, 5:6], T.col[:, 2:3], F.Identity, ["col2"], ["col5"], scale=1024.0, bias=-256.0 * 1024.0)
     for t in range(2):
         act(T["ne%d" % t][:, SEG - 1:K16 * SEG:SEG], T.idj[:, 0:K16], F.Identity, ["idj"], ["nez%d" % t],
             scale=0.0, bias=1024.0)
@@ -207,9 +206,21 @@ def rank_program(g, core, T, topo):
     C4 = ["c40", "c41", "c42", "c43"]
     CD = ["cd0", "cd0b", "cd1", "cd2", "cd3", "cd4"]
 
+    def cd_part(r):
+        ts(T.cd[:, SEG * r:SEG * r + SEG], T.cdi[:, SEG * r:SEG * r + SEG], cc, T.spare[:, r:r + 1],
+           A.is_equal, A.mult, ["cdi", "pf", "spare"], ["cdp%d" % r])
+
+    def cd_ends():
+        parts = ["cdp%d" % r for r in range(4)]
+        act(T.cd[:, 0:4 * SEG:SEG], T.idj[:, 0:4], F.Identity, ["idj"], parts + ["cd0"], scale=0.0, bias=4096.0)
+        act(T.cd[:, CH:4 * SEG:SEG], T.idj[:, 0:4], F.Identity, ["idj", "cd0"], ["cd0b"], scale=0.0, bias=256.0)
+
     def cd_copy(i):
         w = min(4 * SEG, (K16 - 4 * i) * SEG)
         act(T.cd[:, 4 * SEG * i:4 * SEG * i + w], T.cd[:, 0:w], F.Copy, ["cd0", "cd0b"], ["cd%d" % i])
+
+    def val_of(v):
+        act(T.val[:, C * v:C * v + C], T.val[:, 0:C], F.Identity, ["val0"], ["val%d" % v], bias=4.0 * C * v)
 
     def qz(b):
         quant(T.zq[:, 128 * b:128 * b + 128], T.zp[:, 128 * b:128 * b + 128], T.zz[:, 3 - b:515 - b],
@@ -223,7 +234,7 @@ def rank_program(g, core, T, topo):
         ts(T.ft[:, h[0]:h[1]], buf[:, o:o + h[1] - h[0]], 0.0, None, A.is_gt, None, [bk], ["ft" + c for c in runs(h)])
 
     def q_bits():
-        quant(T.fq[:, 128:256], T.fp[:, 128:256], T.ft[:], ["fta", "ftb", "ftz"], ["fq"])
+        quant(T.fq[:, 128:272], T.fp[:, 128:272], T.ft[:], ["fta", "ftb", "ftz"], ["fq"])
 
     def list_mm(bk, which):
         o = 128 * which
@@ -234,7 +245,7 @@ def rank_program(g, core, T, topo):
         for i, o in ((0, 128), (1, 56)):
             t = 2 * half + i
             mm(bk, 144, T.zq[:, 128 * t:128 * t + 128], T.zp[:, 128 * t:128 * t + 128],
-               T.fq[:, o:o + 144], T.fp[:, o:o + 144], i == 0, i == 1, ["fq", "fz0", "fz1", "z%d" % t])
+               T.fq[:, o:o + 144], T.fp[:, o:o + 144], i == 0, i == 1, ["fq", "fz0", "z%d" % t])
 
     def row_read(v, bk, half):
         buf, o = bank(bk)
@@ -284,7 +295,7 @@ def rank_program(g, core, T, topo):
             a, b = 4 * c, min(4 * c + 4, K16)
             op("v", lambda a=a, b=b: V.tensor_copy(T.tab[:].indirect(T[name][:, a:b]),
                                                    T.val[:, C * v + 16 * a:C * v + 16 * b]),
-               [name, "val"], ["tab"])
+               [name, "val%d" % v], ["tab"])
 
     def pool_names(v):
         return ["pool"] + ["n%d%d%s" % (t, b, c) for t in range(v) for b in range(4) for c in "ab"]
@@ -354,7 +365,7 @@ def rank_program(g, core, T, topo):
     def n_read(q, v, b, bk, h):
         unload(q, bk, T.pool, 4 * (M + C * v), b, h, ["n%d%d%s" % (v, b, c) for c in runs(h)])
 
-    def visit(v, after_b):
+    def guests(v):
         r_mm(v, "n", HB)
         r_mm(v, "y", HA)
         pointers(v)
@@ -362,50 +373,43 @@ def rank_program(g, core, T, topo):
         q_b()
         d_mm("n", HB)
         d_mm("y", HA)
-        for b in range(4):
-            y_read("sv"[b % 2], "n", b, HB)
-        y_read("s", "y", 0, HA)
-        y_read("v", "y", 1, HA)
-        q_y(v, HB)
-        after_b()
-        y_read("s", "y", 2, HA)
-        y_read("v", "y", 3, HA)
-        q_y(v, HA)
 
     NB = ("@n1", "@n2", "@n3", "@n0")
 
     def first_bits(v):
         a_mm(T["yq%d" % v], T["yp%d" % v], "y%db" % v, "@n0", HB)
 
-    def next_addresses(v, gap):
+    def next_addresses(v, gap0, gap1):
         w, y = v + 1, ["y%da" % v, "y%db" % v]
         send(nxt, far, by(T["sq%d" % w][:]), by(T["yq%d" % v][:]), "st%d" % w, y)
         a_mm(T["yq%d" % v], T["yp%d" % v], "y%da" % v, "@y0", HA)
         n_mm(v, 0, NB[0], ALL)
         n_mm(v, 1, NB[1], ALL)
         bits("@n0", HB)
+        gap0()
         bits("@y0", HA)
         q_bits()
         list_mm("@y1", 0)
-        gap()
+        row_mm("@y2", 0)
+        row_mm("@y3", 1)
+        gap1()
         list_scan("@y1")
         list_u16(w)
         send(nxt, far, T["la%d" % w][:], T["ao%d" % w][:], "la%d" % w, ["ao%d" % w])
         send(nxt, far, T["sp%d" % w][:], T["yp%d" % v][:], "st%d" % w, y)
         n_read("s", v, 0, NB[0], ALL)
         n_read("s", v, 1, NB[1], ALL)
-        list_f32(w)
-        row_mm("@y2", 0)
-        row_mm("@y3", 1)
         n_mm(v, 2, NB[2], ALL)
         n_mm(v, 3, NB[3], ALL)
         row_read(w, "@y2", 0)
         row_read(w, "@y3", 1)
+        list_f32(w)
 
     def late_n(v):
         n_read("s", v, 2, NB[2], ALL)
         n_read("s", v, 3, NB[3], ALL)
 
+    quant(T.aq[:, 0:128], T.ap[:, 0:128], T.wa[:], names("wa"), ["qwa"])
     quant(T.sq0[:], T.sp0[:], T.xin[:], ["xin"], ["s0"])
     a_mm(T.sq0, T.sp0, "s0", "@n0", ALL)
     qz(0)
@@ -413,63 +417,78 @@ def rank_program(g, core, T, topo):
     bits("@n0", ALL)
     q_bits()
     list_mm("@n1", 1)
+    list_mm("@n2", 0)
     qz(2)
-    ts(T.boff[:], T.pn[:, 512:584], 4.0, t4, A.mult, A.add, ["@n1", "pf"], ["boffa", "boffb"])
     qz(3)
-    quant(T.aq[:, 0:128], T.ap[:, 0:128], T.wa[:], names("wa"), ["qwa"])
+    ts(T.boff[:], T.pn[:, 512:584], 4.0, t4, A.mult, A.add, ["@n1", "pf"], ["boffa", "boffb"])
+    list_scan("@n2")
     read_map(0)
     row_mm("@n3", 0)
     row_mm("@n0", 1)
-    list_mm("@n2", 0)
     r_mm(0, "y", ALL)
     q_b()
     row_read(0, "@n3", 0)
     row_read(0, "@n0", 1)
-    d_mm("y", ALL)
-    op("v", lambda: V.tensor_tensor(T.cd[:, 0:4 * SEG], T.cdi[:], T.cdj[:], A.mult), ["cdi", "cdj"], ["cd0"])
-    list_scan("@n2")
-    op("v", lambda: V.memset(T.cd[:, 0:4 * SEG:SEG], 4096.0), [], ["cd0"])
-    op("v", lambda: V.memset(T.cd[:, CH:4 * SEG:SEG], 256.0), ["cd0"], ["cd0b"])
     list_f32(0)
-    cd_copy(1)
-    compare("v", 0, range(0, 4))
+    d_mm("y", ALL)
+    for r in range(4):
+        cd_part(r)
+    compare("v", 0, range(0, 5))
+    compare("s", 0, range(5, 9))
     for b in range(4):
         y_read("sv"[b % 2], "y", b, ALL)
+    cd_ends()
     own(0)
-    cd_copy(2)
-    cd_copy(3)
-    cd_copy(4)
-    compare("s", 0, range(15, K16))
+    compare("s", 0, range(9, 15))
+    for i in (1, 2, 3, 4):
+        cd_copy(i)
     q_y(0, HB)
     first_bits(0)
     q_y(0, HA)
-    next_addresses(0, lambda: compare("v", 0, range(4, 7)))
-    compare("v", 0, range(7, 15))
-    dedupe(0, lambda: None)
+    next_addresses(0, nop, lambda: compare("v", 0, range(15, K16)))
+    dedupe(0, nop)
     own(1)
-    compare("s", 1, range(0, 14))
+    compare("s", 1, range(0, K16))
     late_n(0)
-    for c in (4, 3, 2, 1):
-        scatter(0, (c,))
-        compare("v", 1, (13 + c,))
+    val_of(1)
+    val_of(2)
+    scatter(0, (4, 3, 2, 1))
     dedupe(1, lambda: scatter(0, (0,)))
 
-    visit(1, lambda: first_bits(1))
-    next_addresses(1, lambda: scatter(1, (4,)))
+    guests(1)
+    scatter(1, (4,))
+    for b in range(4):
+        y_read("sv"[b % 2], "n", b, HB)
+    y_read("s", "y", 0, HA)
+    y_read("v", "y", 1, HA)
+    q_y(1, HB)
+    first_bits(1)
+    y_read("s", "y", 2, HA)
+    y_read("v", "y", 3, HA)
+    q_y(1, HA)
+    next_addresses(1, lambda: scatter(1, (3,)), lambda: scatter(1, (2,)))
     own(2)
     compare("s", 2, range(0, 9))
     late_n(1)
-    scatter(1, (3, 2))
-    compare("v", 2, range(9, 14))
     scatter(1, (1,))
-    compare("v", 2, range(14, K16))
-    dedupe(2, lambda: scatter(1, (0,)))
+    compare("v", 2, range(9, 13))
+    scatter(1, (0,))
+    compare("v", 2, range(13, K16))
+    dedupe(2, nop)
 
-    def last_b():
-        for b in range(4):
-            n_mm(2, b, "@n%d" % b, HB)
-
-    visit(2, last_b)
+    guests(2)
+    for b in range(4):
+        y_read("svss"[b], "n", b, HB)
+    scatter(2, (4, 3))
+    y_read("s", "y", 0, HA)
+    y_read("s", "y", 1, HA)
+    q_y(2, HB)
+    for b in range(4):
+        n_mm(2, b, "@n%d" % b, HB)
+    scatter(2, (2,))
+    y_read("s", "y", 2, HA)
+    y_read("s", "y", 3, HA)
+    q_y(2, HA)
     send(home, near, by(T.oq[:, 0:C]), by(T.yq2[:]), "st3", ["y2a", "y2b"])
     send(home, near, T.op[:, 0:C], T.yp2[:], "st3", ["y2a", "y2b"])
     for b in range(4):
@@ -478,9 +497,9 @@ def rank_program(g, core, T, topo):
         n_read("s", 2, b, "@n%d" % b, HB)
     for b in range(4):
         n_read("s", 2, b, "@y%d" % b, HA)
-    scatter(2, (4, 3, 2, 1, 0))
+    scatter(2, (1, 0))
 
-    win, c1, c2, c3 = T.pool[:], 128, 280, 400
+    win, c1, c2, c3 = T.pool[:], 128, 304, 384
 
     def g_m(q, a, b, res, out):
         gather(q, T.mt[:, 4 * a:4 * b], win, T.moff[:, a // 4:b // 4], pool_names(NV) + [res], [out])
@@ -497,15 +516,17 @@ def rank_program(g, core, T, topo):
     select_scan(T.tab, "tab", c1, M)
     select_u16(T.moff, "moffb", c1, M)
     g_m("s", c1, c2, "moffb", "mt1")
-    g_m("v", c2, c3, "moffb", "mt2")
+    g_m("v", c3, M, "moffb", "mt3")
     mm("@y0", C, T.wq[:, 0:128], T.wp[:, 0:128], T.oq[:, 0:C], T.op[:, 0:C], True, True, ["w", "s3"])
     q_m(0, c1, ["mt0"], "o0")
+    q_m(c3, M, ["mt3"], "o2")
     store("y", T.oc[:, 0:4 * (C + c1)], by(T.oq[:, 0:C + c1]), ["s3", "o0"])
-    g_m("v", c3, M, "moffb", "mt3")
-    q_m(c1, M, ["mt1", "mt2", "mt3"], "o1")
+    store("y", T.oc[:, 4 * (C + c3):4 * (C + M)], by(T.oq[:, C + c3:C + M]), ["o2"])
+    g_m("v", c2, c3, "moffb", "mt2")
+    q_m(c1, c3, ["mt1", "mt2"], "o1")
     act(T.yo[:], T.py[:, 0:C], F.Copy, ["@y0"], ["yo"])
-    store("y", T.oc[:, 4 * (C + c1):4 * (C + M)], by(T.oq[:, C + c1:C + M]), ["o1"])
+    store("y", T.oc[:, 4 * (C + c1):4 * (C + c3)], by(T.oq[:, C + c1:C + c3]), ["o1"])
     store("s", T.y[:], T.yo[:], ["yo"])
     for k in range(4):
-        store("ys"[k % 2], T.osc[4 * k:4 * k + 4, :], T.op[32 * k:32 * k + 4, :], ["o0", "o1", "s3"])
+        store("ys"[k % 2], T.osc[4 * k:4 * k + 4, :], T.op[32 * k:32 * k + 4, :], ["o0", "o1", "o2", "s3"])
     _emit(g, T, ops)

@@ -28,8 +28,27 @@ for _t in range(NV):
                        ("ar", 320, BF), ("so", K16, U16), ("ao", K16, U16), ("la", K16, U16), ("ls", K16, U16)):
         SCRATCH[_n + str(_t)] = ("sbuf", [128, _w], _d)
 SEMAPHORES = ["cv", "cs", "ct", "cg", "sent", "dx", "du", "dm", "dw", "st1", "st2", "st3",
-              "la1", "la2", "ls1", "ls2", "out"]
+              "sa1", "sa2", "sb1", "sb2", "la1", "la2", "ls1", "ls2", "out"]
 COUNTER = {"v": "cv", "s": "cs", "t": "ct", "g": "cg"}
+
+ORDER = list(range(11)) + [
+    16, 29, 32, 33, 17, 31, 34, 35, 11, 19, 36, 58, 38, 12, 28, 18, 21, 41, 13, 47, 39, 40, 45, 14, 46, 84, 42, 83, 15,
+    43, 37, 44, 53, 49, 50, 78, 54, 52, 30, 20, 55, 57, 67, 68, 76, 75, 91, 51, 26, 73, 72, 56, 69, 80, 92, 79, 74, 70,
+    71, 85, 24, 93, 27, 94, 65, 63, 95, 59, 66, 60, 62, 61, 64, 90, 87, 48, 86, 88, 96, 97, 98, 89, 100, 99, 105, 106,
+    81, 101, 22, 82, 102, 103, 107, 104, 114, 108, 119, 113, 111, 110, 116, 23, 109, 115, 77, 112, 121, 133, 124, 118,
+    127, 123, 148, 143, 126, 25, 160, 136, 122, 134, 147, 120, 128, 117, 135, 125, 145, 149, 132, 131, 153, 146, 154,
+    152, 129, 150, 130, 155, 167, 168, 170, 156, 159, 151, 137, 169, 140, 172, 175, 165, 193, 166, 138, 158, 176, 162,
+    141, 164, 177, 185, 142, 173, 178, 157, 184, 161, 181, 163, 144, 223, 182, 196, 197, 179, 183, 180, 194, 190, 186,
+    139, 195, 199, 198, 222, 213, 174, 219, 187, 188, 220, 189, 207, 211, 171, 200, 201, 218, 210, 215, 203, 205, 206,
+    225, 216, 234, 212, 226, 227, 192, 202, 228, 208, 230, 217, 209, 214, 204, 191, 229, 241, 233, 242, 221, 243, 244,
+    235, 245, 236, 239, 237, 246, 231, 248, 240, 247, 249, 250, 238, 252, 261, 253, 254, 262, 263, 251, 260, 256, 255,
+    265, 258, 232, 266, 257, 267, 269, 264, 268, 270, 273, 259, 274, 224, 290, 271, 275, 276, 278, 291, 279, 289, 277,
+    280, 281, 282, 295, 294, 283, 284, 293, 292, 286, 298, 287, 299, 288, 296, 297, 300, 313, 308, 301, 303, 307, 304,
+    272, 311, 312, 285, 328, 322, 306, 321, 317, 319, 314, 302, 320, 309, 310, 305, 327, 315, 329, 318, 323, 334, 331,
+    336, 324, 335, 316, 337, 338, 333, 325, 339, 341, 326, 342, 332, 330, 344, 340, 346, 345, 343, 347, 348, 349, 350,
+    352, 356, 351, 353, 357, 354, 355, 360, 364, 361, 358, 359, 362, 366, 363, 365, 367, 368, 372, 369, 374, 383, 384,
+    385, 378, 386, 375, 380, 388, 389, 382, 371, 373, 379, 381, 377, 376, 391, 387, 390, 370, 393, 395, 397, 394, 396,
+    392, 398, 399, 400, 401, 402, 403, 404, 405]
 
 
 def _emit(g, T, ops):
@@ -37,7 +56,8 @@ def _emit(g, T, ops):
     known = {q: {} for q in queue}
     total, waited = {}, {}
     writer, readers = {}, {}
-    for q, fn, reads, writes, sem, inc in ops:
+    assert sorted(ORDER) == list(range(len(ops)))
+    for q, fn, reads, writes, sem, inc in [ops[i] for i in ORDER]:
         need = [writer[r] for r in list(reads) + list(writes) if r in writer]
         for r in writes:
             need += readers.get(r, [])
@@ -130,7 +150,9 @@ def rank_program(g, core, T, topo):
     far, near = topo.mask(core, nxt), topo.mask(core, home)
     nfar, nnear = bin(far).count("1"), bin(near).count("1")
     for t in (1, 2):
-        arrive("st%d" % t, 2 * nfar, ["s%d" % t])
+        arrive("st%d" % t, nfar, ["p%d" % t])
+        arrive("sa%d" % t, nfar, ["s%da" % t])
+        arrive("sb%d" % t, nfar, ["s%db" % t])
         arrive("la%d" % t, nfar, ["la%d" % t])
         arrive("ls%d" % t, nfar, ["ls%d" % t])
     arrive("st3", 2 * nnear, ["s3"])
@@ -316,7 +338,7 @@ def rank_program(g, core, T, topo):
 
     def pointers(v):
         la = T["la%d" % v]
-        gather("v", T.prow[:, 0:CUT], T.tab[:], la[:, 0:CUT // 16], ["tab", "la%d" % v], ["prowa"])
+        gather("s", T.prow[:, 0:CUT], T.tab[:], la[:, 0:CUT // 16], ["tab", "la%d" % v], ["prowa"])
         gather("s", T.prow[:, CUT:C], T.tab[:], la[:, CUT // 16:K16], ["tab", "la%d" % v], ["prowb"])
         select_scan(T.prow, "prowa", 0, CUT)
         select_scan(T.prow, "prowb", CUT, C)
@@ -335,7 +357,8 @@ def rank_program(g, core, T, topo):
     def r_mm(v, x, h):
         for b in range(4):
             mm("@%s%d" % (x, b), h[1] - h[0], T.wq[:, 128 * b:128 * b + 128], T.wp[:, 128 * b:128 * b + 128],
-               T["sq%d" % v][:, h[0]:h[1]], T["sp%d" % v][:, h[0]:h[1]], True, False, ["w", "s%d" % v])
+               T["sq%d" % v][:, h[0]:h[1]], T["sp%d" % v][:, h[0]:h[1]], True, False,
+               ["w", "p%d" % v, "s%d%s" % (v, runs(h))] if v else ["w", "s0"])
 
     def d_mm(x, h):
         for b in range(4):
@@ -381,7 +404,8 @@ def rank_program(g, core, T, topo):
 
     def next_addresses(v, gap0, gap1):
         w, y = v + 1, ["y%da" % v, "y%db" % v]
-        send(nxt, far, by(T["sq%d" % w][:]), by(T["yq%d" % v][:]), "st%d" % w, y)
+        send(nxt, far, by(T["sq%d" % w][:, CUT:C]), by(T["yq%d" % v][:, CUT:C]), "sb%d" % w, y[1:])
+        send(nxt, far, by(T["sq%d" % w][:, 0:CUT]), by(T["yq%d" % v][:, 0:CUT]), "sa%d" % w, y[:1])
         a_mm(T["yq%d" % v], T["yp%d" % v], "y%da" % v, "@y0", HA)
         n_mm(v, 0, NB[0], ALL)
         n_mm(v, 1, NB[1], ALL)
@@ -425,18 +449,22 @@ def rank_program(g, core, T, topo):
     read_map(0)
     row_mm("@n3", 0)
     row_mm("@n0", 1)
-    r_mm(0, "y", ALL)
-    q_b()
+    r_mm(0, "y", HA)
     row_read(0, "@n3", 0)
     row_read(0, "@n0", 1)
+    r_mm(0, "n", HB)
+    q_b()
     list_f32(0)
-    d_mm("y", ALL)
+    d_mm("n", HB)
+    d_mm("y", HA)
     for r in range(4):
         cd_part(r)
     compare("v", 0, range(0, 5))
     compare("s", 0, range(5, 9))
     for b in range(4):
-        y_read("sv"[b % 2], "y", b, ALL)
+        y_read("sv"[b % 2], "n", b, HB)
+    for b in range(4):
+        y_read("sv"[b % 2], "y", b, HA)
     cd_ends()
     own(0)
     compare("s", 0, range(9, 15))
@@ -468,12 +496,11 @@ def rank_program(g, core, T, topo):
     q_y(1, HA)
     next_addresses(1, lambda: scatter(1, (3,)), lambda: scatter(1, (2,)))
     own(2)
-    compare("s", 2, range(0, 9))
+    compare("s", 2, range(0, 14))
     late_n(1)
     scatter(1, (1,))
-    compare("v", 2, range(9, 13))
     scatter(1, (0,))
-    compare("v", 2, range(13, K16))
+    compare("v", 2, range(14, K16))
     dedupe(2, nop)
 
     guests(2)

@@ -2,85 +2,76 @@ from concourse.mybir import dt, AluOpType, AxisListType, ActivationFunctionType
 
 C, M, NV = 288, 512, 3
 K16 = C // 16
-CH = 64
-SEG = CH + 2
 POOL = M + NV * C
-BIG, KEEP = 16384.0, 8192.0
-CUT = 160
+X = 8.0
+UP = 511.0
+CH, CUT = 64, 160
+FIN, ST = (0, 128, 256, 320, 384, M), (0, 128, 256, M)
+R = CH // 16
+O = [8 * _r * _r + 10 * _r for _r in range(R + 1)]
+PER = O[R]
+NE = PER * (K16 // R) + O[K16 % R]
 HA, HB, ALL = (0, CUT), (CUT, C), (0, C)
-
 Q4, U8, BF, F32, I32, U16 = "float8_e4m3fn_x4", "uint8", "bfloat16", "float32", "int32", "uint16"
 SCRATCH = {"py": ("psum", [128, 2048], F32), "pn": ("psum", [128, 2048], F32)}
 for _n, _w, _d in (
         ("xin", 4 * C, BF), ("uin", 512, BF), ("pool", 4 * POOL, BF), ("wq", 512, Q4), ("wp", 512, U8),
         ("uq", 128, Q4), ("up", 128, U8), ("oq", C + M, Q4), ("op", C + M, U8), ("bt", 4 * C, BF), ("bq", C, Q4),
-        ("bp", C, U8), ("yt", 4 * C, BF), ("mt", 4 * M, BF), ("yo", C, F32), ("ft", 576, BF), ("fq", 384, Q4),
-        ("fp", 384, U8), ("ze", 528, BF), ("zz", 528, BF), ("wa", 512, BF), ("wb", 512, BF), ("eq", 512, Q4),
+        ("bp", C, U8), ("yt", 4 * C, BF), ("mt", 4 * M, BF), ("yo", C, F32), ("ft", 672, BF), ("fq", 400, Q4),
+        ("fp", 400, U8), ("ze", 528, BF), ("zz", 528, BF), ("wa", 512, BF), ("wb", 512, BF), ("eq", 512, Q4),
         ("ep", 512, U8), ("zq", 512, Q4), ("zp", 512, U8), ("aq", 256, Q4), ("ap", 256, U8), ("pi", 8, I32),
-        ("pj", 8, I32), ("pf", 8, F32), ("j16", 16, F32), ("jm", 4, F32), ("spare", 8, F32), ("d16", 16, F32),
-        ("col", 8, F32), ("gm", 8, F32), ("c4b", 12, F32), ("mi", 192, BF), ("mk", 192, BF), ("idj", 128, BF),
-        ("c4", 512, BF), ("cdi", 4 * SEG, BF), ("cd", K16 * SEG, BF), ("tab", M + 4 * CH, F32),
+        ("pj", 8, I32), ("pf", 8, F32), ("j16", 16, F32), ("spare", 8, F32), ("d16", 16, F32), ("d4", 4, F32),
+        ("col", 8, F32), ("g8", 8, F32), ("ia", 128, BF), ("ib", 128, BF), ("iz", 128, BF), ("idj", 128, BF),
+        ("i4", 384, BF), ("c4", 384, BF), ("cdi", 2 * CH, BF), ("cd", NE, BF), ("tab", M + 4 * CH, F32),
         ("val", NV * C, F32), ("sca", 72, F32), ("prow", C, F32), ("scp", M, F32), ("boff", 72, U16),
-        ("moff", 128, U16), ("ne0", K16 * SEG, BF), ("ne1", K16 * SEG, BF), ("scd", K16 * SEG, BF)):
+        ("moff", 128, U16), ("pos", 2, U16), ("pe", 4, F32), ("ne0", NE, BF), ("ne1", NE, BF), ("scd", NE, BF)):
     SCRATCH[_n] = ("sbuf", [128, _w], _d)
 for _t in range(NV):
-    for _n, _w, _d in (("sq", C, Q4), ("sp", C, U8), ("yq", C, Q4), ("yp", C, U8), ("af", K16, F32), ("am", K16, F32),
-                       ("ar", 320, BF), ("so", K16, U16), ("ao", K16, U16), ("la", K16, U16), ("ls", K16, U16)):
+    for _n, _w, _d in (("sq", C, Q4), ("sp", C, U8), ("yq", C, Q4), ("yp", C, U8), ("af", K16, F32),
+                       ("ar", C, BF), ("so", 32, U16), ("ao", K16, U16), ("la", K16, U16), ("ls", K16, U16)):
         SCRATCH[_n + str(_t)] = ("sbuf", [128, _w], _d)
-SEMAPHORES = ["cv", "cs", "ct", "cg", "sent", "dx", "du", "dm", "dw", "st1", "st2", "st3",
-              "sa1", "sa2", "sb1", "sb2", "la1", "la2", "ls1", "ls2", "out"]
+SEMAPHORES = ["cv", "cs", "ct", "cg", "sent", "dx", "du", "dm", "dw", "dp", "out"] + [
+    _a + _b for _a in ("sa", "sb", "pa", "la", "ls") for _b in "123"]
 COUNTER = {"v": "cv", "s": "cs", "t": "ct", "g": "cg"}
 
-ORDER = list(range(11)) + [
-    16, 29, 32, 33, 17, 31, 34, 35, 11, 19, 36, 58, 38, 12, 28, 18, 21, 41, 13, 47, 39, 40, 45, 14, 46, 84, 42, 83, 15,
-    43, 37, 44, 53, 49, 50, 78, 54, 52, 30, 20, 55, 57, 67, 68, 76, 75, 91, 51, 26, 73, 72, 56, 69, 80, 92, 79, 74, 70,
-    71, 85, 24, 93, 27, 94, 65, 63, 95, 59, 66, 60, 62, 61, 64, 90, 87, 48, 86, 88, 96, 97, 98, 89, 100, 99, 105, 106,
-    81, 101, 22, 82, 102, 103, 107, 104, 114, 108, 119, 113, 111, 110, 116, 23, 109, 115, 77, 112, 121, 133, 124, 118,
-    127, 123, 148, 143, 126, 25, 160, 136, 122, 134, 147, 120, 128, 117, 135, 125, 145, 149, 132, 131, 153, 146, 154,
-    152, 129, 150, 130, 155, 167, 168, 170, 156, 159, 151, 137, 169, 140, 172, 175, 165, 193, 166, 138, 158, 176, 162,
-    141, 164, 177, 185, 142, 173, 178, 157, 184, 161, 181, 163, 144, 223, 182, 196, 197, 179, 183, 180, 194, 190, 186,
-    139, 195, 199, 198, 222, 213, 174, 219, 187, 188, 220, 189, 207, 211, 171, 200, 201, 218, 210, 215, 203, 205, 206,
-    225, 216, 234, 212, 226, 227, 192, 202, 228, 208, 230, 217, 209, 214, 204, 191, 229, 241, 233, 242, 221, 243, 244,
-    235, 245, 236, 239, 237, 246, 231, 248, 240, 247, 249, 250, 238, 252, 261, 253, 254, 262, 263, 251, 260, 256, 255,
-    265, 258, 232, 266, 257, 267, 269, 264, 268, 270, 273, 259, 274, 224, 290, 271, 275, 276, 278, 291, 279, 289, 277,
-    280, 281, 282, 295, 294, 283, 284, 293, 292, 286, 298, 287, 299, 288, 296, 297, 300, 313, 308, 301, 303, 307, 304,
-    272, 311, 312, 285, 328, 322, 306, 321, 317, 319, 314, 302, 320, 309, 310, 305, 327, 315, 329, 318, 323, 334, 331,
-    336, 324, 335, 316, 337, 338, 333, 325, 339, 341, 326, 342, 332, 330, 344, 340, 346, 345, 343, 347, 348, 349, 350,
-    352, 356, 351, 353, 357, 354, 355, 360, 364, 361, 358, 359, 362, 366, 363, 365, 367, 368, 372, 369, 374, 383, 384,
-    385, 378, 386, 375, 380, 388, 389, 382, 371, 373, 379, 381, 377, 376, 391, 387, 390, 370, 393, 395, 397, 394, 396,
-    392, 398, 399, 400, 401, 402, 403, 404, 405]
+ORDER = [0,5,1,2,3,4,17,6,12,82,21,20,22,23,18,7,24,25,8,84,80,19,85,29,33,62,26,9,36,30,11,27,35,39,40,42,63,41,72,31,28,37,38,10,52,51,88,46,57,73,47,34,54,43,53,89,49,90,44,45,55,50,91,68,48,66,92,58,60,59,98,96,94,32,13,15,16,14,56,97,93,64,69,70,109,108,61,106,95,99,110,105,104,124,125,65,101,103,71,100,67,127,126,102,129,130,107,186,83,81,187,77,74,131,128,174,134,168,182,111,115,112,133,132,116,114,173,135,118,177,181,119,113,117,120,136,122,78,121,142,138,169,167,183,184,123,139,79,179,75,140,178,143,166,159,175,171,153,141,185,176,76,170,172,180,144,87,86,160,145,188,154,151,157,152,146,149,189,150,147,155,164,190,163,158,162,161,226,225,227,224,148,137,165,191,216,214,192,213,156,197,204,202,198,201,193,205,194,231,206,215,228,208,195,196,229,220,223,199,232,221,222,230,210,207,203,233,212,235,234,238,237,236,200,211,239,240,209,241,251,244,217,250,245,249,255,252,243,254,242,218,253,256,219,247,246,257,248,263,259,260,261,280,264,262,281,265,278,287,266,270,279,271,272,267,273,288,274,283,282,268,286,289,323,322,276,285,284,269,258,312,311,310,313,302,308,299,290,293,307,297,301,303,294,298,292,296,304,309,300,295,305,306,291,275,314,325,317,328,315,277,326,316,327,318,320,324,329,332,319,331,321,330,333,335,334,338,340,339,355,337,342,344,336,343,356,341,349,348,347,345,353,346,357,352,362,364,366,351,350,368,358,367,354,359,363,365,361,360,374,369,376,370,380,375,372,377,378,371,381,373,379,383,382,387,386,391,389,384,385,392,390,388,395,393,394,399,398,397,396]
+ON_V = {19,36,77,78,102,103,105,109,132,134,165,166,169,174,177,178,181,202,205,208,214,215,228,235,238,247,253,293,299,302,305,306,311,313,331,334,351,369,383,384,385}
 
 
-def _emit(g, T, ops):
+def _emit(g, T, arrivals, ops):
     queue = {"v": g.vector, "s": g.scalar, "t": g.tensor, "g": g, "y": g.sync}
     known = {q: {} for q in queue}
     total, waited = {}, {}
     writer, readers = {}, {}
+    for sem, count, writes in arrivals:
+        total[sem] = count
+        for r in writes:
+            writer[r] = ("g", sem, count, {sem: count})
     assert sorted(ORDER) == list(range(len(ops)))
-    for q, fn, reads, writes, sem, inc in [ops[i] for i in ORDER]:
+    for i in ORDER:
+        fns, reads, writes, sem, inc = ops[i]
+        q = ("v" if i in ON_V else "s") if len(fns) > 1 else list(fns)[0]
         need = [writer[r] for r in list(reads) + list(writes) if r in writer]
         for r in writes:
             need += readers.get(r, [])
         for r in reads:
             if r[0] == "@":
                 need += [e for e in readers.get(r, []) if e[0] != q]
-        if fn is not None:
-            for eq, esem, count, clock in sorted(need, key=lambda e: -e[2]):
-                if (eq == q == "t") or known[q].get(esem, 0) >= count:
-                    continue
-                queue[q].wait_ge(T.sem[esem], count)
-                waited[esem] = max(waited.get(esem, 0), count)
-                for s, v in clock.items():
-                    known[q][s] = max(known[q].get(s, 0), v)
+        for eq, esem, count, clock in sorted(need, key=lambda e: -e[2]):
+            if (eq == q == "t") or known[q].get(esem, 0) >= count:
+                continue
+            queue[q].wait_ge(T.sem[esem], count)
+            waited[esem] = max(waited.get(esem, 0), count)
+            for s, v in clock.items():
+                known[q][s] = max(known[q].get(s, 0), v)
         if sem is None:
             sem, inc = COUNTER[q], 1
         total[sem] = total.get(sem, 0) + inc
-        clock = dict(known[q]) if fn is not None else {}
+        clock = dict(known[q])
         clock[sem] = total[sem]
-        if fn is not None:
-            ins = fn()
-            if sem != "sent":
-                ins.then_inc(T.sem[sem], inc)
+        ins = fns[q]()
+        if sem != "sent":
+            ins.then_inc(T.sem[sem], inc)
         ev = (q, sem, total[sem], clock)
         for r in reads:
             readers.setdefault(r, []).append(ev)
@@ -100,19 +91,13 @@ def rank_program(g, core, T, topo):
     nxt, home = T.cores[(rank + 1) % n], T.cores[(rank - (NV - 1)) % n]
     V, S, P = g.vector, g.scalar, g.tensor
     A, F = AluOpType, ActivationFunctionType
-    ops = []
+    ops, arrivals = [], []
 
-    def op(q, fn, reads, writes, sem=None, inc=None):
-        ops.append((q, fn, reads, writes, sem, inc))
-
-    def by(view):
-        return view.bitcast(dt.uint8)
-
-    def bank(name):
-        return T["p" + name[1]], 512 * int(name[2])
-
-    def runs(h):
-        return "a" if h == HA else "b" if h == HB else "ab"
+    def op(q, fn, reads, writes, sem=None, inc=None): ops.append(({q: fn}, reads, writes, sem, inc))
+    def either(fv, fs, reads, writes): ops.append(({"v": fv, "s": fs}, reads, writes, None, None))
+    def by(view): return view.bitcast(dt.uint8)
+    def bank(name): return T["p" + name[1]], 512 * int(name[2])
+    def runs(h): return "a" if h == HA else "b" if h == HB else "ab"
 
     def ts(out, in0, s1, s2, op0, op1, reads, writes):
         if op1 is None:
@@ -120,15 +105,25 @@ def rank_program(g, core, T, topo):
         else:
             op("v", lambda: V.tensor_scalar(out, in0, s1, s2, op0, op1), reads, writes)
 
-    def quant(q, p, src, reads, writes):
-        op("v", lambda: V.quantize_mx(q, p, src), reads, writes)
+    def line(out, in_, scale, bias, reads, writes):
+        either(lambda: V.tensor_scalar(out, in_, scale, bias, A.mult, A.add),
+               lambda: S.activation(out, in_, F.Identity, scale=scale, bias=bias), reads, writes)
+
+    def times(out, in_, scale, reads, writes):
+        either(lambda: V.tensor_scalar(out, in_, scale, None, A.mult),
+               lambda: S.activation(out, in_, F.Copy, scale=scale), reads, writes)
+
+    def copy(out, in_, reads, writes):
+        either(lambda: V.tensor_copy(out, in_), lambda: S.activation(out, in_, F.Copy), reads, writes)
+
+    def act(out, in_, func, scale, bias, reads, writes):
+        op("s", lambda: S.activation(out, in_, func, scale=scale, bias=bias), reads, writes)
+
+    def quant(q, p, src, reads, writes): op("v", lambda: V.quantize_mx(q, p, src), reads, writes)
 
     def mm(bk, cols, lq, lp, rq, rp, start, stop, reads):
         buf, o = bank(bk)
         op("t", lambda: P.matmul_mx(buf[:, o:o + cols], lq, lp, rq, rp, start, stop), reads, [bk])
-
-    def act(out, in_, func, reads, writes, **kw):
-        op("s", lambda: S.activation(out, in_, func, **kw), reads, writes)
 
     def iota(out, pattern, base, mult, writes, small=True):
         if small:
@@ -136,131 +131,105 @@ def rank_program(g, core, T, topo):
         else:
             op("g", lambda: g.iota(out, pattern, base, mult), [], writes)
 
-    def send(dst, mask, out, in_, sem, reads):
+    def send(dst, out, in_, sem, reads, lands):
         rid, pid = topo.addr(dst)[:2]
-        op("g", lambda: g.remote_dma(out, in_, T.sem[sem], T.sem["sent"], pid, rid, mask),
-           reads, [], "sent", bin(mask).count("1"))
-
-    def arrive(sem, count, writes):
-        op("g", None, [], writes, sem, count)
-
-    def nop():
-        pass
-
-    far, near = topo.mask(core, nxt), topo.mask(core, home)
-    nfar, nnear = bin(far).count("1"), bin(near).count("1")
-    for t in (1, 2):
-        arrive("st%d" % t, nfar, ["p%d" % t])
-        arrive("sa%d" % t, nfar, ["s%da" % t])
-        arrive("sb%d" % t, nfar, ["s%db" % t])
-        arrive("la%d" % t, nfar, ["la%d" % t])
-        arrive("ls%d" % t, nfar, ["ls%d" % t])
-    arrive("st3", 2 * nnear, ["s3"])
+        mask = topo.mask(core, dst)
+        k = bin(mask).count("1")
+        op("g", lambda: g.remote_dma(out, in_, T.sem[sem], T.sem["sent"], pid, rid, mask), reads, [], "sent", k)
+        arrivals.append((sem, k, lands))
 
     op("y", lambda: g.sync.dma_start(T.xin[:], T.x[:]), [], ["xin"], "dx", 16)
     op("s", lambda: S.dma_start(T.uin[:], T.u[:]), [], ["uin"], "du", 16)
     op("y", lambda: g.sync.dma_start(T.pool[:, 0:4 * M], T.m[:]), [], ["pool"], "dm", 16)
     op("y", lambda: g.sync.dma_start(by(T.wq[:]), T.wc[:]), [], ["w0"], "dw", 16)
-    op("y", lambda: g.sync.dma_start(T.wp[:], T.ws[:]), [], ["w"], "dw", 16)
+    op("y", lambda: g.sync.dma_start(T.wp[:], T.ws[:]), [], ["w"], "dp", 16)
 
     cc, grp, w4, t4 = (T.pf[:, i:i + 1] for i in range(4))
+    weight, inv, inv1024, low, minus = (T.col[:, i:i + 1] for i in range(1, 6))
     iota(T.pi[:, 0:1], [[0, 1]], 0, 1, ["pi"], small=False)
     iota(T.j16[:], [[1, 16]], 0, 0, ["j16"])
-    iota(T.mi[:, 0:64], [[1, 4], [0, 4], [-1, 4]], 0, 0, ["mi0"])
+    iota(T.ib[:], [[1, 8], [8, 4], [0, 4]], 0, 0, ["ib"])
     iota(T.idj[:], [[1, 128]], 0, -1, ["idj"])
-    iota(T.mi[:, 64:128], [[0, 4], [1, 4], [-1, 4]], 0, 0, ["mi1"])
-    iota(T.mi[:, 128:192], [[0, 16], [1, 4]], -3, 0, ["mi2"])
-    iota(T.cdi[:], [[-16, 4], [1, SEG]], 0, 0, ["cdi"])
-    iota(T.ar0[:, C:320], [[0, 32]], 300, 0, ["art0"])
-    iota(T.tab[:], [[4, M + 4 * CH]], 0, 0, ["tab"])
-    iota(T.val[:, 0:C], [[4, C]], 4 * M, 0, ["val0"])
-    for t in range(1, NV):
-        iota(T["ar%d" % t][:, C:320], [[0, 32]], 300, 0, ["art%d" % t])
+    iota(T.ia[:], [[1, 8], [0, 4], [8, 4]], 0, 0, ["ia"])
+    iota(T.iz[:], [[1, 8], [0, 16]], 0, 0, ["iz"])
+    iota(T.i4[:], [[0, 96], [1, 4]], 0, 0, ["i4"])
+    iota(T.cdi[:], [[1, 2 * CH]], -CH, 0, ["cdi"])
+    iota(T.tab[:], [[4, M + 4 * CH]], 4 * int(UP), 0, ["tab"])
+    for v in range(NV):
+        iota(T.val[:, C * v:C * v + C], [[4, C]], 4 * (M + C * v + int(UP)), 0, ["val%d" % v])
 
-    act(T.jm[:], T.j16[:, 0:4], F.Identity, ["j16"], ["jm"], bias=-1.0)
-    op("v", lambda: V.memset(T.ze[:], 0.0), [], ["ze"])
-    op("v", lambda: V.memset(T.ft[:, C:576], 0.0), [], ["ftz"])
+    op("v", lambda: V.memset(T.ze[:], 0.0), [], ["ze", "zero"])
+    times(T.zz[:], T.ze[:], 0.0, ["zero"], ["zz"])
+    times(T.ft[:, C:672], T.ze[:, 0:672 - C], 0.0, ["zero"], ["ftz"])
     ts(T.pj[:, 0:1], T.pi[:, 0:1], 15, None, A.bitwise_and, None, ["pi"], ["pj0"])
     ts(T.pj[:, 1:2], T.pi[:, 0:1], 4, None, A.arith_shift_right, None, ["pi"], ["pj1"])
     ts(T.pj[:, 2:3], T.pi[:, 0:1], 2, 3, A.arith_shift_right, A.bitwise_and, ["pi"], ["pj2"])
     ts(T.pj[:, 3:4], T.pi[:, 0:1], 3, None, A.bitwise_and, None, ["pi"], ["pj3"])
     quant(T.fq[:, 0:128], T.fp[:, 0:128], T.ze[:, 0:512], ["ze"], ["fz0"])
     op("v", lambda: V.tensor_copy(T.pf[:, 0:4], T.pj[:, 0:4]), ["pj0", "pj1", "pj2", "pj3"], ["pf"])
-    ts(T.mk[:, 0:64], T.mi[:, 0:64], 0.0, None, A.is_equal, None, ["mi0"], ["mk0"])
     ts(T.d16[:], T.j16[:], cc, 1.0, A.is_lt, A.add, ["j16", "pf"], ["d16"])
-    ts(T.c4b[:, 0:4], T.j16[:, 0:4], w4, -BIG, A.is_equal, A.mult, ["j16", "pf"], ["c4b0"])
     op("v", lambda: V.tensor_reduce(T.col[:, 0:1], T.d16[:], AxisListType.X, A.mult), ["d16"], ["col0"])
-    ts(T.c4b[:, 8:12], T.jm[:], w4, KEEP, A.is_equal, A.mult, ["jm", "pf"], ["c4b2"])
-    ts(T.col[:, 1:2], cc, 8.5, T.col[:, 0:1], A.is_lt, A.mult, ["pf", "col0"], ["col1"])
-    ts(T.col[:, 2:3], w4, 2.5, -KEEP, A.is_lt, A.mult, ["pf"], ["col2"])
-    ts(T.gm[:], T.j16[:, 0:8], grp, T.col[:, 1:2], A.is_equal, A.mult, ["j16", "pf", "col1"], ["gm"])
-    ts(T.ze[:, 3:512:4], T.idj[:], 0.0, 64.0, A.is_equal, A.mult, ["idj"], ["ze"])
-    op("v", lambda: V.tensor_tensor(T.c4b[:, 4:8], T.c4b[:, 8:12], T.c4b[:, 0:4], A.add), ["c4b0", "c4b2"], ["c4b1"])
-    act(T.spare[:, 4:5], cc, F.Identity, ["pf"], ["sp4"], scale=-4.0, bias=-float(M))
-    act(T.spare[:, 0:4], T.j16[:, 0:4], F.Identity, ["j16", "sp4"], ["spare"], scale=-64.0, bias=T.spare[:, 4:5])
-
-    def weights(tile, mask, name):
-        for m in range(8):
-            act(tile[:, 64 * m:64 * m + 64], T.mk[:, 64 * mask:64 * mask + 64], F.Copy, ["mk%d" % mask, "gm"],
-                [name + str(m)], scale=T.gm[:, m:m + 1])
-
-    def names(name):
-        return [name + str(m) for m in range(8)]
-
-    weights(T.wb, 0, "wb")
-    ts(T.mk[:, 64:192], T.mi[:, 64:192], 0.0, None, A.is_equal, None, ["mi1", "mi2"], ["mk1", "mk2"])
-    op("v", lambda: V.memset(T.zz[:, 512:528], 0.0), [], ["zzt"])
-    weights(T.wa, 1, "wa")
-    weights(T.zz, 2, "zz")
+    ts(weight, cc, 8.5, T.col[:, 0:1], A.is_lt, A.mult, ["pf", "col0"], ["weight"])
+    line(T.g8[:, 0:4], T.j16[:, 0:4], 8.0, grp, ["j16", "pf"], ["g8"])
+    ts(T.d4[:, 0:3], T.j16[:, 0:3], w4, 1.0 / X, A.is_lt, A.max, ["j16", "pf"], ["d4"])
+    op("v", lambda: V.tensor_reduce(inv, T.d4[:, 0:3], AxisListType.X, A.mult), ["d4"], ["inv"])
+    times(inv1024, inv, 1024.0, ["inv"], ["inv1024"])
+    line(low, t4, 1.0, -4.0 * UP, ["pf"], ["low"])
+    ts(T.c4[:], T.i4[:], w4, X, A.not_equal, A.mult, ["i4", "pf"], ["c4"])
+    ts(T.ze[:, 3:512:4], T.idj[:], 0.0, 64.0, A.is_equal, A.mult, ["idj"], ["ze", "zero"])
+    line(T.spare[:, 4:5], cc, -4.0, -float(M), ["pf"], ["sp4"])
+    line(T.spare[:, 0:4], T.j16[:, 0:4], -64.0, T.spare[:, 4:5], ["j16", "sp4"], ["spare"])
+    times(minus, weight, -1.0, ["weight"], ["minus"])
+    for tile, src, name in ((T.wb, T.ib, "b"), (T.wa, T.ia, "a")):
+        parts = ["w%s%d" % (name, t) for t in range(4)]
+        for t in range(4):
+            act(tile[:, t:512:4], src[:], F.Abs, -1.0, T.g8[:, t:t + 1], ["i" + name, "g8"], [parts[t]])
+        act(tile[:], tile[:], F.Relu, minus, weight, parts + ["minus", "weight"], parts)
+    act(T.iz[:], T.iz[:], F.Abs, -1.0, grp, ["iz", "pf"], ["iz"])
+    act(T.zz[:, 3:512:4], T.iz[:], F.Relu, minus, weight, ["iz", "minus", "weight"], ["zz"])
     for b in range(4):
         quant(T.eq[:, 128 * b:128 * b + 128], T.ep[:, 128 * b:128 * b + 128], T.ze[:, 3 - b:515 - b], ["ze"], ["e%d" % b])
-    quant(T.aq[:, 128:256], T.ap[:, 128:256], T.wb[:], names("wb"), ["qwb"])
+    quant(T.aq[:, 128:256], T.ap[:, 128:256], T.wb[:], ["wb%d" % t for t in range(4)], ["qwb"])
+    quant(T.aq[:, 0:128], T.ap[:, 0:128], T.wa[:], ["wa%d" % t for t in range(4)], ["qwa"])
     quant(T.uq[:], T.up[:], T.uin[:], ["uin"], ["uq"])
-    for i in range(4):
-        act(T.c4[:, i:512:4], T.idj[:], F.Identity, ["idj", "c4b1"], ["c4%d" % i], scale=0.0, bias=T.c4b[:, 4 + i:5 + i])
-    act(T.col[:, 3:4], T.col[:, 2:3], F.Identity, ["col2", "pf"], ["col3"], bias=t4)
-    act(T.col[:, 4:5], T.col[:, 2:3], F.Identity, ["col2"], ["col4"], bias=-256.0)
-    act(T.col[:, 5:6], T.col[:, 2:3], F.Identity, ["col2"], ["col5"], scale=1024.0, bias=-256.0 * 1024.0)
-    for t in range(2):
-        act(T["ne%d" % t][:, SEG - 1:K16 * SEG:SEG], T.idj[:, 0:K16], F.Identity, ["idj"], ["nez%d" % t],
-            scale=0.0, bias=1024.0)
-
-    C4 = ["c40", "c41", "c42", "c43"]
-    CD = ["cd0", "cd0b", "cd1", "cd2", "cd3", "cd4"]
-
-    def cd_part(r):
-        ts(T.cd[:, SEG * r:SEG * r + SEG], T.cdi[:, SEG * r:SEG * r + SEG], cc, T.spare[:, r:r + 1],
-           A.is_equal, A.mult, ["cdi", "pf", "spare"], ["cdp%d" % r])
-
-    def cd_ends():
-        parts = ["cdp%d" % r for r in range(4)]
-        act(T.cd[:, 0:4 * SEG:SEG], T.idj[:, 0:4], F.Identity, ["idj"], parts + ["cd0"], scale=0.0, bias=4096.0)
-        act(T.cd[:, CH:4 * SEG:SEG], T.idj[:, 0:4], F.Identity, ["idj", "cd0"], ["cd0b"], scale=0.0, bias=256.0)
-
-    def cd_copy(i):
-        w = min(4 * SEG, (K16 - 4 * i) * SEG)
-        act(T.cd[:, 4 * SEG * i:4 * SEG * i + w], T.cd[:, 0:w], F.Copy, ["cd0", "cd0b"], ["cd%d" % i])
-
-    def val_of(v):
-        act(T.val[:, C * v:C * v + C], T.val[:, 0:C], F.Identity, ["val0"], ["val%d" % v], bias=4.0 * C * v)
-
-    def qz(b):
-        quant(T.zq[:, 128 * b:128 * b + 128], T.zp[:, 128 * b:128 * b + 128], T.zz[:, 3 - b:515 - b],
-              names("zz") + ["zzt"], ["z%d" % b])
+    for b in range(4):
+        quant(T.zq[:, 128 * b:128 * b + 128], T.zp[:, 128 * b:128 * b + 128], T.zz[:, 3 - b:515 - b], ["zz"], ["z%d" % b])
+    act(T.cdi[:], T.cdi[:], F.Abs, -1.0, cc, ["cdi", "pf"], ["cdi"])
+    act(T.cdi[:], T.cdi[:], F.Relu, -1.0, 1.0, ["cdi"], ["cdi"])
+    for r in range(R):
+        a = CH - 16 * r
+        act(T.cd[:, O[r]:O[r + 1]], T.cdi[:, a:a + O[r + 1] - O[r]], F.Identity, T.spare[:, r:r + 1], 0.0,
+            ["cdi", "spare"], ["cdp%d" % r])
+        act(T.cd[:, O[r]:O[r + 1]:16 * (r + 1)], T.j16[:, 0:2], F.Identity, 256.0 - 4096.0, 4096.0, ["j16"], ["cdp%d" % r])
+    act(T.pe[:, 0:1], t4, F.Identity, 8.0, 26.0, ["pf"], ["pe0"])
+    act(T.pe[:, 1:2], T.pe[:, 0:1], F.Identity, t4, 16.0, ["pf", "pe0"], ["pe1"])
+    act(T.pe[:, 2:3], w4, F.Identity, float(PER), T.pe[:, 1:2], ["pf", "pe1"], ["pe2"])
+    act(T.pe[:, 0:2], T.j16[:, 0:2], F.Identity, 4.0 * PER, T.pe[:, 2:3], ["j16", "pe2"], ["pe0", "pe1"])
+    ts(T.pos[:], T.pe[:, 0:2], NE - 1.0, None, A.min, None, ["pe0", "pe1"], ["pos"])
+    CD, have = ["cdp%d" % r for r in range(R)], PER
+    while have < NE:
+        w = min(have, NE - have)
+        copy(T.cd[:, have:have + w], T.cd[:, 0:w], list(CD), ["cd%d" % (len(CD) + 1)])
+        CD.append("cd%d" % (len(CD) + 1))
+        have += w
+    for x in range(2):
+        for r in range(R):
+            z = len(range(O[r + 1] - 1, NE, PER))
+            act(T["ne%d" % x][:, O[r + 1] - 1:NE:PER], T.j16[:, 0:z], F.Identity, 0.0, 1024.0, ["j16"], ["nez%d%d" % (x, r)])
 
     def a_mm(q, p, res, bk, h):
         mm(bk, h[1] - h[0], T.uq[:], T.up[:], q[:, h[0]:h[1]], p[:, h[0]:h[1]], True, True, ["uq", res])
 
     def bits(bk, h):
         buf, o = bank(bk)
-        ts(T.ft[:, h[0]:h[1]], buf[:, o:o + h[1] - h[0]], 0.0, None, A.is_gt, None, [bk], ["ft" + c for c in runs(h)])
+        ts(T.ft[:, h[0]:h[1]], buf[:, o:o + h[1] - h[0]], 0.0, 1.0, A.is_gt, A.add, [bk], ["ft" + c for c in runs(h)])
 
-    def q_bits():
-        quant(T.fq[:, 128:272], T.fp[:, 128:272], T.ft[:], ["fta", "ftb", "ftz"], ["fq"])
+    def q_bits(w):
+        quant(T.fq[:, 128:128 + w], T.fp[:, 128:128 + w], T.ft[:, 0:4 * w], ["fta", "ftb", "ftz"], ["fq"])
 
     def list_mm(bk, which):
-        o = 128 * which
-        mm(bk, 128, T.aq[:, o:o + 128], T.ap[:, o:o + 128], T.fq[:, 128:256], T.fp[:, 128:256], True, True,
+        w = 128 * which
+        mm(bk, 128, T.aq[:, w:w + 128], T.ap[:, w:w + 128], T.fq[:, 128:256], T.fp[:, 128:256], True, True,
            ["fq", "qwb" if which else "qwa"])
 
     def row_mm(bk, half):
@@ -273,48 +242,42 @@ def rank_program(g, core, T, topo):
         buf, o = bank(bk)
         for i in range(2):
             t = 2 * half + i
-            act(T["ar%d" % v][:, t:C:4], buf[:, o + 72 * i:o + 72 * i + 72], F.Identity, [bk], ["ar%d%d" % (v, t)],
-                bias=-256.0)
+            line(T["ar%d" % v][:, t:C:4], buf[:, o + 72 * i:o + 72 * i + 72], 1024.0, -1024.0 * (UP + 256.0), [bk],
+                 ["ar%d%d" % (v, t)])
 
     def list_scan(bk):
         buf, o = bank(bk)
-        op("v", lambda: V.tensor_tensor_scan(T.sca[:], T.c4[:, 0:72], buf[:, o:o + 72], 0.0, A.add, A.max),
-           [bk] + C4, ["sca"])
+        op("v", lambda: V.tensor_tensor_scan(T.sca[:], T.c4[:, 0:72], buf[:, o:o + 72], 0.0, A.mult, A.max),
+           [bk, "c4"], ["sca"])
 
-    def list_u16(v):
-        ts(T["ao%d" % v][:], T.sca[:, 3:72:4], T.col[:, 2:3], None, A.add, None, ["sca", "col2"], ["ao%d" % v])
+    def list_out(v):
+        ts(T["ao%d" % v][:], T.sca[:, 3:72:4], inv, -UP, A.mult, A.add, ["sca", "inv"], ["ao%d" % v])
+        send(nxt, T["la%d" % v][:], T["ao%d" % v][:], "la%d" % v, ["ao%d" % v], ["la%d" % v])
 
     def list_f32(v):
-        act(T["am%d" % v][:], T.sca[:, 3:72:4], F.Identity, ["sca", "col4"], ["am%d" % v], bias=T.col[:, 4:5])
-        act(T["af%d" % v][:], T.sca[:, 3:72:4], F.Identity, ["sca", "col5"], ["af%d" % v], scale=1024.0, bias=T.col[:, 5:6])
+        line(T["af%d" % v][:], T.sca[:, 3:72:4], inv1024, -1024.0 * (UP + 256.0), ["sca", "inv1024"], ["af%d" % v])
 
-    def compare(q, v, ks):
-        for k in ks:
-            c0, x = CH * (k // 4), v % 2
-            o, i, s = T["ne%d" % x][:, SEG * k:SEG * k + CH], T["ar%d" % v][:, c0:c0 + CH], T["am%d" % v][:, k:k + 1]
-            rd = ["ar%d%d" % (v, t) for t in range(4)] + ["art%d" % v, "am%d" % v]
-            if q == "v":
-                ts(o, i, s, 1024.0, A.not_equal, A.mult, rd, ["ne%d_%d" % (x, k)])
-            else:
-                act(o, i, F.Abs, rd + ["af%d" % v], ["ne%d_%d" % (x, k)], scale=-1024.0, bias=T["af%d" % v][:, k:k + 1])
-
-    def own(v):
-        act(T["ne%d" % (v % 2)][:, CH:K16 * SEG:SEG], T["am%d" % v][:], F.Copy, ["am%d" % v], ["neo%d" % (v % 2)],
-            scale=-1.0)
-
-    def dedupe(v, gap):
+    def dedupe(v):
         x = v % 2
+        for k in range(K16):
+            c0, w, z = CH * (k // R), 16 * (k % R + 1), PER * (k // R) + O[k % R]
+            o, i, s = T["ne%d" % x][:, z:z + w], T["ar%d" % v][:, c0:c0 + w], T["af%d" % v][:, k:k + 1]
+            either(lambda o=o, i=i, s=s: V.tensor_scalar(o, i, s, 1024.0, A.not_equal, A.mult),
+                   lambda o=o, i=i, s=s: S.activation(o, i, F.Abs, scale=-1.0, bias=s),
+                   ["ar%d%d" % (v, t) for t in range(4)] + ["af%d" % v], ["ne%d_%d" % (x, k)])
+        for r in range(R):
+            times(T["ne%d" % x][:, O[r + 1] - 2:NE:PER], T["af%d" % v][:, r:K16:R], -1.0 / 1024.0, ["af%d" % v],
+                  ["neo%d%d" % (x, r)])
         op("v", lambda: V.tensor_tensor_scan(T.scd[:], T.cd[:], T["ne%d" % x][:], 0.0, A.add, A.min),
-           CD + ["neo%d" % x, "nez%d" % x] + ["ne%d_%d" % (x, k) for k in range(K16)], ["scd"])
-        gap()
-        ts(T["so%d" % v][:], T.scd[:, CH:K16 * SEG:SEG], -1.0, 256.0, A.mult, A.add, ["scd"], ["so%d" % v])
+           CD + ["ne%s%d%d" % (c, x, r) for r in range(R) for c in "oz"] + ["ne%d_%d" % (x, k) for k in range(K16)], ["scd"])
+        ts(T["so%d" % v][:], T.scd[:].indirect(T.pos[:]), -1.0, 256.0, A.mult, A.add, ["scd", "pos"], ["so%d" % v])
         if v:
-            send(nxt, far, T["ls%d" % v][:], T["so%d" % v][:], "ls%d" % v, ["so%d" % v])
+            send(nxt, T["ls%d" % v][:], T["so%d" % v][:, 0:K16], "ls%d" % v, ["so%d" % v], ["ls%d" % v])
 
-    def scatter(v, chunks):
+    def scatter(v):
         name = "ls%d" % v if v else "so0"
-        for c in chunks:
-            a, b = 4 * c, min(4 * c + 4, K16)
+        for a in reversed(range(0, K16, R)):
+            b = min(a + R, K16)
             op("v", lambda a=a, b=b: V.tensor_copy(T.tab[:].indirect(T[name][:, a:b]),
                                                    T.val[:, C * v + 16 * a:C * v + 16 * b]),
                [name, "val%d" % v], ["tab"])
@@ -322,238 +285,137 @@ def rank_program(g, core, T, topo):
     def pool_names(v):
         return ["pool"] + ["n%d%d%s" % (t, b, c) for t in range(v) for b in range(4) for c in "ab"]
 
-    def gather(q, out, win, off, reads, writes):
-        if q == "v":
-            op("v", lambda: V.tensor_copy(out, win.indirect(off)), reads, writes)
-        else:
-            act(out, win.indirect(off), F.Copy, reads, writes)
+    def gather(out, win, off, reads, writes): copy(out, win.indirect(off), reads, writes)
 
-    def select_scan(src, res, a, b):
-        op("v", lambda: V.tensor_tensor_scan(T.scp[:, a:b], T.c4[:, a:b], src[:, a:b], 0.0, A.add, A.max),
-           [res] + C4, ["scp%d" % min(a, 1)])
+    def pick(src, res, off, out, a, b):
+        op("v", lambda: V.tensor_tensor_scan(T.scp[:, a:b], T.c4[:, 0:b - a], src[:, a:b], 0.0, A.mult, A.max),
+           [res, "c4"], ["scp%d" % min(a, 1)])
+        ts(off[:, a // 4:b // 4], T.scp[:, a + 3:b:4], inv, low, A.mult, A.add,
+           ["scp%d" % min(a, 1), "inv", "low"], [out])
 
-    def select_u16(off, out, a, b):
-        ts(off[:, a // 4:b // 4], T.scp[:, a + 3:b:4], T.col[:, 3:4], None, A.add, None,
-           ["scp%d" % min(a, 1), "col3"], [out])
+    def pointers(v, h):
+        c = runs(h)
+        gather(T.prow[:, h[0]:h[1]], T.tab[:, 0:M], T["la%d" % v][:, h[0] // 16:h[1] // 16], ["tab", "la%d" % v],
+               ["prow" + c])
+        pick(T.prow, "prow" + c, T.boff, "boff" + c, h[0], h[1])
 
-    def pointers(v):
-        la = T["la%d" % v]
-        gather("s", T.prow[:, 0:CUT], T.tab[:], la[:, 0:CUT // 16], ["tab", "la%d" % v], ["prowa"])
-        gather("s", T.prow[:, CUT:C], T.tab[:], la[:, CUT // 16:K16], ["tab", "la%d" % v], ["prowb"])
-        select_scan(T.prow, "prowa", 0, CUT)
-        select_scan(T.prow, "prowb", CUT, C)
-        select_u16(T.boff, "boffa", 0, CUT)
-        select_u16(T.boff, "boffb", CUT, C)
+    def read_map(v, h):
+        win, c, mid = T.pool[:, 0:4 * (M + C * v)], runs(h), (h[0] + h[1]) // 2
+        for i, (a, b) in enumerate(((h[0], mid), (mid, h[1]))):
+            gather(T.bt[:, 4 * a:4 * b], win, T.boff[:, a // 4:b // 4], pool_names(v) + ["boff" + c], ["bt%s%d" % (c, i)])
+        quant(T.bq[:, h[0]:h[1]], T.bp[:, h[0]:h[1]], T.bt[:, 4 * h[0]:4 * h[1]], ["bt%s0" % c, "bt%s1" % c], ["bq" + c])
 
-    def read_map(v):
-        win = T.pool[:, 0:4 * (M + C * v)]
-        gather("s", T.bt[:, 0:4 * CUT], win, T.boff[:, 0:CUT // 4], pool_names(v) + ["boffa"], ["bta"])
-        gather("v", T.bt[:, 4 * CUT:4 * C], win, T.boff[:, CUT // 4:72], pool_names(v) + ["boffb"], ["btb"])
-
-    def q_b():
-        quant(T.bq[:, CUT:C], T.bp[:, CUT:C], T.bt[:, 4 * CUT:4 * C], ["btb"], ["bqb"])
-        quant(T.bq[:, 0:CUT], T.bp[:, 0:CUT], T.bt[:, 0:4 * CUT], ["bta"], ["bqa"])
-
-    def r_mm(v, x, h):
+    def r_mm(v, x, h, first=True):
         for b in range(4):
             mm("@%s%d" % (x, b), h[1] - h[0], T.wq[:, 128 * b:128 * b + 128], T.wp[:, 128 * b:128 * b + 128],
-               T["sq%d" % v][:, h[0]:h[1]], T["sp%d" % v][:, h[0]:h[1]], True, False,
-               ["w", "p%d" % v, "s%d%s" % (v, runs(h))] if v else ["w", "s0"])
+               T["sq%d" % v][:, h[0]:h[1]], T["sp%d" % v][:, h[0]:h[1]], first, not first,
+               ["w0", "w", "p%d" % v, "s%d%s" % (v, runs(h))] if v else ["w0", "w", "s0"])
 
-    def d_mm(x, h):
+    def new_state(v, x, h):
+        c = runs(h)
         for b in range(4):
             mm("@%s%d" % (x, b), h[1] - h[0], T.eq[:, 128 * b:128 * b + 128], T.ep[:, 128 * b:128 * b + 128],
-               T.bq[:, h[0]:h[1]], T.bp[:, h[0]:h[1]], False, True, ["e%d" % b] + ["bq" + c for c in runs(h)])
-
-    def unload(q, bk, tile, o, b, h, res):
-        buf, p = bank(bk)
-        out, in_ = tile[:, o + 4 * h[0] + b:o + 4 * h[1]:4], buf[:, p:p + h[1] - h[0]]
-        if q == "v":
-            ts(out, in_, 0.015625, None, A.mult, None, [bk], res)
-        else:
-            act(out, in_, F.Copy, [bk], res, scale=0.015625)
-
-    def y_read(q, x, b, h):
-        unload(q, "@%s%d" % (x, b), T.yt, 0, b, h, ["yt%s%d" % (c, b) for c in runs(h)])
-
-    def q_y(v, h):
+               T.bq[:, h[0]:h[1]], T.bp[:, h[0]:h[1]], v == 0, v != 0, ["e%d" % b, "bq" + c])
+        if v == 0:
+            r_mm(0, x, h, False)
+        for b in range(4):
+            unload("@%s%d" % (x, b), T.yt, 0, b, h, ["yt%s%d" % (c, b)])
         quant(T["yq%d" % v][:, h[0]:h[1]], T["yp%d" % v][:, h[0]:h[1]], T.yt[:, 4 * h[0]:4 * h[1]],
-              ["yt%s%d" % (runs(h), b) for b in range(4)], ["y%d%s" % (v, runs(h))])
+              ["yt%s%d" % (c, b) for b in range(4)], ["y%d%s" % (v, c)])
 
-    def n_mm(v, b, bk, h):
+    def unload(bk, tile, o, b, h, res):
+        buf, p = bank(bk)
+        times(tile[:, o + 4 * h[0] + b:o + 4 * h[1]:4], buf[:, p:p + h[1] - h[0]], 0.015625, [bk], res)
+
+    def to_pool(v, b, bk, h):
         mm(bk, h[1] - h[0], T.eq[:, 128 * b:128 * b + 128], T.ep[:, 128 * b:128 * b + 128],
            T["yq%d" % v][:, h[0]:h[1]], T["yp%d" % v][:, h[0]:h[1]], True, True,
            ["e%d" % b] + ["y%d%s" % (v, c) for c in runs(h)])
+        unload(bk, T.pool, 4 * (M + C * v), b, h, ["n%d%d%s" % (v, b, c) for c in runs(h)])
 
-    def n_read(q, v, b, bk, h):
-        unload(q, bk, T.pool, 4 * (M + C * v), b, h, ["n%d%d%s" % (v, b, c) for c in runs(h)])
+    def pass_codes(v, dst, q, h):
+        send(dst, by(q[:, h[0]:h[1]]), by(T["yq%d" % v][:, h[0]:h[1]]), "s%s%d" % (runs(h)[0], v + 1),
+             ["y%d%s" % (v, c) for c in runs(h)], ["s%d%s" % (v + 1, c) for c in runs(h)])
 
-    def guests(v):
-        r_mm(v, "n", HB)
-        r_mm(v, "y", HA)
-        pointers(v)
-        read_map(v)
-        q_b()
-        d_mm("n", HB)
-        d_mm("y", HA)
+    def pass_scales(v, dst, p):
+        send(dst, p[:, 0:C], T["yp%d" % v][:], "pa%d" % (v + 1), ["y%da" % v, "y%db" % v], ["p%d" % (v + 1)])
 
-    NB = ("@n1", "@n2", "@n3", "@n0")
+    def visit(v):
+        w = v + 1
+        if v:
+            r_mm(v, "n", HB)
+            r_mm(v, "y", HA)
+            pointers(v, HB)
+            pointers(v, HA)
+        read_map(v, HB)
+        read_map(v, HA)
+        new_state(v, "n", HB)
+        new_state(v, "y", HA)
+        if w < NV:
+            pass_codes(v, nxt, T["sq%d" % w], HB)
+            pass_codes(v, nxt, T["sq%d" % w], HA)
+            pass_scales(v, nxt, T["sp%d" % w])
+            a_mm(T["yq%d" % v], T["yp%d" % v], "y%db" % v, "@n0", HB)
+            bits("@n0", HB)
+            a_mm(T["yq%d" % v], T["yp%d" % v], "y%da" % v, "@y0", HA)
+            bits("@y0", HA)
+            q_bits(128)
+            list_mm("@y1", 0)
+            list_scan("@y1")
+            list_out(w)
+            row_mm("@y2", 0)
+            row_mm("@y3", 1)
+            for b in range(4):
+                to_pool(v, b, "@n%d" % ((b + 2) % 4), ALL)
+            row_read(w, "@y2", 0)
+            row_read(w, "@y3", 1)
+            list_f32(w)
+        if v == 0:
+            dedupe(0)
+        scatter(v)
+        if w < NV:
+            dedupe(w)
 
-    def first_bits(v):
-        a_mm(T["yq%d" % v], T["yp%d" % v], "y%db" % v, "@n0", HB)
-
-    def next_addresses(v, gap0, gap1):
-        w, y = v + 1, ["y%da" % v, "y%db" % v]
-        send(nxt, far, by(T["sq%d" % w][:, CUT:C]), by(T["yq%d" % v][:, CUT:C]), "sb%d" % w, y[1:])
-        send(nxt, far, by(T["sq%d" % w][:, 0:CUT]), by(T["yq%d" % v][:, 0:CUT]), "sa%d" % w, y[:1])
-        a_mm(T["yq%d" % v], T["yp%d" % v], "y%da" % v, "@y0", HA)
-        n_mm(v, 0, NB[0], ALL)
-        n_mm(v, 1, NB[1], ALL)
-        bits("@n0", HB)
-        gap0()
-        bits("@y0", HA)
-        q_bits()
-        list_mm("@y1", 0)
-        row_mm("@y2", 0)
-        row_mm("@y3", 1)
-        gap1()
-        list_scan("@y1")
-        list_u16(w)
-        send(nxt, far, T["la%d" % w][:], T["ao%d" % w][:], "la%d" % w, ["ao%d" % w])
-        send(nxt, far, T["sp%d" % w][:], T["yp%d" % v][:], "st%d" % w, y)
-        n_read("s", v, 0, NB[0], ALL)
-        n_read("s", v, 1, NB[1], ALL)
-        n_mm(v, 2, NB[2], ALL)
-        n_mm(v, 3, NB[3], ALL)
-        row_read(w, "@y2", 0)
-        row_read(w, "@y3", 1)
-        list_f32(w)
-
-    def late_n(v):
-        n_read("s", v, 2, NB[2], ALL)
-        n_read("s", v, 3, NB[3], ALL)
-
-    quant(T.aq[:, 0:128], T.ap[:, 0:128], T.wa[:], names("wa"), ["qwa"])
     quant(T.sq0[:], T.sp0[:], T.xin[:], ["xin"], ["s0"])
     a_mm(T.sq0, T.sp0, "s0", "@n0", ALL)
-    qz(0)
-    qz(1)
     bits("@n0", ALL)
-    q_bits()
+    q_bits(144)
     list_mm("@n1", 1)
     list_mm("@n2", 0)
-    qz(2)
-    qz(3)
-    ts(T.boff[:], T.pn[:, 512:584], 4.0, t4, A.mult, A.add, ["@n1", "pf"], ["boffa", "boffb"])
+    ts(T.boff[:], T.pn[:, 512:584], 4.0, low, A.mult, A.add, ["@n1", "low"], ["boffa", "boffb"])
     list_scan("@n2")
-    read_map(0)
     row_mm("@n3", 0)
     row_mm("@n0", 1)
-    r_mm(0, "y", HA)
     row_read(0, "@n3", 0)
     row_read(0, "@n0", 1)
-    r_mm(0, "n", HB)
-    q_b()
     list_f32(0)
-    d_mm("n", HB)
-    d_mm("y", HA)
-    for r in range(4):
-        cd_part(r)
-    compare("v", 0, range(0, 5))
-    compare("s", 0, range(5, 9))
+    for v in range(NV):
+        visit(v)
+    pass_codes(2, home, T.oq, ALL)
+    pass_scales(2, home, T.op)
     for b in range(4):
-        y_read("sv"[b % 2], "n", b, HB)
+        to_pool(2, b, "@n%d" % b, HB)
     for b in range(4):
-        y_read("sv"[b % 2], "y", b, HA)
-    cd_ends()
-    own(0)
-    compare("s", 0, range(9, 15))
-    for i in (1, 2, 3, 4):
-        cd_copy(i)
-    q_y(0, HB)
-    first_bits(0)
-    q_y(0, HA)
-    next_addresses(0, nop, lambda: compare("v", 0, range(15, K16)))
-    dedupe(0, nop)
-    own(1)
-    compare("s", 1, range(0, K16))
-    late_n(0)
-    val_of(1)
-    val_of(2)
-    scatter(0, (4, 3, 2, 1))
-    dedupe(1, lambda: scatter(0, (0,)))
+        to_pool(2, b, "@y%d" % b, HA)
 
-    guests(1)
-    scatter(1, (4,))
-    for b in range(4):
-        y_read("sv"[b % 2], "n", b, HB)
-    y_read("s", "y", 0, HA)
-    y_read("v", "y", 1, HA)
-    q_y(1, HB)
-    first_bits(1)
-    y_read("s", "y", 2, HA)
-    y_read("v", "y", 3, HA)
-    q_y(1, HA)
-    next_addresses(1, lambda: scatter(1, (3,)), lambda: scatter(1, (2,)))
-    own(2)
-    compare("s", 2, range(0, 14))
-    late_n(1)
-    scatter(1, (1,))
-    scatter(1, (0,))
-    compare("v", 2, range(14, K16))
-    dedupe(2, nop)
-
-    guests(2)
-    for b in range(4):
-        y_read("svss"[b], "n", b, HB)
-    scatter(2, (4, 3))
-    y_read("s", "y", 0, HA)
-    y_read("s", "y", 1, HA)
-    q_y(2, HB)
-    for b in range(4):
-        n_mm(2, b, "@n%d" % b, HB)
-    scatter(2, (2,))
-    y_read("s", "y", 2, HA)
-    y_read("s", "y", 3, HA)
-    q_y(2, HA)
-    send(home, near, by(T.oq[:, 0:C]), by(T.yq2[:]), "st3", ["y2a", "y2b"])
-    send(home, near, T.op[:, 0:C], T.yp2[:], "st3", ["y2a", "y2b"])
-    for b in range(4):
-        n_mm(2, b, "@y%d" % b, HA)
-    for b in range(4):
-        n_read("s", 2, b, "@n%d" % b, HB)
-    for b in range(4):
-        n_read("s", 2, b, "@y%d" % b, HA)
-    scatter(2, (1, 0))
-
-    win, c1, c2, c3 = T.pool[:], 128, 304, 384
-
-    def g_m(q, a, b, res, out):
-        gather(q, T.mt[:, 4 * a:4 * b], win, T.moff[:, a // 4:b // 4], pool_names(NV) + [res], [out])
-
-    def q_m(a, b, reads, out):
-        quant(T.oq[:, C + a:C + b], T.op[:, C + a:C + b], T.mt[:, 4 * a:4 * b], reads, [out])
+    S3 = ["s3a", "s3b", "p3"]
+    pick(T.tab, "tab", T.moff, "moffa", 0, 128)
+    pick(T.tab, "tab", T.moff, "moffb", 128, M)
+    for a, b in zip(FIN, FIN[1:]):
+        gather(T.mt[:, 4 * a:4 * b], T.pool[:], T.moff[:, a // 4:b // 4],
+               pool_names(NV) + ["moffa" if a < 128 else "moffb"], ["mt%d" % a])
+    mm("@n0", C, T.wq[:, 0:128], T.wp[:, 0:128], T.oq[:, 0:C], T.op[:, 0:C], True, True, ["w0", "w"] + S3)
+    copy(T.yo[:], T.pn[:, 0:C], ["@n0"], ["yo"])
 
     def store(q, out, in_, reads):
         op(q, lambda: (g.sync if q == "y" else S).dma_start(out, in_), reads, [], "out", 16)
 
-    select_scan(T.tab, "tab", 0, c1)
-    select_u16(T.moff, "moffa", 0, c1)
-    g_m("s", 0, c1, "moffa", "mt0")
-    select_scan(T.tab, "tab", c1, M)
-    select_u16(T.moff, "moffb", c1, M)
-    g_m("s", c1, c2, "moffb", "mt1")
-    g_m("v", c3, M, "moffb", "mt3")
-    mm("@y0", C, T.wq[:, 0:128], T.wp[:, 0:128], T.oq[:, 0:C], T.op[:, 0:C], True, True, ["w", "s3"])
-    q_m(0, c1, ["mt0"], "o0")
-    q_m(c3, M, ["mt3"], "o2")
-    store("y", T.oc[:, 0:4 * (C + c1)], by(T.oq[:, 0:C + c1]), ["s3", "o0"])
-    store("y", T.oc[:, 4 * (C + c3):4 * (C + M)], by(T.oq[:, C + c3:C + M]), ["o2"])
-    g_m("v", c2, c3, "moffb", "mt2")
-    q_m(c1, c3, ["mt1", "mt2"], "o1")
-    act(T.yo[:], T.py[:, 0:C], F.Copy, ["@y0"], ["yo"])
-    store("y", T.oc[:, 4 * (C + c1):4 * (C + c3)], by(T.oq[:, C + c1:C + c3]), ["o1"])
+    for a, b in zip(ST, ST[1:]):
+        quant(T.oq[:, C + a:C + b], T.op[:, C + a:C + b], T.mt[:, 4 * a:4 * b],
+              ["mt%d" % x for x, y in zip(FIN, FIN[1:]) if x < b and y > a], ["o%d" % a])
+        lo = 0 if a == 0 else C + a
+        store("y", T.oc[:, 4 * lo:4 * (C + b)], by(T.oq[:, lo:C + b]), ["o%d" % a] + (S3 if a == 0 else []))
     store("s", T.y[:], T.yo[:], ["yo"])
     for k in range(4):
-        store("ys"[k % 2], T.osc[4 * k:4 * k + 4, :], T.op[32 * k:32 * k + 4, :], ["o0", "o1", "o2", "s3"])
-    _emit(g, T, ops)
+        store("ys"[k % 2], T.osc[4 * k:4 * k + 4, :], T.op[32 * k:32 * k + 4, :], ["o%d" % a for a in ST[:-1]] + S3)
+    _emit(g, T, arrivals, ops)

@@ -3,9 +3,9 @@ from concourse.mybir import dt, AluOpType, AxisListType, ActivationFunctionType
 C, M, NV = 288, 512, 3
 K16 = C // 16
 POOL = M + NV * C
-X = 8.0
+KEEP = 8192.0
 UP = 511.0
-CH, CUT = 64, 160
+CH, CUT = 64, 128
 FIN, ST = (0, 128, 256, 320, 384, M), (0, 128, 256, M)
 R = CH // 16
 O = [8 * _r * _r + 10 * _r for _r in range(R + 1)]
@@ -18,24 +18,24 @@ for _n, _w, _d in (
         ("xin", 4 * C, BF), ("uin", 512, BF), ("pool", 4 * POOL, BF), ("wq", 512, Q4), ("wp", 512, U8),
         ("uq", 128, Q4), ("up", 128, U8), ("oq", C + M, Q4), ("op", C + M, U8), ("bt", 4 * C, BF), ("bq", C, Q4),
         ("bp", C, U8), ("yt", 4 * C, BF), ("mt", 4 * M, BF), ("yo", C, F32), ("ft", 672, BF), ("fq", 400, Q4),
-        ("fp", 400, U8), ("ze", 528, BF), ("zz", 528, BF), ("wa", 512, BF), ("wb", 512, BF), ("eq", 512, Q4),
-        ("ep", 512, U8), ("zq", 512, Q4), ("zp", 512, U8), ("aq", 256, Q4), ("ap", 256, U8), ("pi", 8, I32),
-        ("pj", 8, I32), ("pf", 8, F32), ("j16", 16, F32), ("spare", 8, F32), ("d16", 16, F32), ("d4", 4, F32),
-        ("col", 8, F32), ("g8", 8, F32), ("ia", 128, BF), ("ib", 128, BF), ("iz", 128, BF), ("idj", 128, BF),
-        ("i4", 384, BF), ("c4", 384, BF), ("cdi", 2 * CH, BF), ("cd", NE, BF), ("tab", M + 4 * CH, F32),
+        ("fp", 400, U8), ("ze", 528, BF), ("wa", 512, BF), ("wb", 512, BF), ("eq", 512, Q4),
+        ("ep", 512, U8), ("aq", 256, Q4), ("ap", 256, U8), ("pi", 8, I32),
+        ("pj", 8, I32), ("pf", 8, F32), ("j16", 16, F32), ("spare", 8, F32), ("d16", 16, F32),
+        ("col", 8, F32), ("g8", 8, F32), ("ia", 128, BF), ("ib", 128, BF), ("idj", 128, BF), ("idt", M, BF),
+        ("i4", 384, BF), ("c4", 384, BF), ("cdi", 2 * CH, BF), ("cd", NE - 2 * PER, BF), ("tab", M + 4 * CH, F32),
         ("val", NV * C, F32), ("sca", 72, F32), ("prow", C, F32), ("scp", M, F32), ("boff", 72, U16),
-        ("moff", 128, U16), ("pos", 2, U16), ("pe", 4, F32), ("ne0", NE, BF), ("ne1", NE, BF), ("scd", NE, BF)):
+        ("moff", 128, U16), ("pos", 4, U16), ("pe", 4, F32), ("ne", NE, BF), ("scd", NE, BF)):
     SCRATCH[_n] = ("sbuf", [128, _w], _d)
 for _t in range(NV):
     for _n, _w, _d in (("sq", C, Q4), ("sp", C, U8), ("yq", C, Q4), ("yp", C, U8), ("af", K16, F32),
-                       ("ar", C, BF), ("so", 32, U16), ("ao", K16, U16), ("la", K16, U16), ("ls", K16, U16)):
+                       ("ar", C, BF), ("so", 32, U16), ("ao", K16, U16), ("la", K16, U16)):
         SCRATCH[_n + str(_t)] = ("sbuf", [128, _w], _d)
 SEMAPHORES = ["cv", "cs", "ct", "cg", "sent", "dx", "du", "dm", "dw", "dp", "out"] + [
-    _a + _b for _a in ("sa", "sb", "pa", "la", "ls") for _b in "123"]
+    _a + _b for _a in ("sa", "sb", "pa", "la", "lb") for _b in "123"]
 COUNTER = {"v": "cv", "s": "cs", "t": "ct", "g": "cg"}
 
-ORDER = [0,5,1,2,3,4,17,6,12,82,21,20,22,23,18,7,24,25,8,84,80,19,85,29,33,62,26,9,36,30,11,27,35,39,40,42,63,41,72,31,28,37,38,10,52,51,88,46,57,73,47,34,54,43,53,89,49,90,44,45,55,50,91,68,48,66,92,58,60,59,98,96,94,32,13,15,16,14,56,97,93,64,69,70,109,108,61,106,95,99,110,105,104,124,125,65,101,103,71,100,67,127,126,102,129,130,107,186,83,81,187,77,74,131,128,174,134,168,182,111,115,112,133,132,116,114,173,135,118,177,181,119,113,117,120,136,122,78,121,142,138,169,167,183,184,123,139,79,179,75,140,178,143,166,159,175,171,153,141,185,176,76,170,172,180,144,87,86,160,145,188,154,151,157,152,146,149,189,150,147,155,164,190,163,158,162,161,226,225,227,224,148,137,165,191,216,214,192,213,156,197,204,202,198,201,193,205,194,231,206,215,228,208,195,196,229,220,223,199,232,221,222,230,210,207,203,233,212,235,234,238,237,236,200,211,239,240,209,241,251,244,217,250,245,249,255,252,243,254,242,218,253,256,219,247,246,257,248,263,259,260,261,280,264,262,281,265,278,287,266,270,279,271,272,267,273,288,274,283,282,268,286,289,323,322,276,285,284,269,258,312,311,310,313,302,308,299,290,293,307,297,301,303,294,298,292,296,304,309,300,295,305,306,291,275,314,325,317,328,315,277,326,316,327,318,320,324,329,332,319,331,321,330,333,335,334,338,340,339,355,337,342,344,336,343,356,341,349,348,347,345,353,346,357,352,362,364,366,351,350,368,358,367,354,359,363,365,361,360,374,369,376,370,380,375,372,377,378,371,381,373,379,383,382,387,386,391,389,384,385,392,390,388,395,393,394,399,398,397,396]
-ON_V = {19,36,77,78,102,103,105,109,132,134,165,166,169,174,177,178,181,202,205,208,214,215,228,235,238,247,253,293,299,302,305,306,311,313,331,334,351,369,383,384,385}
+ORDER = [0,1,2,4,3,17,5,21,20,22,18,19,7,6,75,8,23,24,27,9,35,25,66,42,40,39,11,77,26,41,47,55,28,67,45,51,52,38,44,78,30,36,68,76,12,43,70,33,14,69,79,53,49,46,74,37,73,29,56,80,10,48,50,34,81,57,83,54,88,87,82,13,16,84,62,89,85,91,60,90,93,86,58,64,97,144,94,161,98,31,63,59,61,65,173,158,96,101,155,92,71,100,95,102,154,99,145,151,147,106,146,163,32,104,107,109,103,148,113,152,156,108,110,171,72,153,157,150,105,149,112,168,167,111,169,172,117,159,122,15,119,114,116,162,115,160,123,118,165,176,166,164,170,129,124,174,177,125,130,138,136,126,131,127,178,132,139,137,140,128,142,133,175,134,179,135,121,120,141,143,180,244,245,189,248,247,255,190,192,263,191,259,249,258,252,253,182,193,246,196,183,184,195,181,262,250,194,197,198,275,256,199,203,204,257,274,254,272,264,202,273,269,251,201,207,200,208,188,186,206,185,205,260,210,267,271,213,187,265,270,209,211,266,268,212,261,217,276,214,219,222,215,216,278,223,218,224,221,229,277,279,225,240,230,238,226,231,241,227,280,232,239,236,228,242,233,281,237,243,234,282,235,220,284,283,285,286,321,291,322,292,327,329,335,325,326,323,331,333,324,332,334,328,293,330,294,336,340,298,297,295,337,349,351,352,339,350,296,299,338,300,301,305,303,304,306,348,355,346,343,341,342,347,290,345,302,344,289,288,356,307,313,314,309,310,287,353,308,312,317,315,357,318,316,354,319,311,358,366,368,364,320,362,367,359,360,361,372,365,376,374,369,363,370,373,380,377,375,371,378,381,379,383,382,391,395,389,387,386,392,384,385,390,388,393,396,394,400,398,399,397]
+ON_V = {34,71,87,91,104,115,148,152,154,161,189,195,199,206,216,254,255,264,291,298,301,325,326,369,383,386}
 
 
 def _emit(g, T, arrivals, ops):
@@ -145,37 +145,37 @@ def rank_program(g, core, T, topo):
     op("y", lambda: g.sync.dma_start(T.wp[:], T.ws[:]), [], ["w"], "dp", 16)
 
     cc, grp, w4, t4 = (T.pf[:, i:i + 1] for i in range(4))
-    weight, inv, inv1024, low, minus = (T.col[:, i:i + 1] for i in range(1, 6))
+    weight, lst, key, low, minus, held, c7 = (T.col[:, i:i + 1] for i in range(1, 8))
     iota(T.pi[:, 0:1], [[0, 1]], 0, 1, ["pi"], small=False)
     iota(T.j16[:], [[1, 16]], 0, 0, ["j16"])
     iota(T.ib[:], [[1, 8], [8, 4], [0, 4]], 0, 0, ["ib"])
     iota(T.idj[:], [[1, 128]], 0, -1, ["idj"])
     iota(T.ia[:], [[1, 8], [0, 4], [8, 4]], 0, 0, ["ia"])
-    iota(T.iz[:], [[1, 8], [0, 16]], 0, 0, ["iz"])
+    iota(T.idt[:], [[1024, M]], -256 * 1024, 0, ["idt"])
     iota(T.i4[:], [[0, 96], [1, 4]], 0, 0, ["i4"])
     iota(T.cdi[:], [[1, 2 * CH]], -CH, 0, ["cdi"])
-    iota(T.tab[:], [[4, M + 4 * CH]], 4 * int(UP), 0, ["tab"])
+    iota(T.tab[:], [[4, M + 4 * CH]], 0, 0, ["tab"])
     for v in range(NV):
-        iota(T.val[:, C * v:C * v + C], [[4, C]], 4 * (M + C * v + int(UP)), 0, ["val%d" % v])
+        iota(T.val[:, C * v:C * v + C], [[4, C]], 4 * (M + C * v), 0, ["val%d" % v])
 
     op("v", lambda: V.memset(T.ze[:], 0.0), [], ["ze", "zero"])
-    times(T.zz[:], T.ze[:], 0.0, ["zero"], ["zz"])
     times(T.ft[:, C:672], T.ze[:, 0:672 - C], 0.0, ["zero"], ["ftz"])
     ts(T.pj[:, 0:1], T.pi[:, 0:1], 15, None, A.bitwise_and, None, ["pi"], ["pj0"])
     ts(T.pj[:, 1:2], T.pi[:, 0:1], 4, None, A.arith_shift_right, None, ["pi"], ["pj1"])
     ts(T.pj[:, 2:3], T.pi[:, 0:1], 2, 3, A.arith_shift_right, A.bitwise_and, ["pi"], ["pj2"])
     ts(T.pj[:, 3:4], T.pi[:, 0:1], 3, None, A.bitwise_and, None, ["pi"], ["pj3"])
-    quant(T.fq[:, 0:128], T.fp[:, 0:128], T.ze[:, 0:512], ["ze"], ["fz0"])
     op("v", lambda: V.tensor_copy(T.pf[:, 0:4], T.pj[:, 0:4]), ["pj0", "pj1", "pj2", "pj3"], ["pf"])
     ts(T.d16[:], T.j16[:], cc, 1.0, A.is_lt, A.add, ["j16", "pf"], ["d16"])
     op("v", lambda: V.tensor_reduce(T.col[:, 0:1], T.d16[:], AxisListType.X, A.mult), ["d16"], ["col0"])
     ts(weight, cc, 8.5, T.col[:, 0:1], A.is_lt, A.mult, ["pf", "col0"], ["weight"])
     line(T.g8[:, 0:4], T.j16[:, 0:4], 8.0, grp, ["j16", "pf"], ["g8"])
-    ts(T.d4[:, 0:3], T.j16[:, 0:3], w4, 1.0 / X, A.is_lt, A.max, ["j16", "pf"], ["d4"])
-    op("v", lambda: V.tensor_reduce(inv, T.d4[:, 0:3], AxisListType.X, A.mult), ["d4"], ["inv"])
-    times(inv1024, inv, 1024.0, ["inv"], ["inv1024"])
-    line(low, t4, 1.0, -4.0 * UP, ["pf"], ["low"])
-    ts(T.c4[:], T.i4[:], w4, X, A.not_equal, A.mult, ["i4", "pf"], ["c4"])
+    act(lst, w4, F.Identity, KEEP, UP - 3 * KEEP, ["pf"], ["lst"])
+    act(key, w4, F.Identity, 512 * KEEP, -512.0 - 512 * 3 * KEEP, ["pf"], ["key"])
+    act(low, t4, F.Identity, 1.0, 2 * UP, ["pf"], ["low"])
+    act(c7, t4, F.Identity, 1.0, -3 * KEEP, ["pf"], ["c7"])
+    act(held, w4, F.Identity, KEEP, c7, ["pf", "c7"], ["held"])
+    ts(T.c4[:], T.i4[:], w4, 5 * KEEP, A.is_gt, A.mult, ["i4", "pf"], ["c4"])
+    line(T.c4[:], T.c4[:], 1.0, -4 * KEEP, ["c4"], ["c4"])
     ts(T.ze[:, 3:512:4], T.idj[:], 0.0, 64.0, A.is_equal, A.mult, ["idj"], ["ze", "zero"])
     line(T.spare[:, 4:5], cc, -4.0, -float(M), ["pf"], ["sp4"])
     line(T.spare[:, 0:4], T.j16[:, 0:4], -64.0, T.spare[:, 4:5], ["j16", "sp4"], ["spare"])
@@ -185,15 +185,11 @@ def rank_program(g, core, T, topo):
         for t in range(4):
             act(tile[:, t:512:4], src[:], F.Abs, -1.0, T.g8[:, t:t + 1], ["i" + name, "g8"], [parts[t]])
         act(tile[:], tile[:], F.Relu, minus, weight, parts + ["minus", "weight"], parts)
-    act(T.iz[:], T.iz[:], F.Abs, -1.0, grp, ["iz", "pf"], ["iz"])
-    act(T.zz[:, 3:512:4], T.iz[:], F.Relu, minus, weight, ["iz", "minus", "weight"], ["zz"])
     for b in range(4):
         quant(T.eq[:, 128 * b:128 * b + 128], T.ep[:, 128 * b:128 * b + 128], T.ze[:, 3 - b:515 - b], ["ze"], ["e%d" % b])
     quant(T.aq[:, 128:256], T.ap[:, 128:256], T.wb[:], ["wb%d" % t for t in range(4)], ["qwb"])
     quant(T.aq[:, 0:128], T.ap[:, 0:128], T.wa[:], ["wa%d" % t for t in range(4)], ["qwa"])
     quant(T.uq[:], T.up[:], T.uin[:], ["uin"], ["uq"])
-    for b in range(4):
-        quant(T.zq[:, 128 * b:128 * b + 128], T.zp[:, 128 * b:128 * b + 128], T.zz[:, 3 - b:515 - b], ["zz"], ["z%d" % b])
     act(T.cdi[:], T.cdi[:], F.Abs, -1.0, cc, ["cdi", "pf"], ["cdi"])
     act(T.cdi[:], T.cdi[:], F.Relu, -1.0, 1.0, ["cdi"], ["cdi"])
     for r in range(R):
@@ -204,83 +200,78 @@ def rank_program(g, core, T, topo):
     act(T.pe[:, 0:1], t4, F.Identity, 8.0, 26.0, ["pf"], ["pe0"])
     act(T.pe[:, 1:2], T.pe[:, 0:1], F.Identity, t4, 16.0, ["pf", "pe0"], ["pe1"])
     act(T.pe[:, 2:3], w4, F.Identity, float(PER), T.pe[:, 1:2], ["pf", "pe1"], ["pe2"])
-    act(T.pe[:, 0:2], T.j16[:, 0:2], F.Identity, 4.0 * PER, T.pe[:, 2:3], ["j16", "pe2"], ["pe0", "pe1"])
-    ts(T.pos[:], T.pe[:, 0:2], NE - 1.0, None, A.min, None, ["pe0", "pe1"], ["pos"])
+    ts(T.pos[:, 0:1], T.pe[:, 2:3], 2 * PER - 1.0, None, A.min, None, ["pe2"], ["posa"])
+    ts(T.pos[:, 2:3], T.pe[:, 2:3], NE - 2 * PER - 1.0, None, A.min, None, ["pe2"], ["posb"])
     CD, have = ["cdp%d" % r for r in range(R)], PER
-    while have < NE:
-        w = min(have, NE - have)
+    while have < NE - 2 * PER:
+        w = min(have, NE - 2 * PER - have)
         copy(T.cd[:, have:have + w], T.cd[:, 0:w], list(CD), ["cd%d" % (len(CD) + 1)])
         CD.append("cd%d" % (len(CD) + 1))
         have += w
-    for x in range(2):
-        for r in range(R):
-            z = len(range(O[r + 1] - 1, NE, PER))
-            act(T["ne%d" % x][:, O[r + 1] - 1:NE:PER], T.j16[:, 0:z], F.Identity, 0.0, 1024.0, ["j16"], ["nez%d%d" % (x, r)])
+    for r in range(R):
+        z = len(range(O[r + 1] - 1, NE, PER))
+        act(T.ne[:, O[r + 1] - 1:NE:PER], T.j16[:, 0:z], F.Identity, 0.0, 1024.0, ["j16"], ["nez%d" % r])
 
     def a_mm(q, p, res, bk, h):
         mm(bk, h[1] - h[0], T.uq[:], T.up[:], q[:, h[0]:h[1]], p[:, h[0]:h[1]], True, True, ["uq", res])
 
     def bits(bk, h):
         buf, o = bank(bk)
-        ts(T.ft[:, h[0]:h[1]], buf[:, o:o + h[1] - h[0]], 0.0, 1.0, A.is_gt, A.add, [bk], ["ft" + c for c in runs(h)])
+        act(T.ft[:, h[0]:h[1]], buf[:, o:o + h[1] - h[0]], F.Sign, 2.0 ** 50, -2.0 ** -100, [bk], ["ft" + c for c in runs(h)])
 
-    def q_bits(w):
-        quant(T.fq[:, 128:128 + w], T.fp[:, 128:128 + w], T.ft[:, 0:4 * w], ["fta", "ftb", "ftz"], ["fq"])
+    def q_bits():
+        quant(T.fq[:, 128:256], T.fp[:, 128:256], T.ft[:, 0:512], ["fta", "ftb", "ftz"], ["fq"])
 
-    def list_mm(bk, which):
+    def q_bits_b():
+        quant(T.fq[:, 272:400], T.fp[:, 272:400], T.ft[:, CUT:CUT + 512], ["ftb", "ftz"], ["fqb"])
+
+    def list_mm(bk, which, o=128, res="fq"):
         w = 128 * which
-        mm(bk, 128, T.aq[:, w:w + 128], T.ap[:, w:w + 128], T.fq[:, 128:256], T.fp[:, 128:256], True, True,
-           ["fq", "qwb" if which else "qwa"])
+        mm(bk, 128, T.aq[:, w:w + 128], T.ap[:, w:w + 128], T.fq[:, o:o + 128], T.fp[:, o:o + 128], True, True,
+           [res, "qwb" if which else "qwa"])
 
-    def row_mm(bk, half):
-        for i, o in ((0, 128), (1, 56)):
-            t = 2 * half + i
-            mm(bk, 144, T.zq[:, 128 * t:128 * t + 128], T.zp[:, 128 * t:128 * t + 128],
-               T.fq[:, o:o + 144], T.fp[:, o:o + 144], i == 0, i == 1, ["fq", "fz0", "z%d" % t])
-
-    def row_read(v, bk, half):
+    def list_scan(bk, h):
         buf, o = bank(bk)
-        for i in range(2):
-            t = 2 * half + i
-            line(T["ar%d" % v][:, t:C:4], buf[:, o + 72 * i:o + 72 * i + 72], 1024.0, -1024.0 * (UP + 256.0), [bk],
-                 ["ar%d%d" % (v, t)])
+        w = (h[1] - h[0]) // 4
+        op("v", lambda: V.tensor_tensor_scan(T.sca[:, h[0] // 4:h[1] // 4], T.c4[:, 0:w], buf[:, o:o + w], 0.0,
+                                             A.add, A.max), [bk, "c4"], ["sca" + c for c in runs(h)])
 
-    def list_scan(bk):
-        buf, o = bank(bk)
-        op("v", lambda: V.tensor_tensor_scan(T.sca[:], T.c4[:, 0:72], buf[:, o:o + 72], 0.0, A.mult, A.max),
-           [bk, "c4"], ["sca"])
+    def list_out(v, h):
+        a, b, c = h[0] // 16, h[1] // 16, runs(h)
+        ts(T["ao%d" % v][:, a:b], T.sca[:, h[0] // 4 + 3:h[1] // 4:4], lst, 0.5, A.add, A.mult, ["sca" + c, "lst"],
+           ["ao%d%s" % (v, c)])
+        send(nxt, T["la%d" % v][:, a:b], T["ao%d" % v][:, a:b], "l%s%d" % (c, v), ["ao%d%s" % (v, c)], ["la%d%s" % (v, c)])
 
-    def list_out(v):
-        ts(T["ao%d" % v][:], T.sca[:, 3:72:4], inv, -UP, A.mult, A.add, ["sca", "inv"], ["ao%d" % v])
-        send(nxt, T["la%d" % v][:], T["ao%d" % v][:], "la%d" % v, ["ao%d" % v], ["la%d" % v])
-
-    def list_f32(v):
-        line(T["af%d" % v][:], T.sca[:, 3:72:4], inv1024, -1024.0 * (UP + 256.0), ["sca", "inv1024"], ["af%d" % v])
-
-    def dedupe(v):
-        x = v % 2
-        for k in range(K16):
+    def slots(v, h):
+        c = runs(h)
+        k0, k1 = h[0] // 16, h[1] // 16
+        z0, z1 = (0, 2 * PER) if c == "a" else (2 * PER, NE)
+        la, ar, af = T["la%d" % v], T["ar%d" % v], T["af%d" % v]
+        gather(ar[:, h[0]:h[1]], T.idt[:], la[:, k0:k1], ["idt", "la%d%s" % (v, c)], ["ar%d%s" % (v, c)])
+        if v:
+            ts(af[:, k0:k1], la[:, k0:k1], 1024.0, -256.0 * 1024, A.mult, A.add, ["la%d%s" % (v, c)], ["af%d%s" % (v, c)])
+        for k in range(k0, k1):
             c0, w, z = CH * (k // R), 16 * (k % R + 1), PER * (k // R) + O[k % R]
-            o, i, s = T["ne%d" % x][:, z:z + w], T["ar%d" % v][:, c0:c0 + w], T["af%d" % v][:, k:k + 1]
+            o, i, s = T.ne[:, z:z + w], ar[:, c0:c0 + w], af[:, k:k + 1]
             either(lambda o=o, i=i, s=s: V.tensor_scalar(o, i, s, 1024.0, A.not_equal, A.mult),
                    lambda o=o, i=i, s=s: S.activation(o, i, F.Abs, scale=-1.0, bias=s),
-                   ["ar%d%d" % (v, t) for t in range(4)] + ["af%d" % v], ["ne%d_%d" % (x, k)])
+                   ["ar%d%s" % (v, c), "af%d%s" % (v, c)], ["ne_%d" % k])
         for r in range(R):
-            times(T["ne%d" % x][:, O[r + 1] - 2:NE:PER], T["af%d" % v][:, r:K16:R], -1.0 / 1024.0, ["af%d" % v],
-                  ["neo%d%d" % (x, r)])
-        op("v", lambda: V.tensor_tensor_scan(T.scd[:], T.cd[:], T["ne%d" % x][:], 0.0, A.add, A.min),
-           CD + ["ne%s%d%d" % (c, x, r) for r in range(R) for c in "oz"] + ["ne%d_%d" % (x, k) for k in range(K16)], ["scd"])
-        ts(T["so%d" % v][:], T.scd[:].indirect(T.pos[:]), -1.0, 256.0, A.mult, A.add, ["scd", "pos"], ["so%d" % v])
-        if v:
-            send(nxt, T["ls%d" % v][:], T["so%d" % v][:, 0:K16], "ls%d" % v, ["so%d" % v], ["ls%d" % v])
+            times(T.ne[:, z0 + O[r + 1] - 2:z1:PER], af[:, k0 + r:k1:R], -1.0 / 1024.0, ["af%d%s" % (v, c)],
+                  ["neo%d%s" % (r, c)])
+        op("v", lambda: V.tensor_tensor_scan(T.scd[:, z0:z1], T.cd[:, 0:z1 - z0], T.ne[:, z0:z1], 0.0, A.add, A.min),
+           CD + ["neo%d%s" % (r, c) for r in range(R)] + ["nez%d" % r for r in range(R)]
+           + ["ne_%d" % k for k in range(k0, k1)], ["scd" + c])
+        s = 0 if c == "a" else 16
+        ts(T["so%d" % v][:, s:s + 16], T.scd[:, z0:z1].indirect(T.pos[:, s // 8:s // 8 + 1]), -1.0, 256.0, A.mult, A.add,
+           ["scd" + c, "pos" + c], ["so%d%s" % (v, c)])
 
     def scatter(v):
-        name = "ls%d" % v if v else "so0"
         for a in reversed(range(0, K16, R)):
-            b = min(a + R, K16)
-            op("v", lambda a=a, b=b: V.tensor_copy(T.tab[:].indirect(T[name][:, a:b]),
-                                                   T.val[:, C * v + 16 * a:C * v + 16 * b]),
-               [name, "val%d" % v], ["tab"])
+            b, s = min(a + R, K16), 8 * (a >= 8)
+            op("v", lambda a=a, b=b, s=s: V.tensor_copy(T.tab[:].indirect(T["so%d" % v][:, a + s:b + s]),
+                                                        T.val[:, C * v + 16 * a:C * v + 16 * b]),
+               ["so%d%s" % (v, "ab"[a >= 8]), "val%d" % v], ["tab"])
 
     def pool_names(v):
         return ["pool"] + ["n%d%d%s" % (t, b, c) for t in range(v) for b in range(4) for c in "ab"]
@@ -288,14 +279,13 @@ def rank_program(g, core, T, topo):
     def gather(out, win, off, reads, writes): copy(out, win.indirect(off), reads, writes)
 
     def pick(src, res, off, out, a, b):
-        op("v", lambda: V.tensor_tensor_scan(T.scp[:, a:b], T.c4[:, 0:b - a], src[:, a:b], 0.0, A.mult, A.max),
+        op("v", lambda: V.tensor_tensor_scan(T.scp[:, a:b], T.c4[:, 0:b - a], src[:, a:b], 0.0, A.add, A.max),
            [res, "c4"], ["scp%d" % min(a, 1)])
-        ts(off[:, a // 4:b // 4], T.scp[:, a + 3:b:4], inv, low, A.mult, A.add,
-           ["scp%d" % min(a, 1), "inv", "low"], [out])
+        ts(off[:, a // 4:b // 4], T.scp[:, a + 3:b:4], held, None, A.add, None, ["scp%d" % min(a, 1), "held"], [out])
 
     def pointers(v, h):
         c = runs(h)
-        gather(T.prow[:, h[0]:h[1]], T.tab[:, 0:M], T["la%d" % v][:, h[0] // 16:h[1] // 16], ["tab", "la%d" % v],
+        gather(T.prow[:, h[0]:h[1]], T.tab[:, 0:M], T["la%d" % v][:, h[0] // 16:h[1] // 16], ["tab", "la%d%s" % (v, c)],
                ["prow" + c])
         pick(T.prow, "prow" + c, T.boff, "boff" + c, h[0], h[1])
 
@@ -357,38 +347,32 @@ def rank_program(g, core, T, topo):
             pass_scales(v, nxt, T["sp%d" % w])
             a_mm(T["yq%d" % v], T["yp%d" % v], "y%db" % v, "@n0", HB)
             bits("@n0", HB)
+            q_bits_b()
+            list_mm("@n1", 0, 272, "fqb")
+            list_scan("@n1", HB)
+            list_out(w, HB)
             a_mm(T["yq%d" % v], T["yp%d" % v], "y%da" % v, "@y0", HA)
             bits("@y0", HA)
-            q_bits(128)
+            q_bits()
             list_mm("@y1", 0)
-            list_scan("@y1")
-            list_out(w)
-            row_mm("@y2", 0)
-            row_mm("@y3", 1)
+            list_scan("@y1", HA)
+            list_out(w, HA)
             for b in range(4):
                 to_pool(v, b, "@n%d" % ((b + 2) % 4), ALL)
-            row_read(w, "@y2", 0)
-            row_read(w, "@y3", 1)
-            list_f32(w)
-        if v == 0:
-            dedupe(0)
+        slots(v, HB)
+        slots(v, HA)
         scatter(v)
-        if w < NV:
-            dedupe(w)
 
     quant(T.sq0[:], T.sp0[:], T.xin[:], ["xin"], ["s0"])
-    a_mm(T.sq0, T.sp0, "s0", "@n0", ALL)
-    bits("@n0", ALL)
-    q_bits(144)
-    list_mm("@n1", 1)
-    list_mm("@n2", 0)
-    ts(T.boff[:], T.pn[:, 512:584], 4.0, low, A.mult, A.add, ["@n1", "low"], ["boffa", "boffb"])
-    list_scan("@n2")
-    row_mm("@n3", 0)
-    row_mm("@n0", 1)
-    row_read(0, "@n3", 0)
-    row_read(0, "@n0", 1)
-    list_f32(0)
+    a_mm(T.sq0, T.sp0, "s0", "@y0", ALL)
+    bits("@y0", ALL)
+    q_bits()
+    list_mm("@y1", 1)
+    list_mm("@y2", 0)
+    ts(T.boff[:], T.py[:, 512:584], 2.0, low, A.mult, A.add, ["@y1", "low"], ["boffa", "boffb"])
+    list_scan("@y2", ALL)
+    ts(T.la0[:], T.sca[:, 3:72:4], lst, 0.5, A.add, A.mult, ["scaa", "scab", "lst"], ["la0a", "la0b"])
+    line(T.af0[:], T.sca[:, 3:72:4], 512.0, key, ["scaa", "scab", "key"], ["af0a", "af0b"])
     for v in range(NV):
         visit(v)
     pass_codes(2, home, T.oq, ALL)
@@ -413,8 +397,8 @@ def rank_program(g, core, T, topo):
     for a, b in zip(ST, ST[1:]):
         quant(T.oq[:, C + a:C + b], T.op[:, C + a:C + b], T.mt[:, 4 * a:4 * b],
               ["mt%d" % x for x, y in zip(FIN, FIN[1:]) if x < b and y > a], ["o%d" % a])
-        lo = 0 if a == 0 else C + a
-        store("y", T.oc[:, 4 * lo:4 * (C + b)], by(T.oq[:, lo:C + b]), ["o%d" % a] + (S3 if a == 0 else []))
+        store("y", T.oc[:, 4 * (C + a):4 * (C + b)], by(T.oq[:, C + a:C + b]), ["o%d" % a])
+    store("y", T.oc[:, 0:4 * C], by(T.oq[:, 0:C]), ["s3a", "s3b"])
     store("s", T.y[:], T.yo[:], ["yo"])
     for k in range(4):
         store("ys"[k % 2], T.osc[4 * k:4 * k + 4, :], T.op[32 * k:32 * k + 4, :], ["o%d" % a for a in ST[:-1]] + S3)

@@ -3,39 +3,41 @@ from concourse.mybir import dt, AluOpType, AxisListType, ActivationFunctionType
 C, M, NV = 288, 512, 3
 K16 = C // 16
 POOL = M + NV * C
-KEEP = 8192.0
+KEEP = 6144.0
 UP = 511.0
-CH, CUT = 64, 128
-FIN, ST = (0, 128, 256, 320, 384, M), (0, 128, 256, M)
-R = CH // 16
+R, CUT, HALF = 4, 128, 64
+CH = 16 * R
+PK, FIN, ST = (0, 128, 320, M), (0, 128, 256, 320, 384, M), (0, 128, 256, M)
 O = [8 * _r * _r + 10 * _r for _r in range(R + 1)]
 PER = O[R]
-NE = PER * (K16 // R) + O[K16 % R]
-HA, HB, ALL = (0, CUT), (CUT, C), (0, C)
+HA, HB = (0, CUT), (CUT, C)
+NE = {_c: PER * (_k // R) + O[_k % R] for _c, _k in (("a", CUT // 16), ("b", (C - CUT) // 16))}
+NX, CW = NE["b"], 192
 Q4, U8, BF, F32, I32, U16 = "float8_e4m3fn_x4", "uint8", "bfloat16", "float32", "int32", "uint16"
 SCRATCH = {"py": ("psum", [128, 2048], F32), "pn": ("psum", [128, 2048], F32)}
 for _n, _w, _d in (
         ("xin", 4 * C, BF), ("uin", 512, BF), ("pool", 4 * POOL, BF), ("wq", 512, Q4), ("wp", 512, U8),
         ("uq", 128, Q4), ("up", 128, U8), ("oq", C + M, Q4), ("op", C + M, U8), ("bt", 4 * C, BF), ("bq", C, Q4),
-        ("bp", C, U8), ("yt", 4 * C, BF), ("mt", 4 * M, BF), ("yo", C, F32), ("ft", 672, BF), ("fq", 400, Q4),
-        ("fp", 400, U8), ("ze", 528, BF), ("wa", 512, BF), ("wb", 512, BF), ("eq", 512, Q4),
+        ("bp", C, U8), ("yt", 4 * C, BF), ("mt", 4 * M, BF), ("yo", C, F32), ("ft", CUT + 512, BF), ("fq", 256, Q4),
+        ("fp", 256, U8), ("ze", 528, BF), ("wa", 512, BF), ("wb", 512, BF), ("eq", 512, Q4),
         ("ep", 512, U8), ("aq", 256, Q4), ("ap", 256, U8), ("pi", 8, I32),
         ("pj", 8, I32), ("pf", 8, F32), ("j16", 16, F32), ("spare", 8, F32), ("d16", 16, F32),
         ("col", 8, F32), ("g8", 8, F32), ("ia", 128, BF), ("ib", 128, BF), ("idj", 128, BF), ("idt", M, BF),
-        ("i4", 384, BF), ("c4", 384, BF), ("cdi", 2 * CH, BF), ("cd", NE - 2 * PER, BF), ("tab", M + 4 * CH, F32),
+        ("i4", CW, BF), ("c4", CW, BF), ("cdi", 2 * CH, BF), ("cd", NX, BF), ("tab", M + 4 * CH, F32),
         ("val", NV * C, F32), ("sca", 72, F32), ("prow", C, F32), ("scp", M, F32), ("boff", 72, U16),
-        ("moff", 128, U16), ("pos", 4, U16), ("pe", 4, F32), ("ne", NE, BF), ("scd", NE, BF)):
+        ("moff", 128, U16), ("pos", 4, U16), ("pe", 4, F32), ("nea", NE["a"], BF), ("neb", NE["b"], BF),
+        ("scda", NE["a"], BF), ("scdb", NE["b"], BF)):
     SCRATCH[_n] = ("sbuf", [128, _w], _d)
 for _t in range(NV):
     for _n, _w, _d in (("sq", C, Q4), ("sp", C, U8), ("yq", C, Q4), ("yp", C, U8), ("af", K16, F32),
-                       ("ar", C, BF), ("so", 32, U16), ("ao", K16, U16), ("la", K16, U16)):
+                       ("ar", C, BF), ("so", 32, U16), ("ao", 32, U16), ("la", 32, U16), ("sl", 32, U16)):
         SCRATCH[_n + str(_t)] = ("sbuf", [128, _w], _d)
-SEMAPHORES = ["cv", "cs", "ct", "cg", "sent", "dx", "du", "dm", "dw", "dp", "out"] + [
-    _a + _b for _a in ("sa", "sb", "pa", "la", "lb") for _b in "123"]
+SEMAPHORES = ["cv", "cs", "ct", "cg", "sent", "dxa", "dxb", "du", "dm", "dw", "dp", "out"] + [
+    _a + _b for _a in ("sa", "sb", "pa", "la", "lb", "sl") for _b in "123"]
 COUNTER = {"v": "cv", "s": "cs", "t": "ct", "g": "cg"}
 
-ORDER = [0,1,2,4,3,17,5,21,20,22,18,19,7,6,75,8,23,24,27,9,35,25,66,42,40,39,11,77,26,41,47,55,28,67,45,51,52,38,44,78,30,36,68,76,12,43,70,33,14,69,79,53,49,46,74,37,73,29,56,80,10,48,50,34,81,57,83,54,88,87,82,13,16,84,62,89,85,91,60,90,93,86,58,64,97,144,94,161,98,31,63,59,61,65,173,158,96,101,155,92,71,100,95,102,154,99,145,151,147,106,146,163,32,104,107,109,103,148,113,152,156,108,110,171,72,153,157,150,105,149,112,168,167,111,169,172,117,159,122,15,119,114,116,162,115,160,123,118,165,176,166,164,170,129,124,174,177,125,130,138,136,126,131,127,178,132,139,137,140,128,142,133,175,134,179,135,121,120,141,143,180,244,245,189,248,247,255,190,192,263,191,259,249,258,252,253,182,193,246,196,183,184,195,181,262,250,194,197,198,275,256,199,203,204,257,274,254,272,264,202,273,269,251,201,207,200,208,188,186,206,185,205,260,210,267,271,213,187,265,270,209,211,266,268,212,261,217,276,214,219,222,215,216,278,223,218,224,221,229,277,279,225,240,230,238,226,231,241,227,280,232,239,236,228,242,233,281,237,243,234,282,235,220,284,283,285,286,321,291,322,292,327,329,335,325,326,323,331,333,324,332,334,328,293,330,294,336,340,298,297,295,337,349,351,352,339,350,296,299,338,300,301,305,303,304,306,348,355,346,343,341,342,347,290,345,302,344,289,288,356,307,313,314,309,310,287,353,308,312,317,315,357,318,316,354,319,311,358,366,368,364,320,362,367,359,360,361,372,365,376,374,369,363,370,373,380,377,375,371,378,381,379,383,382,391,395,389,387,386,392,384,385,390,388,393,396,394,400,398,399,397]
-ON_V = {34,71,87,91,104,115,148,152,154,161,189,195,199,206,216,254,255,264,291,298,301,325,326,369,383,386}
+ORDER = [2,0,6,18,21,1,23,22,3,7,80,19,13,73,20,24,37,4,25,27,10,38,34,56,74,26,66,8,28,5,44,57,55,45,81,82,43,46,31,47,83,62,41,91,30,9,42,92,40,58,39,64,79,36,93,63,53,12,48,84,85,51,60,59,67,11,65,77,94,49,32,87,76,78,35,54,95,16,97,29,86,110,102,61,96,88,120,101,116,15,107,50,103,113,105,108,104,111,89,98,90,114,100,112,115,52,167,117,126,177,181,123,109,180,129,172,106,118,124,71,173,169,119,130,176,178,127,174,179,171,168,121,68,72,170,175,70,125,136,131,151,128,122,182,199,137,153,99,196,14,132,75,183,133,187,138,198,184,195,188,144,194,145,159,197,193,191,155,69,189,185,190,139,140,146,141,163,161,192,143,142,157,160,154,147,204,205,215,200,186,148,164,201,217,149,202,206,218,152,165,162,216,135,208,150,214,209,33,203,213,210,166,207,211,212,225,219,222,134,223,246,226,158,220,156,224,227,240,228,231,237,232,300,256,229,301,230,250,243,311,17,259,234,221,253,313,233,247,235,310,305,302,241,312,307,238,248,236,244,242,251,257,260,245,297,239,249,254,261,306,266,252,258,298,281,255,262,267,274,303,268,269,304,275,285,299,276,291,308,309,282,286,270,289,314,293,272,277,271,329,318,327,264,323,315,283,332,265,278,331,320,326,321,319,330,328,324,273,279,316,295,325,322,287,317,280,284,290,333,263,334,351,294,288,339,292,336,296,340,399,360,367,342,411,408,364,410,337,341,335,357,373,409,398,343,338,406,407,344,345,354,395,346,349,348,347,401,370,400,361,402,358,405,403,396,350,404,362,352,359,355,412,397,365,371,413,353,356,374,363,368,366,385,414,372,375,369,381,376,386,377,415,379,382,383,378,384,380,418,389,391,416,390,432,387,392,419,393,417,420,388,394,424,423,421,426,422,430,427,425,434,428,429,431,436,433,435,438,440,439,437]
+ON_V = {28,34,37,58,64,71,72,102,109,118,128,167,170,171,173,189,206,207,208,211,218,225,231,235,245,261,296,302,305,311,312,322,325,330,331,339,345,380,398,403,406,407,422,424,425}
 
 
 def _emit(g, T, arrivals, ops):
@@ -97,7 +99,8 @@ def rank_program(g, core, T, topo):
     def either(fv, fs, reads, writes): ops.append(({"v": fv, "s": fs}, reads, writes, None, None))
     def by(view): return view.bitcast(dt.uint8)
     def bank(name): return T["p" + name[1]], 512 * int(name[2])
-    def runs(h): return "a" if h == HA else "b" if h == HB else "ab"
+    def run(h): return "a" if h == HA else "b"
+    def cols(h): return h[0] // 16, (h[1] - h[0]) // 16
 
     def ts(out, in0, s1, s2, op0, op1, reads, writes):
         if op1 is None:
@@ -121,15 +124,18 @@ def rank_program(g, core, T, topo):
 
     def quant(q, p, src, reads, writes): op("v", lambda: V.quantize_mx(q, p, src), reads, writes)
 
-    def mm(bk, cols, lq, lp, rq, rp, start, stop, reads):
+    def mm(bk, w, lq, lp, rq, rp, start, stop, reads):
         buf, o = bank(bk)
-        op("t", lambda: P.matmul_mx(buf[:, o:o + cols], lq, lp, rq, rp, start, stop), reads, [bk])
+        op("t", lambda: P.matmul_mx(buf[:, o:o + w], lq, lp, rq, rp, start, stop), reads, [bk])
 
     def iota(out, pattern, base, mult, writes, small=True):
         if small:
             op("g", lambda: g.iota(out, pattern, base, mult, allow_small_or_imprecise_dtypes=True), [], writes)
         else:
             op("g", lambda: g.iota(out, pattern, base, mult), [], writes)
+
+    def dma(q, out, in_, reads, writes, sem):
+        op(q, lambda: (g.sync if q == "y" else S).dma_start(out, in_), reads, writes, sem, 16)
 
     def send(dst, out, in_, sem, reads, lands):
         rid, pid = topo.addr(dst)[:2]
@@ -138,178 +144,175 @@ def rank_program(g, core, T, topo):
         op("g", lambda: g.remote_dma(out, in_, T.sem[sem], T.sem["sent"], pid, rid, mask), reads, [], "sent", k)
         arrivals.append((sem, k, lands))
 
-    op("y", lambda: g.sync.dma_start(T.xin[:], T.x[:]), [], ["xin"], "dx", 16)
-    op("s", lambda: S.dma_start(T.uin[:], T.u[:]), [], ["uin"], "du", 16)
-    op("y", lambda: g.sync.dma_start(T.pool[:, 0:4 * M], T.m[:]), [], ["pool"], "dm", 16)
-    op("y", lambda: g.sync.dma_start(by(T.wq[:]), T.wc[:]), [], ["w0"], "dw", 16)
-    op("y", lambda: g.sync.dma_start(T.wp[:], T.ws[:]), [], ["w"], "dp", 16)
+    for h in (HB, HA):
+        dma("y", T.xin[:, 4 * h[0]:4 * h[1]], T.x[:, 4 * h[0]:4 * h[1]], [], ["xin" + run(h)], "dx" + run(h))
+    dma("s", T.uin[:], T.u[:], [], ["uin"], "du")
+    dma("y", T.pool[:, 0:4 * M], T.m[:], [], ["pool"], "dm")
+    dma("s", T.wp[:], T.ws[:], [], ["w"], "dp")
+    dma("y", by(T.wq[:]), T.wc[:], [], ["w0"], "dw")
 
-    cc, grp, w4, t4 = (T.pf[:, i:i + 1] for i in range(4))
-    weight, lst, key, low, minus, held, c7 = (T.col[:, i:i + 1] for i in range(1, 8))
+    cc, grp2, w4, t4 = (T.pf[:, i:i + 1] for i in range(4))
+    weight, lst, key, low, minus, held, c7 = (T.col[:, i:i + 1] for i in (0, 2, 3, 4, 5, 6, 7))
     iota(T.pi[:, 0:1], [[0, 1]], 0, 1, ["pi"], small=False)
     iota(T.j16[:], [[1, 16]], 0, 0, ["j16"])
-    iota(T.ib[:], [[1, 8], [8, 4], [0, 4]], 0, 0, ["ib"])
+    iota(T.ib[:], [[2, 8], [16, 4], [0, 4]], 0, 0, ["ib"])
     iota(T.idj[:], [[1, 128]], 0, -1, ["idj"])
-    iota(T.ia[:], [[1, 8], [0, 4], [8, 4]], 0, 0, ["ia"])
+    iota(T.ia[:], [[2, 8], [0, 4], [16, 4]], 0, 0, ["ia"])
     iota(T.idt[:], [[1024, M]], -256 * 1024, 0, ["idt"])
-    iota(T.i4[:], [[0, 96], [1, 4]], 0, 0, ["i4"])
+    iota(T.i4[:], [[0, CW // 4], [32000, 4]], 0, 0, ["i4"])
     iota(T.cdi[:], [[1, 2 * CH]], -CH, 0, ["cdi"])
-    iota(T.tab[:], [[4, M + 4 * CH]], 0, 0, ["tab"])
+    iota(T.tab[:, 0:M], [[4, M]], 0, 0, ["tab"])
     for v in range(NV):
         iota(T.val[:, C * v:C * v + C], [[4, C]], 4 * (M + C * v), 0, ["val%d" % v])
 
     op("v", lambda: V.memset(T.ze[:], 0.0), [], ["ze", "zero"])
-    times(T.ft[:, C:672], T.ze[:, 0:672 - C], 0.0, ["zero"], ["ftz"])
+    times(T.ft[:, C:CUT + 512], T.ze[:, 0:CUT + 512 - C], 0.0, ["zero"], ["ftz"])
     ts(T.pj[:, 0:1], T.pi[:, 0:1], 15, None, A.bitwise_and, None, ["pi"], ["pj0"])
-    ts(T.pj[:, 1:2], T.pi[:, 0:1], 4, None, A.arith_shift_right, None, ["pi"], ["pj1"])
+    ts(T.pj[:, 1:2], T.pi[:, 0:1], 3, 14, A.arith_shift_right, A.bitwise_and, ["pi"], ["pj1"])
     ts(T.pj[:, 2:3], T.pi[:, 0:1], 2, 3, A.arith_shift_right, A.bitwise_and, ["pi"], ["pj2"])
     ts(T.pj[:, 3:4], T.pi[:, 0:1], 3, None, A.bitwise_and, None, ["pi"], ["pj3"])
     op("v", lambda: V.tensor_copy(T.pf[:, 0:4], T.pj[:, 0:4]), ["pj0", "pj1", "pj2", "pj3"], ["pf"])
     ts(T.d16[:], T.j16[:], cc, 1.0, A.is_lt, A.add, ["j16", "pf"], ["d16"])
-    op("v", lambda: V.tensor_reduce(T.col[:, 0:1], T.d16[:], AxisListType.X, A.mult), ["d16"], ["col0"])
-    ts(weight, cc, 8.5, T.col[:, 0:1], A.is_lt, A.mult, ["pf", "col0"], ["weight"])
-    line(T.g8[:, 0:4], T.j16[:, 0:4], 8.0, grp, ["j16", "pf"], ["g8"])
-    act(lst, w4, F.Identity, KEEP, UP - 3 * KEEP, ["pf"], ["lst"])
-    act(key, w4, F.Identity, 512 * KEEP, -512.0 - 512 * 3 * KEEP, ["pf"], ["key"])
-    act(low, t4, F.Identity, 1.0, 2 * UP, ["pf"], ["low"])
-    act(c7, t4, F.Identity, 1.0, -3 * KEEP, ["pf"], ["c7"])
-    act(held, w4, F.Identity, KEEP, c7, ["pf", "c7"], ["held"])
-    ts(T.c4[:], T.i4[:], w4, 5 * KEEP, A.is_gt, A.mult, ["i4", "pf"], ["c4"])
-    line(T.c4[:], T.c4[:], 1.0, -4 * KEEP, ["c4"], ["c4"])
-    ts(T.ze[:, 3:512:4], T.idj[:], 0.0, 64.0, A.is_equal, A.mult, ["idj"], ["ze", "zero"])
+    op("v", lambda: V.tensor_reduce(weight, T.d16[:], AxisListType.X, A.mult), ["d16"], ["weight"])
+    ts(T.g8[:, 4:5], cc, 8.5, grp2, A.is_gt, A.add, ["pf"], ["g80"])
+    line(T.g8[:, 0:4], T.j16[:, 0:4], 16.0, T.g8[:, 4:5], ["j16", "g80"], ["g8"])
+    line(lst, w4, KEEP, UP - 3 * KEEP, ["pf"], ["lst"])
+    line(key, w4, 512 * KEEP, -512.0 - 512 * 3 * KEEP, ["pf"], ["key"])
+    line(low, t4, 1.0, 2 * UP, ["pf"], ["low"])
+    line(c7, t4, 1.0, -3 * KEEP, ["pf"], ["c7"])
+    line(held, w4, KEEP, c7, ["pf", "c7"], ["held"])
+    line(T.pe[:, 3:4], w4, 32000.0, 25000.0, ["pf"], ["pe3"])
+    ts(T.c4[:], T.i4[:], T.pe[:, 3:4], KEEP, A.subtract, A.min, ["i4", "pe3"], ["c4"])
+    ts(T.ze[:, 3:512:4], T.idj[:], 0.0, 64.0, A.is_equal, A.mult, ["idj", "ze"], ["ze", "zero"])
     line(T.spare[:, 4:5], cc, -4.0, -float(M), ["pf"], ["sp4"])
     line(T.spare[:, 0:4], T.j16[:, 0:4], -64.0, T.spare[:, 4:5], ["j16", "sp4"], ["spare"])
     times(minus, weight, -1.0, ["weight"], ["minus"])
-    for tile, src, name in ((T.wb, T.ib, "b"), (T.wa, T.ia, "a")):
-        parts = ["w%s%d" % (name, t) for t in range(4)]
-        for t in range(4):
-            act(tile[:, t:512:4], src[:], F.Abs, -1.0, T.g8[:, t:t + 1], ["i" + name, "g8"], [parts[t]])
-        act(tile[:], tile[:], F.Relu, minus, weight, parts + ["minus", "weight"], parts)
+    WA, WB = ["wa%d" % t for t in range(4)], ["wb%d" % t for t in range(4)]
+    for t in range(4):
+        ts(T.wb[:, t:512:4], T.ib[:], T.g8[:, t:t + 1], weight, A.is_equal, A.mult, ["ib", "g8", "weight"], [WB[t]])
+    for t in range(4):
+        act(T.wa[:, t:512:4], T.ia[:], F.Abs, -1.0, T.g8[:, t:t + 1], ["ia", "g8"], [WA[t]])
+    act(T.wa[:], T.wa[:], F.Relu, minus, weight, WA + ["minus", "weight"], WA)
     for b in range(4):
         quant(T.eq[:, 128 * b:128 * b + 128], T.ep[:, 128 * b:128 * b + 128], T.ze[:, 3 - b:515 - b], ["ze"], ["e%d" % b])
-    quant(T.aq[:, 128:256], T.ap[:, 128:256], T.wb[:], ["wb%d" % t for t in range(4)], ["qwb"])
-    quant(T.aq[:, 0:128], T.ap[:, 0:128], T.wa[:], ["wa%d" % t for t in range(4)], ["qwa"])
+    quant(T.aq[:, 128:256], T.ap[:, 128:256], T.wb[:], WB, ["qwb"])
+    quant(T.aq[:, 0:128], T.ap[:, 0:128], T.wa[:], WA, ["qwa"])
     quant(T.uq[:], T.up[:], T.uin[:], ["uin"], ["uq"])
     act(T.cdi[:], T.cdi[:], F.Abs, -1.0, cc, ["cdi", "pf"], ["cdi"])
     act(T.cdi[:], T.cdi[:], F.Relu, -1.0, 1.0, ["cdi"], ["cdi"])
     for r in range(R):
         a = CH - 16 * r
-        act(T.cd[:, O[r]:O[r + 1]], T.cdi[:, a:a + O[r + 1] - O[r]], F.Identity, T.spare[:, r:r + 1], 0.0,
-            ["cdi", "spare"], ["cdp%d" % r])
-        act(T.cd[:, O[r]:O[r + 1]:16 * (r + 1)], T.j16[:, 0:2], F.Identity, 256.0 - 4096.0, 4096.0, ["j16"], ["cdp%d" % r])
-    act(T.pe[:, 0:1], t4, F.Identity, 8.0, 26.0, ["pf"], ["pe0"])
-    act(T.pe[:, 1:2], T.pe[:, 0:1], F.Identity, t4, 16.0, ["pf", "pe0"], ["pe1"])
-    act(T.pe[:, 2:3], w4, F.Identity, float(PER), T.pe[:, 1:2], ["pf", "pe1"], ["pe2"])
-    ts(T.pos[:, 0:1], T.pe[:, 2:3], 2 * PER - 1.0, None, A.min, None, ["pe2"], ["posa"])
-    ts(T.pos[:, 2:3], T.pe[:, 2:3], NE - 2 * PER - 1.0, None, A.min, None, ["pe2"], ["posb"])
+        times(T.cd[:, O[r]:O[r + 1]], T.cdi[:, a:a + O[r + 1] - O[r]], T.spare[:, r:r + 1], ["cdi", "spare"], ["cdp%d" % r])
+        line(T.cd[:, O[r]:O[r + 1]:16 * (r + 1)], T.j16[:, 0:2], 256.0 - 4096.0, 4096.0, ["j16"], ["cdp%d" % r])
+    line(T.pe[:, 0:1], t4, 8.0, 26.0, ["pf"], ["pe0"])
+    line(T.pe[:, 1:2], T.pe[:, 0:1], t4, 16.0, ["pf", "pe0"], ["pe1"])
+    line(T.pe[:, 2:3], w4, float(PER), T.pe[:, 1:2], ["pf", "pe1"], ["pe2"])
+    for c, s in (("a", 0), ("b", 2)):
+        ts(T.pos[:, s:s + 1], T.pe[:, 2:3], NE[c] - 1.0, None, A.min, None, ["pe2"], ["pos" + c])
     CD, have = ["cdp%d" % r for r in range(R)], PER
-    while have < NE - 2 * PER:
-        w = min(have, NE - 2 * PER - have)
+    while have < NX:
+        w = min(have, NX - have)
         copy(T.cd[:, have:have + w], T.cd[:, 0:w], list(CD), ["cd%d" % (len(CD) + 1)])
         CD.append("cd%d" % (len(CD) + 1))
         have += w
-    for r in range(R):
-        z = len(range(O[r + 1] - 1, NE, PER))
-        act(T.ne[:, O[r + 1] - 1:NE:PER], T.j16[:, 0:z], F.Identity, 0.0, 1024.0, ["j16"], ["nez%d" % r])
+    for c in "ab":
+        for r in range(R):
+            z = len(range(O[r + 1] - 1, NE[c], PER))
+            line(T["ne" + c][:, O[r + 1] - 1:NE[c]:PER], T.j16[:, 0:z], 0.0, 1024.0, ["j16"], ["nez%d%s" % (r, c)])
 
-    def a_mm(q, p, res, bk, h):
-        mm(bk, h[1] - h[0], T.uq[:], T.up[:], q[:, h[0]:h[1]], p[:, h[0]:h[1]], True, True, ["uq", res])
+    def signs(q, p, res, bk, h):
+        c, w = run(h), h[1] - h[0]
+        o = 128 * (c == "b")
+        mm(bk, w, T.uq[:], T.up[:], q[:, h[0]:h[1]], p[:, h[0]:h[1]], True, True, ["uq", res])
+        buf, z = bank(bk)
+        act(T.ft[:, h[0]:h[1]], buf[:, z:z + w], F.Sign, 2.0 ** 50, -2.0 ** -100, [bk], ["ft" + c])
+        quant(T.fq[:, o:o + 128], T.fp[:, o:o + 128], T.ft[:, h[0]:h[0] + 512],
+              ["ftb", "ftz"] + ["fta"] * (c == "a"), ["fq" + c])
 
-    def bits(bk, h):
-        buf, o = bank(bk)
-        act(T.ft[:, h[0]:h[1]], buf[:, o:o + h[1] - h[0]], F.Sign, 2.0 ** 50, -2.0 ** -100, [bk], ["ft" + c for c in runs(h)])
-
-    def q_bits():
-        quant(T.fq[:, 128:256], T.fp[:, 128:256], T.ft[:, 0:512], ["fta", "ftb", "ftz"], ["fq"])
-
-    def q_bits_b():
-        quant(T.fq[:, 272:400], T.fp[:, 272:400], T.ft[:, CUT:CUT + 512], ["ftb", "ftz"], ["fqb"])
-
-    def list_mm(bk, which, o=128, res="fq"):
-        w = 128 * which
+    def list_mm(bk, which, h):
+        w, o = 128 * which, 128 * (h == HB)
         mm(bk, 128, T.aq[:, w:w + 128], T.ap[:, w:w + 128], T.fq[:, o:o + 128], T.fp[:, o:o + 128], True, True,
-           [res, "qwb" if which else "qwa"])
+           ["fq" + run(h), "qwb" if which else "qwa"])
 
-    def list_scan(bk, h):
+    def list_scan(bk, h, out, res):
         buf, o = bank(bk)
-        w = (h[1] - h[0]) // 4
+        w, c, (s, k) = (h[1] - h[0]) // 4, run(h), cols(h)
         op("v", lambda: V.tensor_tensor_scan(T.sca[:, h[0] // 4:h[1] // 4], T.c4[:, 0:w], buf[:, o:o + w], 0.0,
-                                             A.add, A.max), [bk, "c4"], ["sca" + c for c in runs(h)])
+                                             A.add, A.max), [bk, "c4"], ["sca" + c])
+        ts(out[:, s:s + k], T.sca[:, h[0] // 4 + 3:h[1] // 4:4], lst, 0.5, A.add, A.mult, ["sca" + c, "lst"], [res + c])
 
-    def list_out(v, h):
-        a, b, c = h[0] // 16, h[1] // 16, runs(h)
-        ts(T["ao%d" % v][:, a:b], T.sca[:, h[0] // 4 + 3:h[1] // 4:4], lst, 0.5, A.add, A.mult, ["sca" + c, "lst"],
-           ["ao%d%s" % (v, c)])
-        send(nxt, T["la%d" % v][:, a:b], T["ao%d" % v][:, a:b], "l%s%d" % (c, v), ["ao%d%s" % (v, c)], ["la%d%s" % (v, c)])
+    def keys(v, h):
+        line(T["af%d" % v][:, h[0] // 16:h[1] // 16], T.sca[:, h[0] // 4 + 3:h[1] // 4:4], 512.0, key,
+             ["sca" + run(h), "key"], ["af%d%s" % (v, run(h))])
+
+    def early(v, h): return v > 0 and h == HB
 
     def slots(v, h):
-        c = runs(h)
-        k0, k1 = h[0] // 16, h[1] // 16
-        z0, z1 = (0, 2 * PER) if c == "a" else (2 * PER, NE)
-        la, ar, af = T["la%d" % v], T["ar%d" % v], T["af%d" % v]
-        gather(ar[:, h[0]:h[1]], T.idt[:], la[:, k0:k1], ["idt", "la%d%s" % (v, c)], ["ar%d%s" % (v, c)])
-        if v:
-            ts(af[:, k0:k1], la[:, k0:k1], 1024.0, -256.0 * 1024, A.mult, A.add, ["la%d%s" % (v, c)], ["af%d%s" % (v, c)])
-        for k in range(k0, k1):
-            c0, w, z = CH * (k // R), 16 * (k % R + 1), PER * (k // R) + O[k % R]
-            o, i, s = T.ne[:, z:z + w], ar[:, c0:c0 + w], af[:, k:k + 1]
-            either(lambda o=o, i=i, s=s: V.tensor_scalar(o, i, s, 1024.0, A.not_equal, A.mult),
-                   lambda o=o, i=i, s=s: S.activation(o, i, F.Abs, scale=-1.0, bias=s),
-                   ["ar%d%s" % (v, c), "af%d%s" % (v, c)], ["ne_%d" % k])
+        c, (k0, kn) = run(h), cols(h)
+        ln = "ao" if early(v, h) else "la"
+        la, ar, af, ne, scd = T[ln + str(v)][:, k0:k0 + kn], T["ar%d" % v], T["af%d" % v], T["ne" + c], T["scd" + c]
+        vc = "%d%s" % (v, c)
+        gather(ar[:, h[0]:h[1]], T.idt[:], la, ["idt", ln + vc], ["ar" + vc])
+        if v and not early(v, h):
+            ts(af[:, k0:k0 + kn], la, 1024.0, -256.0 * 1024, A.mult, A.add, ["la" + vc], ["af" + vc])
+        for k in range(kn):
+            c0, w, z = h[0] + CH * (k // R), 16 * (k % R + 1), PER * (k // R) + O[k % R]
+            o, i, x = ne[:, z:z + w], ar[:, c0:c0 + w], af[:, k0 + k:k0 + k + 1]
+            either(lambda o=o, i=i, x=x: V.tensor_scalar(o, i, x, 1024.0, A.not_equal, A.mult),
+                   lambda o=o, i=i, x=x: S.activation(o, i, F.Abs, scale=-1.0, bias=x),
+                   ["ar" + vc, "af" + vc], ["ne%s_%d" % (c, k)])
         for r in range(R):
-            times(T.ne[:, z0 + O[r + 1] - 2:z1:PER], af[:, k0 + r:k1:R], -1.0 / 1024.0, ["af%d%s" % (v, c)],
-                  ["neo%d%s" % (r, c)])
-        op("v", lambda: V.tensor_tensor_scan(T.scd[:, z0:z1], T.cd[:, 0:z1 - z0], T.ne[:, z0:z1], 0.0, A.add, A.min),
-           CD + ["neo%d%s" % (r, c) for r in range(R)] + ["nez%d" % r for r in range(R)]
-           + ["ne_%d" % k for k in range(k0, k1)], ["scd" + c])
-        s = 0 if c == "a" else 16
-        ts(T["so%d" % v][:, s:s + 16], T.scd[:, z0:z1].indirect(T.pos[:, s // 8:s // 8 + 1]), -1.0, 256.0, A.mult, A.add,
-           ["scd" + c, "pos" + c], ["so%d%s" % (v, c)])
+            times(ne[:, O[r + 1] - 2:NE[c]:PER], af[:, k0 + r:k0 + kn:R], -1.0 / 1024.0, ["af" + vc], ["neo%d%s" % (r, c)])
+        op("v", lambda: V.tensor_tensor_scan(scd[:], T.cd[:, 0:NE[c]], ne[:], 0.0, A.add, A.min),
+           CD + ["ne%s%d%s" % (x, r, c) for r in range(R) for x in "oz"] + ["ne%s_%d" % (c, k) for k in range(kn)], ["scd" + c])
+        s = 16 * (c == "b")
+        ts(T["so%d" % v][:, s:s + 16], scd[:].indirect(T.pos[:, s // 8:s // 8 + 1]), -1.0, 256.0, A.mult, A.add,
+           ["scd" + c, "pos" + c], ["so" + vc])
 
-    def scatter(v):
-        for a in reversed(range(0, K16, R)):
-            b, s = min(a + R, K16), 8 * (a >= 8)
-            op("v", lambda a=a, b=b, s=s: V.tensor_copy(T.tab[:].indirect(T["so%d" % v][:, a + s:b + s]),
-                                                        T.val[:, C * v + 16 * a:C * v + 16 * b]),
-               ["so%d%s" % (v, "ab"[a >= 8]), "val%d" % v], ["tab"])
+    def scatter(v, h):
+        s, kn = 16 * (h == HB), cols(h)[1]
+        sn = ("sl" if early(v, h) else "so") + str(v)
+        for a in reversed(range(0, kn, R)):
+            b, j = min(a + R, kn), C * v + h[0]
+            op("v", lambda a=a, b=b, j=j: V.tensor_copy(T.tab[:].indirect(T[sn][:, s + a:s + b]),
+                                                        T.val[:, j + 16 * a:j + 16 * b]),
+               [sn + run(h), "val%d" % v], ["tab"])
 
     def pool_names(v):
         return ["pool"] + ["n%d%d%s" % (t, b, c) for t in range(v) for b in range(4) for c in "ab"]
 
     def gather(out, win, off, reads, writes): copy(out, win.indirect(off), reads, writes)
 
-    def pick(src, res, off, out, a, b):
+    def pick(src, res, off, out, a, b, names):
         op("v", lambda: V.tensor_tensor_scan(T.scp[:, a:b], T.c4[:, 0:b - a], src[:, a:b], 0.0, A.add, A.max),
-           [res, "c4"], ["scp%d" % min(a, 1)])
-        ts(off[:, a // 4:b // 4], T.scp[:, a + 3:b:4], held, None, A.add, None, ["scp%d" % min(a, 1), "held"], [out])
+           [res, "c4"], names)
+        ts(off[:, a // 4:b // 4], T.scp[:, a + 3:b:4], held, None, A.add, None, names + ["held"], [out])
 
     def pointers(v, h):
-        c = runs(h)
-        gather(T.prow[:, h[0]:h[1]], T.tab[:, 0:M], T["la%d" % v][:, h[0] // 16:h[1] // 16], ["tab", "la%d%s" % (v, c)],
-               ["prow" + c])
-        pick(T.prow, "prow" + c, T.boff, "boff" + c, h[0], h[1])
+        for z, a, b in ((("b0", CUT, CUT + HALF), ("b1", CUT + HALF, C)) if h == HB else (("a", 0, CUT),)):
+            gather(T.prow[:, a:b], T.tab[:, 0:M], T["la%d" % v][:, a // 16:b // 16], ["tab", "la%d%s" % (v, run(h))],
+                   ["prow" + z])
+            pick(T.prow, "prow" + z, T.boff, "boff" + z, a, b, ["scp" + z])
 
     def read_map(v, h):
-        win, c, mid = T.pool[:, 0:4 * (M + C * v)], runs(h), (h[0] + h[1]) // 2
+        win, c = T.pool[:, 0:4 * (M + C * v)], run(h)
+        mid = h[0] + HALF if v or c == "a" else (h[0] + h[1]) // 2
         for i, (a, b) in enumerate(((h[0], mid), (mid, h[1]))):
-            gather(T.bt[:, 4 * a:4 * b], win, T.boff[:, a // 4:b // 4], pool_names(v) + ["boff" + c], ["bt%s%d" % (c, i)])
+            gather(T.bt[:, 4 * a:4 * b], win, T.boff[:, a // 4:b // 4],
+                   pool_names(v) + (["boffa"] if c == "a" else ["boffb%d" % i] if v else ["boffb0", "boffb1"]),
+                   ["bt%s%d" % (c, i)])
         quant(T.bq[:, h[0]:h[1]], T.bp[:, h[0]:h[1]], T.bt[:, 4 * h[0]:4 * h[1]], ["bt%s0" % c, "bt%s1" % c], ["bq" + c])
 
-    def r_mm(v, x, h, first=True):
-        for b in range(4):
-            mm("@%s%d" % (x, b), h[1] - h[0], T.wq[:, 128 * b:128 * b + 128], T.wp[:, 128 * b:128 * b + 128],
-               T["sq%d" % v][:, h[0]:h[1]], T["sp%d" % v][:, h[0]:h[1]], first, not first,
-               ["w0", "w", "p%d" % v, "s%d%s" % (v, runs(h))] if v else ["w0", "w", "s0"])
-
     def new_state(v, x, h):
-        c = runs(h)
+        c = run(h)
         for b in range(4):
-            mm("@%s%d" % (x, b), h[1] - h[0], T.eq[:, 128 * b:128 * b + 128], T.ep[:, 128 * b:128 * b + 128],
-               T.bq[:, h[0]:h[1]], T.bp[:, h[0]:h[1]], v == 0, v != 0, ["e%d" % b, "bq" + c])
-        if v == 0:
-            r_mm(0, x, h, False)
-        for b in range(4):
-            unload("@%s%d" % (x, b), T.yt, 0, b, h, ["yt%s%d" % (c, b)])
+            bk = "@%s%d" % (x, b)
+            mm(bk, h[1] - h[0], T.wq[:, 128 * b:128 * b + 128], T.wp[:, 128 * b:128 * b + 128],
+               T["sq%d" % v][:, h[0]:h[1]], T["sp%d" % v][:, h[0]:h[1]], True, False,
+               ["w0", "w", "s%d%s" % (v, c)] + ["p%d" % v] * (v > 0))
+            mm(bk, h[1] - h[0], T.eq[:, 128 * b:128 * b + 128], T.ep[:, 128 * b:128 * b + 128],
+               T.bq[:, h[0]:h[1]], T.bp[:, h[0]:h[1]], False, True, ["e%d" % b, "bq" + c])
+            unload(bk, T.yt, 0, b, h, ["yt%s%d" % (c, b)])
         quant(T["yq%d" % v][:, h[0]:h[1]], T["yp%d" % v][:, h[0]:h[1]], T.yt[:, 4 * h[0]:4 * h[1]],
               ["yt%s%d" % (c, b) for b in range(4)], ["y%d%s" % (v, c)])
 
@@ -319,22 +322,12 @@ def rank_program(g, core, T, topo):
 
     def to_pool(v, b, bk, h):
         mm(bk, h[1] - h[0], T.eq[:, 128 * b:128 * b + 128], T.ep[:, 128 * b:128 * b + 128],
-           T["yq%d" % v][:, h[0]:h[1]], T["yp%d" % v][:, h[0]:h[1]], True, True,
-           ["e%d" % b] + ["y%d%s" % (v, c) for c in runs(h)])
-        unload(bk, T.pool, 4 * (M + C * v), b, h, ["n%d%d%s" % (v, b, c) for c in runs(h)])
-
-    def pass_codes(v, dst, q, h):
-        send(dst, by(q[:, h[0]:h[1]]), by(T["yq%d" % v][:, h[0]:h[1]]), "s%s%d" % (runs(h)[0], v + 1),
-             ["y%d%s" % (v, c) for c in runs(h)], ["s%d%s" % (v + 1, c) for c in runs(h)])
-
-    def pass_scales(v, dst, p):
-        send(dst, p[:, 0:C], T["yp%d" % v][:], "pa%d" % (v + 1), ["y%da" % v, "y%db" % v], ["p%d" % (v + 1)])
+           T["yq%d" % v][:, h[0]:h[1]], T["yp%d" % v][:, h[0]:h[1]], True, True, ["e%d" % b, "y%d%s" % (v, run(h))])
+        unload(bk, T.pool, 4 * (M + C * v), b, h, ["n%d%d%s" % (v, b, run(h))])
 
     def visit(v):
-        w = v + 1
+        w, yq, both = v + 1, T["yq%d" % v], ["y%da" % v, "y%db" % v]
         if v:
-            r_mm(v, "n", HB)
-            r_mm(v, "y", HA)
             pointers(v, HB)
             pointers(v, HA)
         read_map(v, HB)
@@ -342,64 +335,65 @@ def rank_program(g, core, T, topo):
         new_state(v, "n", HB)
         new_state(v, "y", HA)
         if w < NV:
-            pass_codes(v, nxt, T["sq%d" % w], HB)
-            pass_codes(v, nxt, T["sq%d" % w], HA)
-            pass_scales(v, nxt, T["sp%d" % w])
-            a_mm(T["yq%d" % v], T["yp%d" % v], "y%db" % v, "@n0", HB)
-            bits("@n0", HB)
-            q_bits_b()
-            list_mm("@n1", 0, 272, "fqb")
-            list_scan("@n1", HB)
-            list_out(w, HB)
-            a_mm(T["yq%d" % v], T["yp%d" % v], "y%da" % v, "@y0", HA)
-            bits("@y0", HA)
-            q_bits()
-            list_mm("@y1", 0)
-            list_scan("@y1", HA)
-            list_out(w, HA)
+            for h in (HB, HA):
+                c = run(h)
+                send(nxt, by(T["sq%d" % w][:, h[0]:h[1]]), by(yq[:, h[0]:h[1]]), "s%s%d" % (c, w),
+                     ["y%d%s" % (v, c)], ["s%d%s" % (w, c)])
+            send(nxt, T["sp%d" % w][:], T["yp%d" % v][:], "pa%d" % w, both, ["p%d" % w])
+            for h, x in ((HB, "n"), (HA, "y")):
+                c, (s, k) = run(h), cols(h)
+                signs(yq, T["yp%d" % v], "y%d%s" % (v, c), "@%s0" % x, h)
+                list_mm("@%s1" % x, 0, h)
+                list_scan("@%s1" % x, h, T["ao%d" % w], "ao%d" % w)
+                if early(w, h):
+                    keys(w, h)
+                send(nxt, T["la%d" % w][:, s:s + k], T["ao%d" % w][:, s:s + k], "l%s%d" % (c, w), ["ao%d%s" % (w, c)],
+                     ["la%d%s" % (w, c)])
+        else:
+            send(home, by(T.oq[:, 0:C]), by(yq[:]), "sa%d" % w, both, ["s3"])
+            send(home, T.op[:, 0:C], T["yp%d" % v][:], "pa%d" % w, both, ["p3"])
+        for h, x in ((HB, "n"), (HA, "y")):
             for b in range(4):
-                to_pool(v, b, "@n%d" % ((b + 2) % 4), ALL)
-        slots(v, HB)
-        slots(v, HA)
-        scatter(v)
+                to_pool(v, b, "@%s%d" % (x, (b + 2) % 4), h)
+        for h in (HB, HA):
+            if not early(v, h):
+                slots(v, h)
+            scatter(v, h)
+        if w < NV:
+            slots(w, HB)
+            send(nxt, T["sl%d" % w][:, 16:32], T["so%d" % w][:, 16:32], "sl%d" % w, ["so%db" % w], ["sl%db" % w])
 
-    quant(T.sq0[:], T.sp0[:], T.xin[:], ["xin"], ["s0"])
-    a_mm(T.sq0, T.sp0, "s0", "@y0", ALL)
-    bits("@y0", ALL)
-    q_bits()
-    list_mm("@y1", 1)
-    list_mm("@y2", 0)
-    ts(T.boff[:], T.py[:, 512:584], 2.0, low, A.mult, A.add, ["@y1", "low"], ["boffa", "boffb"])
-    list_scan("@y2", ALL)
-    ts(T.la0[:], T.sca[:, 3:72:4], lst, 0.5, A.add, A.mult, ["scaa", "scab", "lst"], ["la0a", "la0b"])
-    line(T.af0[:], T.sca[:, 3:72:4], 512.0, key, ["scaa", "scab", "key"], ["af0a", "af0b"])
+    for h, x in ((HB, "n"), (HA, "y")):
+        c = run(h)
+        quant(T.sq0[:, h[0]:h[1]], T.sp0[:, h[0]:h[1]], T.xin[:, 4 * h[0]:4 * h[1]], ["xin" + c], ["s0" + c])
+        signs(T.sq0, T.sp0, "s0" + c, "@%s0" % x, h)
+        list_mm("@%s1" % x, 1, h)
+        list_mm("@%s2" % x, 0, h)
+        buf, o = bank("@%s1" % x)
+        ts(T.boff[:, h[0] // 4:h[1] // 4], buf[:, o:o + (h[1] - h[0]) // 4], 2.0, low, A.mult, A.add,
+           ["@%s1" % x, "low"], ["boffa"] if c == "a" else ["boffb0", "boffb1"])
+        list_scan("@%s2" % x, h, T.la0, "la0")
+        keys(0, h)
     for v in range(NV):
         visit(v)
-    pass_codes(2, home, T.oq, ALL)
-    pass_scales(2, home, T.op)
-    for b in range(4):
-        to_pool(2, b, "@n%d" % b, HB)
-    for b in range(4):
-        to_pool(2, b, "@y%d" % b, HA)
 
-    S3 = ["s3a", "s3b", "p3"]
-    pick(T.tab, "tab", T.moff, "moffa", 0, 128)
-    pick(T.tab, "tab", T.moff, "moffb", 128, M)
+    def over(cuts, a, b): return [x for x, y in zip(cuts, cuts[1:]) if x < b and y > a]
+
+    for a, b in zip(PK, PK[1:]):
+        pick(T.tab, "tab", T.moff, "moff%d" % a, a, b, ["scpa"] if a < CUT else ["scpb0", "scpb1"])
     for a, b in zip(FIN, FIN[1:]):
         gather(T.mt[:, 4 * a:4 * b], T.pool[:], T.moff[:, a // 4:b // 4],
-               pool_names(NV) + ["moffa" if a < 128 else "moffb"], ["mt%d" % a])
-    mm("@n0", C, T.wq[:, 0:128], T.wp[:, 0:128], T.oq[:, 0:C], T.op[:, 0:C], True, True, ["w0", "w"] + S3)
+               pool_names(NV) + ["moff%d" % x for x in over(PK, a, b)], ["mt%d" % a])
+    mm("@n0", C, T.wq[:, 0:128], T.wp[:, 0:128], T.oq[:, 0:C], T.op[:, 0:C], True, True, ["w0", "w", "s3", "p3"])
     copy(T.yo[:], T.pn[:, 0:C], ["@n0"], ["yo"])
-
-    def store(q, out, in_, reads):
-        op(q, lambda: (g.sync if q == "y" else S).dma_start(out, in_), reads, [], "out", 16)
-
     for a, b in zip(ST, ST[1:]):
-        quant(T.oq[:, C + a:C + b], T.op[:, C + a:C + b], T.mt[:, 4 * a:4 * b],
-              ["mt%d" % x for x, y in zip(FIN, FIN[1:]) if x < b and y > a], ["o%d" % a])
-        store("y", T.oc[:, 4 * (C + a):4 * (C + b)], by(T.oq[:, C + a:C + b]), ["o%d" % a])
-    store("y", T.oc[:, 0:4 * C], by(T.oq[:, 0:C]), ["s3a", "s3b"])
-    store("s", T.y[:], T.yo[:], ["yo"])
+        quant(T.oq[:, C + a:C + b], T.op[:, C + a:C + b], T.mt[:, 4 * a:4 * b], ["mt%d" % x for x in over(FIN, a, b)],
+              ["o%d" % a])
+    dma("y", T.oc[:, 0:4 * C], by(T.oq[:, 0:C]), ["s3"], [], "out")
+    for a, b in zip(ST, ST[1:]):
+        dma("y", T.oc[:, 4 * (C + a):4 * (C + b)], by(T.oq[:, C + a:C + b]), ["o%d" % a], [], "out")
+    dma("s", T.y[:], T.yo[:], ["yo"], [], "out")
     for k in range(4):
-        store("ys"[k % 2], T.osc[4 * k:4 * k + 4, :], T.op[32 * k:32 * k + 4, :], ["o%d" % a for a in ST[:-1]] + S3)
+        dma("ys"[k % 2], T.osc[4 * k:4 * k + 4, :], T.op[32 * k:32 * k + 4, :], ["o%d" % a for a in ST[:-1]] + ["p3"],
+            [], "out")
     _emit(g, T, arrivals, ops)

from concourse.mybir import dt, AluOpType, AxisListType, ActivationFunctionType

C, M, NV = 288, 512, 3
K16 = C // 16
POOL = M + NV * C
KEEP = 6144.0
UP = 511.0
R, CUT, HALF = 4, 128, 64
CH = 16 * R
PK, FIN, ST = (0, 128, 320, M), (0, 128, 256, 320, 384, M), (0, 128, 256, M)
O = [8 * _r * _r + 10 * _r for _r in range(R + 1)]
PER = O[R]
HA, HB = (0, CUT), (CUT, C)
NE = {_c: PER * (_k // R) + O[_k % R] for _c, _k in (("a", CUT // 16), ("b", (C - CUT) // 16))}
NX, CW = NE["b"], 192
Q4, U8, BF, F32, I32, U16 = "float8_e4m3fn_x4", "uint8", "bfloat16", "float32", "int32", "uint16"
SCRATCH = {"py": ("psum", [128, 2048], F32), "pn": ("psum", [128, 2048], F32)}
for _n, _w, _d in (
        ("xin", 4 * C, BF), ("uin", 512, BF), ("pool", 4 * POOL, BF), ("wq", 512, Q4), ("wp", 512, U8),
        ("uq", 128, Q4), ("up", 128, U8), ("oq", C + M, Q4), ("op", C + M, U8), ("bt", 4 * C, BF), ("bq", C, Q4),
        ("bp", C, U8), ("yt", 4 * C, BF), ("mt", 4 * M, BF), ("yo", C, F32), ("ft", CUT + 512, BF), ("fq", 256, Q4),
        ("fp", 256, U8), ("ze", 528, BF), ("wa", 512, BF), ("wb", 512, BF), ("eq", 512, Q4),
        ("ep", 512, U8), ("aq", 256, Q4), ("ap", 256, U8), ("pi", 8, I32),
        ("pj", 8, I32), ("pf", 8, F32), ("j16", 16, F32), ("spare", 8, F32), ("d16", 16, F32),
        ("col", 8, F32), ("g8", 8, F32), ("ia", 128, BF), ("ib", 128, BF), ("idj", 128, BF), ("idt", M, BF),
        ("i4", CW, BF), ("c4", CW, BF), ("cdi", 2 * CH, BF), ("cd", NX, BF), ("tab", M + 4 * CH, F32),
        ("val", NV * C, F32), ("sca", 72, F32), ("prow", C, F32), ("scp", M, F32), ("boff", 72, U16),
        ("moff", 128, U16), ("pos", 4, U16), ("pe", 4, F32), ("nea", NE["a"], BF), ("neb", NE["b"], BF),
        ("scda", NE["a"], BF), ("scdb", NE["b"], BF)):
    SCRATCH[_n] = ("sbuf", [128, _w], _d)
for _t in range(NV):
    for _n, _w, _d in (("sq", C, Q4), ("sp", C, U8), ("yq", C, Q4), ("yp", C, U8), ("af", K16, F32),
                       ("ar", C, BF), ("so", 32, U16), ("ao", 32, U16), ("la", 32, U16), ("sl", 32, U16)):
        SCRATCH[_n + str(_t)] = ("sbuf", [128, _w], _d)
SEMAPHORES = ["cv", "cs", "ct", "cg", "sent", "dxa", "dxb", "du", "dm", "dw", "dp", "out"] + [
    _a + _b for _a in ("sa", "sb", "pa", "la", "lb", "sl") for _b in "123"]
COUNTER = {"v": "cv", "s": "cs", "t": "ct", "g": "cg"}

ORDER = [2,0,6,18,21,1,23,22,3,7,80,19,13,73,20,24,37,4,25,27,10,38,34,56,74,26,66,8,28,5,44,57,55,45,81,82,43,46,31,47,83,62,41,91,30,9,42,92,40,58,39,64,79,36,93,63,53,12,48,84,85,51,60,59,67,11,65,77,94,49,32,87,76,78,35,54,95,16,97,29,86,110,102,61,96,88,120,101,116,15,107,50,103,113,105,108,104,111,89,98,90,114,100,112,115,52,167,117,126,177,181,123,109,180,129,172,106,118,124,71,173,169,119,130,176,178,127,174,179,171,168,121,68,72,170,175,70,125,136,131,151,128,122,182,199,137,153,99,196,14,132,75,183,133,187,138,198,184,195,188,144,194,145,159,197,193,191,155,69,189,185,190,139,140,146,141,163,161,192,143,142,157,160,154,147,204,205,215,200,186,148,164,201,217,149,202,206,218,152,165,162,216,135,208,150,214,209,33,203,213,210,166,207,211,212,225,219,222,134,223,246,226,158,220,156,224,227,240,228,231,237,232,300,256,229,301,230,250,243,311,17,259,234,221,253,313,233,247,235,310,305,302,241,312,307,238,248,236,244,242,251,257,260,245,297,239,249,254,261,306,266,252,258,298,281,255,262,267,274,303,268,269,304,275,285,299,276,291,308,309,282,286,270,289,314,293,272,277,271,329,318,327,264,323,315,283,332,265,278,331,320,326,321,319,330,328,324,273,279,316,295,325,322,287,317,280,284,290,333,263,334,351,294,288,339,292,336,296,340,399,360,367,342,411,408,364,410,337,341,335,357,373,409,398,343,338,406,407,344,345,354,395,346,349,348,347,401,370,400,361,402,358,405,403,396,350,404,362,352,359,355,412,397,365,371,413,353,356,374,363,368,366,385,414,372,375,369,381,376,386,377,415,379,382,383,378,384,380,418,389,391,416,390,432,387,392,419,393,417,420,388,394,424,423,421,426,422,430,427,425,434,428,429,431,436,433,435,438,440,439,437]
ON_V = {28,34,37,58,64,71,72,102,109,118,128,167,170,171,173,189,206,207,208,211,218,225,231,235,245,261,296,302,305,311,312,322,325,330,331,339,345,380,398,403,406,407,422,424,425}


def _emit(g, T, arrivals, ops):
    queue = {"v": g.vector, "s": g.scalar, "t": g.tensor, "g": g, "y": g.sync}
    known = {q: {} for q in queue}
    total, waited = {}, {}
    writer, readers = {}, {}
    for sem, count, writes in arrivals:
        total[sem] = count
        for r in writes:
            writer[r] = ("g", sem, count, {sem: count})
    assert sorted(ORDER) == list(range(len(ops)))
    for i in ORDER:
        fns, reads, writes, sem, inc = ops[i]
        q = ("v" if i in ON_V else "s") if len(fns) > 1 else list(fns)[0]
        need = [writer[r] for r in list(reads) + list(writes) if r in writer]
        for r in writes:
            need += readers.get(r, [])
        for r in reads:
            if r[0] == "@":
                need += [e for e in readers.get(r, []) if e[0] != q]
        for eq, esem, count, clock in sorted(need, key=lambda e: -e[2]):
            if (eq == q == "t") or known[q].get(esem, 0) >= count:
                continue
            queue[q].wait_ge(T.sem[esem], count)
            waited[esem] = max(waited.get(esem, 0), count)
            for s, v in clock.items():
                known[q][s] = max(known[q].get(s, 0), v)
        if sem is None:
            sem, inc = COUNTER[q], 1
        total[sem] = total.get(sem, 0) + inc
        clock = dict(known[q])
        clock[sem] = total[sem]
        ins = fns[q]()
        if sem != "sent":
            ins.then_inc(T.sem[sem], inc)
        ev = (q, sem, total[sem], clock)
        for r in reads:
            readers.setdefault(r, []).append(ev)
        for r in writes:
            writer[r] = ev
            readers[r] = []
    for s in total:
        if waited.get(s, 0) < total[s]:
            queue["y" if s == "out" else "g"].wait_ge(T.sem[s], total[s])


def rank_program(g, core, T, topo):
    rank = T.rank_of(core)
    if rank is None:
        return
    n = len(T.cores)
    nxt, home = T.cores[(rank + 1) % n], T.cores[(rank - (NV - 1)) % n]
    V, S, P = g.vector, g.scalar, g.tensor
    A, F = AluOpType, ActivationFunctionType
    ops, arrivals = [], []

    def op(q, fn, reads, writes, sem=None, inc=None): ops.append(({q: fn}, reads, writes, sem, inc))
    def either(fv, fs, reads, writes): ops.append(({"v": fv, "s": fs}, reads, writes, None, None))
    def by(view): return view.bitcast(dt.uint8)
    def bank(name): return T["p" + name[1]], 512 * int(name[2])
    def run(h): return "a" if h == HA else "b"
    def cols(h): return h[0] // 16, (h[1] - h[0]) // 16

    def ts(out, in0, s1, s2, op0, op1, reads, writes):
        if op1 is None:
            op("v", lambda: V.tensor_scalar(out, in0, s1, None, op0), reads, writes)
        else:
            op("v", lambda: V.tensor_scalar(out, in0, s1, s2, op0, op1), reads, writes)

    def line(out, in_, scale, bias, reads, writes):
        either(lambda: V.tensor_scalar(out, in_, scale, bias, A.mult, A.add),
               lambda: S.activation(out, in_, F.Identity, scale=scale, bias=bias), reads, writes)

    def times(out, in_, scale, reads, writes):
        either(lambda: V.tensor_scalar(out, in_, scale, None, A.mult),
               lambda: S.activation(out, in_, F.Copy, scale=scale), reads, writes)

    def copy(out, in_, reads, writes):
        either(lambda: V.tensor_copy(out, in_), lambda: S.activation(out, in_, F.Copy), reads, writes)

    def act(out, in_, func, scale, bias, reads, writes):
        op("s", lambda: S.activation(out, in_, func, scale=scale, bias=bias), reads, writes)

    def quant(q, p, src, reads, writes): op("v", lambda: V.quantize_mx(q, p, src), reads, writes)

    def mm(bk, w, lq, lp, rq, rp, start, stop, reads):
        buf, o = bank(bk)
        op("t", lambda: P.matmul_mx(buf[:, o:o + w], lq, lp, rq, rp, start, stop), reads, [bk])

    def iota(out, pattern, base, mult, writes, small=True):
        if small:
            op("g", lambda: g.iota(out, pattern, base, mult, allow_small_or_imprecise_dtypes=True), [], writes)
        else:
            op("g", lambda: g.iota(out, pattern, base, mult), [], writes)

    def dma(q, out, in_, reads, writes, sem):
        op(q, lambda: (g.sync if q == "y" else S).dma_start(out, in_), reads, writes, sem, 16)

    def send(dst, out, in_, sem, reads, lands):
        rid, pid = topo.addr(dst)[:2]
        mask = topo.mask(core, dst)
        k = bin(mask).count("1")
        op("g", lambda: g.remote_dma(out, in_, T.sem[sem], T.sem["sent"], pid, rid, mask), reads, [], "sent", k)
        arrivals.append((sem, k, lands))

    for h in (HB, HA):
        dma("y", T.xin[:, 4 * h[0]:4 * h[1]], T.x[:, 4 * h[0]:4 * h[1]], [], ["xin" + run(h)], "dx" + run(h))
    dma("s", T.uin[:], T.u[:], [], ["uin"], "du")
    dma("y", T.pool[:, 0:4 * M], T.m[:], [], ["pool"], "dm")
    dma("s", T.wp[:], T.ws[:], [], ["w"], "dp")
    dma("y", by(T.wq[:]), T.wc[:], [], ["w0"], "dw")

    cc, grp2, w4, t4 = (T.pf[:, i:i + 1] for i in range(4))
    weight, lst, key, low, minus, held, c7 = (T.col[:, i:i + 1] for i in (0, 2, 3, 4, 5, 6, 7))
    iota(T.pi[:, 0:1], [[0, 1]], 0, 1, ["pi"], small=False)
    iota(T.j16[:], [[1, 16]], 0, 0, ["j16"])
    iota(T.ib[:], [[2, 8], [16, 4], [0, 4]], 0, 0, ["ib"])
    iota(T.idj[:], [[1, 128]], 0, -1, ["idj"])
    iota(T.ia[:], [[2, 8], [0, 4], [16, 4]], 0, 0, ["ia"])
    iota(T.idt[:], [[1024, M]], -256 * 1024, 0, ["idt"])
    iota(T.i4[:], [[0, CW // 4], [32000, 4]], 0, 0, ["i4"])
    iota(T.cdi[:], [[1, 2 * CH]], -CH, 0, ["cdi"])
    iota(T.tab[:, 0:M], [[4, M]], 0, 0, ["tab"])
    for v in range(NV):
        iota(T.val[:, C * v:C * v + C], [[4, C]], 4 * (M + C * v), 0, ["val%d" % v])

    op("v", lambda: V.memset(T.ze[:], 0.0), [], ["ze", "zero"])
    times(T.ft[:, C:CUT + 512], T.ze[:, 0:CUT + 512 - C], 0.0, ["zero"], ["ftz"])
    ts(T.pj[:, 0:1], T.pi[:, 0:1], 15, None, A.bitwise_and, None, ["pi"], ["pj0"])
    ts(T.pj[:, 1:2], T.pi[:, 0:1], 3, 14, A.arith_shift_right, A.bitwise_and, ["pi"], ["pj1"])
    ts(T.pj[:, 2:3], T.pi[:, 0:1], 2, 3, A.arith_shift_right, A.bitwise_and, ["pi"], ["pj2"])
    ts(T.pj[:, 3:4], T.pi[:, 0:1], 3, None, A.bitwise_and, None, ["pi"], ["pj3"])
    op("v", lambda: V.tensor_copy(T.pf[:, 0:4], T.pj[:, 0:4]), ["pj0", "pj1", "pj2", "pj3"], ["pf"])
    ts(T.d16[:], T.j16[:], cc, 1.0, A.is_lt, A.add, ["j16", "pf"], ["d16"])
    op("v", lambda: V.tensor_reduce(weight, T.d16[:], AxisListType.X, A.mult), ["d16"], ["weight"])
    ts(T.g8[:, 4:5], cc, 8.5, grp2, A.is_gt, A.add, ["pf"], ["g80"])
    line(T.g8[:, 0:4], T.j16[:, 0:4], 16.0, T.g8[:, 4:5], ["j16", "g80"], ["g8"])
    line(lst, w4, KEEP, UP - 3 * KEEP, ["pf"], ["lst"])
    line(key, w4, 512 * KEEP, -512.0 - 512 * 3 * KEEP, ["pf"], ["key"])
    line(low, t4, 1.0, 2 * UP, ["pf"], ["low"])
    line(c7, t4, 1.0, -3 * KEEP, ["pf"], ["c7"])
    line(held, w4, KEEP, c7, ["pf", "c7"], ["held"])
    line(T.pe[:, 3:4], w4, 32000.0, 25000.0, ["pf"], ["pe3"])
    ts(T.c4[:], T.i4[:], T.pe[:, 3:4], KEEP, A.subtract, A.min, ["i4", "pe3"], ["c4"])
    ts(T.ze[:, 3:512:4], T.idj[:], 0.0, 64.0, A.is_equal, A.mult, ["idj", "ze"], ["ze", "zero"])
    line(T.spare[:, 4:5], cc, -4.0, -float(M), ["pf"], ["sp4"])
    line(T.spare[:, 0:4], T.j16[:, 0:4], -64.0, T.spare[:, 4:5], ["j16", "sp4"], ["spare"])
    times(minus, weight, -1.0, ["weight"], ["minus"])
    WA, WB = ["wa%d" % t for t in range(4)], ["wb%d" % t for t in range(4)]
    for t in range(4):
        ts(T.wb[:, t:512:4], T.ib[:], T.g8[:, t:t + 1], weight, A.is_equal, A.mult, ["ib", "g8", "weight"], [WB[t]])
    for t in range(4):
        act(T.wa[:, t:512:4], T.ia[:], F.Abs, -1.0, T.g8[:, t:t + 1], ["ia", "g8"], [WA[t]])
    act(T.wa[:], T.wa[:], F.Relu, minus, weight, WA + ["minus", "weight"], WA)
    for b in range(4):
        quant(T.eq[:, 128 * b:128 * b + 128], T.ep[:, 128 * b:128 * b + 128], T.ze[:, 3 - b:515 - b], ["ze"], ["e%d" % b])
    quant(T.aq[:, 128:256], T.ap[:, 128:256], T.wb[:], WB, ["qwb"])
    quant(T.aq[:, 0:128], T.ap[:, 0:128], T.wa[:], WA, ["qwa"])
    quant(T.uq[:], T.up[:], T.uin[:], ["uin"], ["uq"])
    act(T.cdi[:], T.cdi[:], F.Abs, -1.0, cc, ["cdi", "pf"], ["cdi"])
    act(T.cdi[:], T.cdi[:], F.Relu, -1.0, 1.0, ["cdi"], ["cdi"])
    for r in range(R):
        a = CH - 16 * r
        times(T.cd[:, O[r]:O[r + 1]], T.cdi[:, a:a + O[r + 1] - O[r]], T.spare[:, r:r + 1], ["cdi", "spare"], ["cdp%d" % r])
        line(T.cd[:, O[r]:O[r + 1]:16 * (r + 1)], T.j16[:, 0:2], 256.0 - 4096.0, 4096.0, ["j16"], ["cdp%d" % r])
    line(T.pe[:, 0:1], t4, 8.0, 26.0, ["pf"], ["pe0"])
    line(T.pe[:, 1:2], T.pe[:, 0:1], t4, 16.0, ["pf", "pe0"], ["pe1"])
    line(T.pe[:, 2:3], w4, float(PER), T.pe[:, 1:2], ["pf", "pe1"], ["pe2"])
    for c, s in (("a", 0), ("b", 2)):
        ts(T.pos[:, s:s + 1], T.pe[:, 2:3], NE[c] - 1.0, None, A.min, None, ["pe2"], ["pos" + c])
    CD, have = ["cdp%d" % r for r in range(R)], PER
    while have < NX:
        w = min(have, NX - have)
        copy(T.cd[:, have:have + w], T.cd[:, 0:w], list(CD), ["cd%d" % (len(CD) + 1)])
        CD.append("cd%d" % (len(CD) + 1))
        have += w
    for c in "ab":
        for r in range(R):
            z = len(range(O[r + 1] - 1, NE[c], PER))
            line(T["ne" + c][:, O[r + 1] - 1:NE[c]:PER], T.j16[:, 0:z], 0.0, 1024.0, ["j16"], ["nez%d%s" % (r, c)])

    def signs(q, p, res, bk, h):
        c, w = run(h), h[1] - h[0]
        o = 128 * (c == "b")
        mm(bk, w, T.uq[:], T.up[:], q[:, h[0]:h[1]], p[:, h[0]:h[1]], True, True, ["uq", res])
        buf, z = bank(bk)
        act(T.ft[:, h[0]:h[1]], buf[:, z:z + w], F.Sign, 2.0 ** 50, -2.0 ** -100, [bk], ["ft" + c])
        quant(T.fq[:, o:o + 128], T.fp[:, o:o + 128], T.ft[:, h[0]:h[0] + 512],
              ["ftb", "ftz"] + ["fta"] * (c == "a"), ["fq" + c])

    def list_mm(bk, which, h):
        w, o = 128 * which, 128 * (h == HB)
        mm(bk, 128, T.aq[:, w:w + 128], T.ap[:, w:w + 128], T.fq[:, o:o + 128], T.fp[:, o:o + 128], True, True,
           ["fq" + run(h), "qwb" if which else "qwa"])

    def list_scan(bk, h, out, res):
        buf, o = bank(bk)
        w, c, (s, k) = (h[1] - h[0]) // 4, run(h), cols(h)
        op("v", lambda: V.tensor_tensor_scan(T.sca[:, h[0] // 4:h[1] // 4], T.c4[:, 0:w], buf[:, o:o + w], 0.0,
                                             A.add, A.max), [bk, "c4"], ["sca" + c])
        ts(out[:, s:s + k], T.sca[:, h[0] // 4 + 3:h[1] // 4:4], lst, 0.5, A.add, A.mult, ["sca" + c, "lst"], [res + c])

    def keys(v, h):
        line(T["af%d" % v][:, h[0] // 16:h[1] // 16], T.sca[:, h[0] // 4 + 3:h[1] // 4:4], 512.0, key,
             ["sca" + run(h), "key"], ["af%d%s" % (v, run(h))])

    def early(v, h): return v > 0 and h == HB

    def slots(v, h):
        c, (k0, kn) = run(h), cols(h)
        ln = "ao" if early(v, h) else "la"
        la, ar, af, ne, scd = T[ln + str(v)][:, k0:k0 + kn], T["ar%d" % v], T["af%d" % v], T["ne" + c], T["scd" + c]
        vc = "%d%s" % (v, c)
        gather(ar[:, h[0]:h[1]], T.idt[:], la, ["idt", ln + vc], ["ar" + vc])
        if v and not early(v, h):
            ts(af[:, k0:k0 + kn], la, 1024.0, -256.0 * 1024, A.mult, A.add, ["la" + vc], ["af" + vc])
        for k in range(kn):
            c0, w, z = h[0] + CH * (k // R), 16 * (k % R + 1), PER * (k // R) + O[k % R]
            o, i, x = ne[:, z:z + w], ar[:, c0:c0 + w], af[:, k0 + k:k0 + k + 1]
            either(lambda o=o, i=i, x=x: V.tensor_scalar(o, i, x, 1024.0, A.not_equal, A.mult),
                   lambda o=o, i=i, x=x: S.activation(o, i, F.Abs, scale=-1.0, bias=x),
                   ["ar" + vc, "af" + vc], ["ne%s_%d" % (c, k)])
        for r in range(R):
            times(ne[:, O[r + 1] - 2:NE[c]:PER], af[:, k0 + r:k0 + kn:R], -1.0 / 1024.0, ["af" + vc], ["neo%d%s" % (r, c)])
        op("v", lambda: V.tensor_tensor_scan(scd[:], T.cd[:, 0:NE[c]], ne[:], 0.0, A.add, A.min),
           CD + ["ne%s%d%s" % (x, r, c) for r in range(R) for x in "oz"] + ["ne%s_%d" % (c, k) for k in range(kn)], ["scd" + c])
        s = 16 * (c == "b")
        ts(T["so%d" % v][:, s:s + 16], scd[:].indirect(T.pos[:, s // 8:s // 8 + 1]), -1.0, 256.0, A.mult, A.add,
           ["scd" + c, "pos" + c], ["so" + vc])

    def scatter(v, h):
        s, kn = 16 * (h == HB), cols(h)[1]
        sn = ("sl" if early(v, h) else "so") + str(v)
        for a in reversed(range(0, kn, R)):
            b, j = min(a + R, kn), C * v + h[0]
            op("v", lambda a=a, b=b, j=j: V.tensor_copy(T.tab[:].indirect(T[sn][:, s + a:s + b]),
                                                        T.val[:, j + 16 * a:j + 16 * b]),
               [sn + run(h), "val%d" % v], ["tab"])

    def pool_names(v):
        return ["pool"] + ["n%d%d%s" % (t, b, c) for t in range(v) for b in range(4) for c in "ab"]

    def gather(out, win, off, reads, writes): copy(out, win.indirect(off), reads, writes)

    def pick(src, res, off, out, a, b, names):
        op("v", lambda: V.tensor_tensor_scan(T.scp[:, a:b], T.c4[:, 0:b - a], src[:, a:b], 0.0, A.add, A.max),
           [res, "c4"], names)
        ts(off[:, a // 4:b // 4], T.scp[:, a + 3:b:4], held, None, A.add, None, names + ["held"], [out])

    def pointers(v, h):
        for z, a, b in ((("b0", CUT, CUT + HALF), ("b1", CUT + HALF, C)) if h == HB else (("a", 0, CUT),)):
            gather(T.prow[:, a:b], T.tab[:, 0:M], T["la%d" % v][:, a // 16:b // 16], ["tab", "la%d%s" % (v, run(h))],
                   ["prow" + z])
            pick(T.prow, "prow" + z, T.boff, "boff" + z, a, b, ["scp" + z])

    def read_map(v, h):
        win, c = T.pool[:, 0:4 * (M + C * v)], run(h)
        mid = h[0] + HALF if v or c == "a" else (h[0] + h[1]) // 2
        for i, (a, b) in enumerate(((h[0], mid), (mid, h[1]))):
            gather(T.bt[:, 4 * a:4 * b], win, T.boff[:, a // 4:b // 4],
                   pool_names(v) + (["boffa"] if c == "a" else ["boffb%d" % i] if v else ["boffb0", "boffb1"]),
                   ["bt%s%d" % (c, i)])
        quant(T.bq[:, h[0]:h[1]], T.bp[:, h[0]:h[1]], T.bt[:, 4 * h[0]:4 * h[1]], ["bt%s0" % c, "bt%s1" % c], ["bq" + c])

    def new_state(v, x, h):
        c = run(h)
        for b in range(4):
            bk = "@%s%d" % (x, b)
            mm(bk, h[1] - h[0], T.wq[:, 128 * b:128 * b + 128], T.wp[:, 128 * b:128 * b + 128],
               T["sq%d" % v][:, h[0]:h[1]], T["sp%d" % v][:, h[0]:h[1]], True, False,
               ["w0", "w", "s%d%s" % (v, c)] + ["p%d" % v] * (v > 0))
            mm(bk, h[1] - h[0], T.eq[:, 128 * b:128 * b + 128], T.ep[:, 128 * b:128 * b + 128],
               T.bq[:, h[0]:h[1]], T.bp[:, h[0]:h[1]], False, True, ["e%d" % b, "bq" + c])
            unload(bk, T.yt, 0, b, h, ["yt%s%d" % (c, b)])
        quant(T["yq%d" % v][:, h[0]:h[1]], T["yp%d" % v][:, h[0]:h[1]], T.yt[:, 4 * h[0]:4 * h[1]],
              ["yt%s%d" % (c, b) for b in range(4)], ["y%d%s" % (v, c)])

    def unload(bk, tile, o, b, h, res):
        buf, p = bank(bk)
        times(tile[:, o + 4 * h[0] + b:o + 4 * h[1]:4], buf[:, p:p + h[1] - h[0]], 0.015625, [bk], res)

    def to_pool(v, b, bk, h):
        mm(bk, h[1] - h[0], T.eq[:, 128 * b:128 * b + 128], T.ep[:, 128 * b:128 * b + 128],
           T["yq%d" % v][:, h[0]:h[1]], T["yp%d" % v][:, h[0]:h[1]], True, True, ["e%d" % b, "y%d%s" % (v, run(h))])
        unload(bk, T.pool, 4 * (M + C * v), b, h, ["n%d%d%s" % (v, b, run(h))])

    def visit(v):
        w, yq, both = v + 1, T["yq%d" % v], ["y%da" % v, "y%db" % v]
        if v:
            pointers(v, HB)
            pointers(v, HA)
        read_map(v, HB)
        read_map(v, HA)
        new_state(v, "n", HB)
        new_state(v, "y", HA)
        if w < NV:
            for h in (HB, HA):
                c = run(h)
                send(nxt, by(T["sq%d" % w][:, h[0]:h[1]]), by(yq[:, h[0]:h[1]]), "s%s%d" % (c, w),
                     ["y%d%s" % (v, c)], ["s%d%s" % (w, c)])
            send(nxt, T["sp%d" % w][:], T["yp%d" % v][:], "pa%d" % w, both, ["p%d" % w])
            for h, x in ((HB, "n"), (HA, "y")):
                c, (s, k) = run(h), cols(h)
                signs(yq, T["yp%d" % v], "y%d%s" % (v, c), "@%s0" % x, h)
                list_mm("@%s1" % x, 0, h)
                list_scan("@%s1" % x, h, T["ao%d" % w], "ao%d" % w)
                if early(w, h):
                    keys(w, h)
                send(nxt, T["la%d" % w][:, s:s + k], T["ao%d" % w][:, s:s + k], "l%s%d" % (c, w), ["ao%d%s" % (w, c)],
                     ["la%d%s" % (w, c)])
        else:
            send(home, by(T.oq[:, 0:C]), by(yq[:]), "sa%d" % w, both, ["s3"])
            send(home, T.op[:, 0:C], T["yp%d" % v][:], "pa%d" % w, both, ["p3"])
        for h, x in ((HB, "n"), (HA, "y")):
            for b in range(4):
                to_pool(v, b, "@%s%d" % (x, (b + 2) % 4), h)
        for h in (HB, HA):
            if not early(v, h):
                slots(v, h)
            scatter(v, h)
        if w < NV:
            slots(w, HB)
            send(nxt, T["sl%d" % w][:, 16:32], T["so%d" % w][:, 16:32], "sl%d" % w, ["so%db" % w], ["sl%db" % w])

    for h, x in ((HB, "n"), (HA, "y")):
        c = run(h)
        quant(T.sq0[:, h[0]:h[1]], T.sp0[:, h[0]:h[1]], T.xin[:, 4 * h[0]:4 * h[1]], ["xin" + c], ["s0" + c])
        signs(T.sq0, T.sp0, "s0" + c, "@%s0" % x, h)
        list_mm("@%s1" % x, 1, h)
        list_mm("@%s2" % x, 0, h)
        buf, o = bank("@%s1" % x)
        ts(T.boff[:, h[0] // 4:h[1] // 4], buf[:, o:o + (h[1] - h[0]) // 4], 2.0, low, A.mult, A.add,
           ["@%s1" % x, "low"], ["boffa"] if c == "a" else ["boffb0", "boffb1"])
        list_scan("@%s2" % x, h, T.la0, "la0")
        keys(0, h)
    for v in range(NV):
        visit(v)

    def over(cuts, a, b): return [x for x, y in zip(cuts, cuts[1:]) if x < b and y > a]

    for a, b in zip(PK, PK[1:]):
        pick(T.tab, "tab", T.moff, "moff%d" % a, a, b, ["scpa"] if a < CUT else ["scpb0", "scpb1"])
    for a, b in zip(FIN, FIN[1:]):
        gather(T.mt[:, 4 * a:4 * b], T.pool[:], T.moff[:, a // 4:b // 4],
               pool_names(NV) + ["moff%d" % x for x in over(PK, a, b)], ["mt%d" % a])
    mm("@n0", C, T.wq[:, 0:128], T.wp[:, 0:128], T.oq[:, 0:C], T.op[:, 0:C], True, True, ["w0", "w", "s3", "p3"])
    copy(T.yo[:], T.pn[:, 0:C], ["@n0"], ["yo"])
    for a, b in zip(ST, ST[1:]):
        quant(T.oq[:, C + a:C + b], T.op[:, C + a:C + b], T.mt[:, 4 * a:4 * b], ["mt%d" % x for x in over(FIN, a, b)],
              ["o%d" % a])
    dma("y", T.oc[:, 0:4 * C], by(T.oq[:, 0:C]), ["s3"], [], "out")
    for a, b in zip(ST, ST[1:]):
        dma("y", T.oc[:, 4 * (C + a):4 * (C + b)], by(T.oq[:, C + a:C + b]), ["o%d" % a], [], "out")
    dma("s", T.y[:], T.yo[:], ["yo"], [], "out")
    for k in range(4):
        dma("ys"[k % 2], T.osc[4 * k:4 * k + 4, :], T.op[32 * k:32 * k + 4, :], ["o%d" % a for a in ST[:-1]] + ["p3"],
            [], "out")
    _emit(g, T, arrivals, ops)
